import numpy as np, ml_dtypes
CORES = [78,86,94,102,110,118]
N = 6
BF = ml_dtypes.bfloat16
def f(rng, *shape):
    return (rng.standard_normal(shape, dtype=np.float32) * np.exp2(rng.integers(-2, 3, shape[:-1] + (1,)))).astype(BF)
def wide(rng, *shape):
    v = f(rng, *shape).astype(np.float32); k = shape[:-2] + (1, shape[-1])
    return (v * np.exp2(rng.integers(-6, 7, k)) * (rng.random(k) > 0.0625)).astype(BF)
P, F, M, C, T, K, D = 4096, 768, 11, 2048, 3, 128, 5
def parts(rng):
    pic = rng.standard_normal((N, 8, 1, P), dtype=np.float32) + rng.standard_normal((N, 8, 16, P), dtype=np.float32)
    pic = (pic * np.exp2(rng.integers(-2, 3, (N, 8, 16, 1)))).astype(np.float32)
    s = rng.integers(0, P, (N, 8, 16, F)); o = rng.integers(0, P, (N, 8, 16, T)); th = M // 2 + rng.integers(-1, 2, (N, 8, T))
    return pic, s, o, th, rng.integers(-256, 257, (N, 8, 16, C)), rng.integers(0, P, (N, 8, 16, C))
def pack(pic, s, o, th, b, e):
    return {"pic": pic.reshape(N, 128, P).astype(BF), "shp": s.reshape(N, 128, F).astype(np.int32), "ofs": o.reshape(N, 128, T).astype(np.int32),
            "thr": th.astype(np.int32), "inc": b.reshape(N, 128, C).astype(np.float32).astype(BF), "ex": e.reshape(N, 128, C).astype(np.int32)}
def setup_inputs(rng):
    return pack(*parts(rng))
def setup_inputs_edge(rng):
    pic, s, o, th, b, e = parts(rng)
    lv = np.array([0, 3, 4, 8, 9, 11, 12, 16])[rng.integers(0, 8, (N, 8, 1, P))]; ch = np.argsort(rng.random((N, 8, 16, 1)), axis=2)
    pic = (ch < lv).astype(np.float32) * np.exp2(rng.integers(-2, 3, (N, 8, 16, 1)))
    return pack(pic, s, o, 3 * M // 4 + rng.integers(-1, 2, (N, 8, T)), b, e)
def setup_inputs_ends(rng):
    pic, s, o, th, b, e = parts(rng)
    s = rng.choice(np.array([0, 1, P // 2, P - 1]), s.shape); o = rng.choice(np.array([0, 1, P - 1]), o.shape)
    b = rng.choice(np.array([-256, -255, -2, -1, 0, 1, 255, 256]), b.shape); e[:, ::2] = rng.choice(np.array([0, 1, P - 1]), (N, 4, 16, C))
    th[:, :3] = 0; th[:, 3] = 16
    pic[:, 4] = -(np.arange(P) >> 5)
    x = np.arange(16)[:, None] * (P >> 4) + rng.integers(0, P >> 5, (N, 16, F))
    s[:, 4] = np.where(rng.random((N, 1, F)) < 0.5, P - 1 - x, x); o[:, 4, :, 0] = 0; th[:, 4, 0] = M
    return pack(pic, s, o, th, b, e)
def setup_inputs_mixed(rng):
    pic, s, o, th, b, e = parts(rng)
    x = np.arange(P); ch = np.argsort(rng.random((N, 3, 16, 1)), axis=2) < 10
    pic[:, :3] = np.where(ch | ((x & 1) == 0), -(x >> 5), x >> 5) * np.exp2(rng.integers(-2, 3, (N, 3, 16, 1)))
    code = rng.integers(0, C - 1, (N, 3, F)); odd = rng.integers(0, 2, (N, 3, F))
    code[:, 0, :K] = np.argsort(rng.random((N, C)), axis=1)[:, :K]; odd[:, 0, :K] = 0
    code[:, 1:, ::3] = C - 1; odd[:, 1, 0] = 0; odd[:, 1, 3] = 1; odd[:, 2, ::3] = 1; odd[:, 2, 1] = 0
    lv = np.zeros((N, 3, 16, F), np.int64)
    for m in range(M):
        lv[:, :, m + D] = lv[:, :, m] + 2 * ((code >> m) & 1) - 1
    at = (8 + lv) * (P >> 4) + rng.integers(0, P >> 5, lv.shape); at = at - (at & 1) + odd[:, :, None, :]
    s[:, :3] = (at - o[:, :3, :, :1]) & (P - 1)
    pic[:, 3] = rng.standard_normal((N, 16, P), dtype=np.float32)
    pic[:, 4:6] = 3 * rng.standard_normal((N, 2, 1, P), dtype=np.float32) + rng.standard_normal((N, 2, 16, P), dtype=np.float32)
    for g, w in enumerate(([M, 16, 0, 1], [1, 0, 0, 0], [1, 16, 0, M], [1, 1, 0, 1], [M, M - 1, 16, 0], [M - 1, 0, M, 16], [M // 2, 16, 0, M // 2], [13, 0, 14, 15])):
        th[:, g] = np.resize(np.array(w), T)
    return pack(pic, s, o, th, b, e)
def setup_inputs_repeat(rng):
    pic, s, o, th, b, e = parts(rng)
    s[:, ::2] = s[:, ::2][..., rng.integers(0, 5, F)]; th[:, ::2] = 0
    s[:, 6, :, :T * K] = rng.integers(0, P, (N, 16, T * K))
    pic[:, 2:4] = 1.0; th[:, 2] = M; th[:, 3] = M + 1
    return pack(pic, s, o, th, b, e)
def setup_inputs_spread(rng):
    pic, s, o, th, b, e = parts(rng); lp = P.bit_length() - 1
    w = wide(rng, N, 128, P).astype(np.float32).reshape(N, 8, 16, P)
    pic = np.where(rng.random((N, 8, 1, P)) < 0.5, np.abs(w), w) * np.exp2(rng.integers(-60, 61, (N, 8, 16, 1)))
    pic = np.where(np.abs(pic) < 2.0 ** -78, 0.0, pic)
    s = np.minimum(np.exp2(lp * rng.random(s.shape)).astype(np.int64), P - 1); e = np.minimum(np.exp2(lp * rng.random(e.shape)).astype(np.int64), P - 1)
    b = np.minimum(np.exp2(8 * rng.random(b.shape)).astype(np.int64), 256) * rng.integers(-1, 2, b.shape)
    return pack(pic, s, o, rng.integers(2, M - 1, (N, 8, T)), b, e)
def check_inputs(d):
    bad = []
    for k, lo, hi in (("shp", 0, P - 1), ("ofs", 0, P - 1), ("thr", 0, 16), ("ex", 0, P - 1)):
        if np.min(d[k]) < lo or np.max(d[k]) > hi: bad.append("range of " + k)
    p = np.abs(np.asarray(d["pic"]).astype(np.float32))
    if not np.all((p == 0) | ((p >= 2.0 ** -100) & (p <= 2.0 ** 100))): bad.append("sizes of pic")
    a = np.asarray(d["inc"]).astype(np.float32)
    if not (np.all(np.abs(a) <= 256) and np.all(a == np.floor(a))): bad.append("whole numbers of inc")
    return bad
def reference(pic, shp, ofs, thr, inc, ex):
    im = pic.astype(np.float32).reshape(N, 8, 16, P); s = shp.astype(np.int64).reshape(N, 8, 16, F); o = ofs.astype(np.int64).reshape(N, 8, 16, T)
    b = inc.astype(np.float32).astype(np.int64).reshape(N, 8, 16, C); e = ex.astype(np.int64).reshape(N, 8, 16, C); bit = 2 ** np.arange(M)[:, None]
    for t in range(T):
        d = D - t; after = np.array(b); new = []
        for r in range(N):
            q = (r + 1 + t) % N
            x = (s[r] + o[r, :, :, t:t + 1]) & (P - 1)
            v = np.take_along_axis(im[r], x.reshape(8, 1, 16 * F), 2).reshape(8, 16, 16, F)
            n = np.add.reduce((v[:, :, :M] > v[:, :, d:d + M]).astype(np.int64), axis=1)
            code = np.add.reduce((n >= 9) * bit, axis=1)
            sure = np.add.reduce(((n >= 12) | (n <= 3)).astype(np.int64), axis=1) >= thr[r][:, t:t + 1]
            up = np.take_along_axis(b[q], code[:, None, :], 2); like = np.take_along_axis(e[q], code[:, None, :], 2)
            new.append(np.where(sure[:, None, :], (s[r] + up) & (P - 1), like))
            used = np.zeros((8, C + 1), bool)
            np.put_along_axis(used, np.where(sure, code, C)[:, t * K:t * K + K], True, 1)
            after[q] = np.where(used[:, None, :C], b[q] >> 1, b[q])
        s = np.stack(new); b = after
    return {"ys": s.reshape(N, 128, F).astype(np.float32), "yi": b.reshape(N, 128, C).astype(np.float32).astype(BF)}

@@ -1,0 +1,595 @@
+from concourse.mybir import AluOpType as A, ActivationFunctionType as F
+
+NS = [16, 16, 16]
+SPLIT = [(4, 4, 11), (4, 4, 11), (3, 3, 10)]
+PA, PV = 2, 2
+PREF = True
+HPRI, MPRI = 0.5, 1.5
+SEED, ITERS, TEMP = 1, 22000, 0.05
+MODELS = [(1.04, 1.5, 3.8, 0.53, 2700, 60.0, 700, 250.0, 100, 2000), (0.85, 1.15, 2.0, 0.43, 2000, 100.0, 400, 350.0, 70, 1200),
+          (1.2, 1.95, 5.5, 0.62, 3500, 40.0, 1000, 180.0, 150, 3000)]
+NC = len(NS)
+C0 = [sum(NS[:c]) for c in range(NC)]
+SPARE, EXO, TABW, PAD = 2048, 2176, 4224, 512
+
+
+def _sb(n, dtype):
+    return ("sbuf", [128, n], dtype)
+
+
+SCRATCH = {
+    "pic_s": _sb(9216, "bfloat16"), "shp_s": _sb(768, "int32"), "ex_s": _sb(2048, "int32"), "inc_s": _sb(2048, "bfloat16"),
+    "tab": _sb(TABW, "float32"), "yit": _sb(EXO, "bfloat16"), "pfi": _sb(EXO + 16, "bfloat16"), "pfx": _sb(2816, "float32"),
+    "ofs_s": _sb(4, "int32"), "thr_s": _sb(4, "int32"), "thf": _sb(4, "float32"), "thc": _sb(4, "float32"), "oc": _sb(4, "float32"),
+    "ci": _sb(4, "int32"), "cl": _sb(8, "float32"), "cf": _sb(160, "bfloat16"), "iI": _sb(256, "bfloat16"), "iG": _sb(128, "bfloat16"),
+    "iC": _sb(256, "bfloat16"), "i256": _sb(EXO + 16, "float32"),
+    "r16e": _sb(160, "float16"), "r16o": _sb(160, "float16"), "r32e": _sb(160, "float32"), "r32o": _sb(160, "float32"),
+    "bo": _sb(128, "float32"), "rep": _sb(128, "float32"), "rt": _sb(768, "float32"), "ub": _sb(144, "bfloat16"), "uh": _sb(144, "bfloat16"),
+    "w2": _sb(14 * 128, "bfloat16"), "ex16": _sb(256, "bfloat16"), "ones": _sb(256, "bfloat16"), "fours": _sb(128, "bfloat16"),
+    "fid": _sb(8, "float32"), "dum": _sb(8, "float32"), "fall": _sb(48, "float32"), "s16": _sb(768, "float16"),
+    "rq_o": _sb(144, "uint16"), "rq_i": _sb(144, "uint16"), "an_o": _sb(2304, "float16"), "an_i": _sb(2304, "float16"),
+    "xi": _sb(768, "int32"), "smn": _sb(768, "float32"), "yo": _sb(768, "float32"),
+    "hf": _sb(8, "float32"), "hg": _sb(8, "float32"), "nb": _sb(8, "float32"), "mn": _sb(8, "float32"),
+    "hl": _sb(8, "uint16"), "tl": _sb(8, "uint16"), "tx": _sb(8, "uint16"),
+    "rr": _sb(128, "float32"), "dd": _sb(576, "float32"), "hv": _sb(128, "float32"), "hi": _sb(432, "int32"), "hx": _sb(288, "int32"),
+    "la": _sb(48, "float32"), "l1": _sb(48, "uint16"), "l2": _sb(48, "uint16"),
+    "px": ("psum", [128, 16, 2, 16], "float32"),
+}
+for _k in ("po", "ps", "pe", "pv0", "pv1", "pd0", "pd1"):
+    SCRATCH[_k] = ("psum", [128, 512], "float32")
+for _c in range(NC):
+    _n = NS[_c]
+    SCRATCH["pm%d" % _n] = _sb(_n, "uint16")
+    SCRATCH["pf%d" % _n] = _sb(2 * _n, "float32")
+    SCRATCH["pq%d" % _n] = _sb(_n, "int32")
+    SCRATCH["aT%d" % _c] = ("sbuf", [128, _n // 2, 2, 16], "float16")
+    SCRATCH["sm%d" % _c] = ("sbuf", [128, _n // 2, 2, 16], "float32")
+    SCRATCH["st%d" % _c] = ("sbuf", [128, _n // 2, 2, 16], "float32")
+    SCRATCH["li%d" % _c] = _sb(16 * _n, "uint16")
+    SCRATCH["mm%d" % _c] = _sb(10 * 16 * _n, "bfloat16")
+    SCRATCH["cc%d" % _c] = _sb(11 * 16 * _n, "bfloat16")
+    SCRATCH["bb%d" % _c] = _sb(3 * 11 * _n, "bfloat16")
+    SCRATCH["su%d" % _c] = _sb(_n, "bfloat16")
+    SCRATCH["sT%d" % _c] = _sb(128, "bfloat16")
+SEMAPHORES = ["v", "a", "p", "q", "loc"] + ["d%d" % k for k in range(24)] + ["r%d" % k for k in range(6 * NC + 8)]
+
+
+def pieces(lo, hi, k):
+    m = -(-(hi - lo) // k)
+    return [(lo + (hi - lo) * j // m, lo + (hi - lo) * (j + 1) // m) for j in range(m)] if hi > lo else []
+
+
+def build(g, core, T, topo):
+    rank = T.rank_of(core)
+    N = len(T.cores)
+    V, S_, P = g.vector, g.scalar, g.tensor
+    ops = []
+    cnt = {"pd": 0, "pv": 0, "r": 0}
+    pri = [-1.0]
+
+    def add(eng, n, fns, r, w, banks=(), k=1.0, kind="c", sem=None):
+        ops.append({"pri": pri[0], "eng": eng, "n": n, "k": k, "fns": fns, "r": list(r), "w": list(w), "banks": list(banks),
+                    "kind": kind, "sem": sem})
+
+    def dve(n, fn, r, w, banks=(), k=1.0):
+        add("v", n, [fn], r, w, banks, k)
+
+    def act(n, fn, r, w, banks=(), k=1.0):
+        add("a", n, [fn], r, w, banks, k)
+
+    def pe(cyc, fns, r, w, banks):
+        add("p", cyc, fns, r, w, banks)
+
+    def dma(q, out, in_, nbytes, r, w):
+        Q = {"s": g.sync, "a": S_, "q": g}[q]
+        add(q, nbytes, [lambda: Q.dma_start(out, in_)], r, w, kind="d")
+
+    def send(dst_rank, out, in_, nbytes, r, w, lanes):
+        dst = T.cores[dst_rank % N]
+        rid, pid, _ = topo.addr(dst)
+        eng = topo.engines(core, dst)
+        half = len(eng) // 2
+        eng = eng[half * lanes[0]:half * (lanes[-1] + 1)]
+        k = cnt["r"]
+        cnt["r"] += 1
+        add("q", nbytes, [lambda: g.remote_dma(out, in_, T.sem["r%d" % k], T.sem.loc, pid, rid, sum(1 << e for e in eng))],
+            r, w, k=lanes, kind="r", sem=("r%d" % k, len(eng)))
+
+    def iota(out, pat, base, cm, n, key):
+        add("q", n, [lambda: g.iota(out, pat, base, cm, allow_small_or_imprecise_dtypes=True)], [], [key])
+
+    quick = (0,) if PREF else (0, 1)
+    W2 = [T.w2[:, 128 * m:128 * (m + 1)] for m in range(14)]
+    col = [T.cl[:, k:k + 1] for k in range(6)]
+    main = T.pic_s[:, PAD:PAD + 4096]
+
+    W0 = 16 * NS[0]
+    dma("s", T.shp_s[:, 0:W0], T.shp[:, 0:W0], 512 * W0, [], [("shp", 0)])
+    dma("a", T.ofs_s[:, 0:3], T.ofs[:], 1536, [], ["ofs"])
+    dma("s", T.shp_s[:, W0:768], T.shp[:, W0:768], 512 * (768 - W0), [], [("shp", c) for c in range(1, NC)])
+    dma("s", main, T.pic[:], 1 << 20, [], ["pic"])
+    dma("a", T.thr_s[0:8, 0:3], T.thr[:], 96, [], ["thr"])
+    if PREF:
+        dma("s", T.inc_s[:], T.inc[:], 1 << 19, [], ["inc_s"])
+    dma("s", T.ex_s[:, 0:1024], T.ex[:, 0:1024], 1 << 19, [], [("ex", 0)])
+    dma("s", T.ex_s[:, 1024:2048], T.ex[:, 1024:2048], 1 << 19, [], [("ex", 1)])
+
+    add("q", 4, [lambda: g.iota(T.ci[:], [[0, 4]], 0, 1)], [], ["ci"])
+    iota(T.cf[:], [[1, 160]], -16, 0, 160, "cf")
+    iota(T.iI[:], [[0, 16], [1, 16]], 0, 0, 256, "iI")
+    iota(T.iG[:], [[16, 8], [0, 16]], 0, 0, 128, "iG")
+    iota(T.iC[:], [[1, 16], [0, 16]], 0, 0, 256, "iC")
+    dma("q", T.tab[:, 0:2048], T.inc[:], 1 << 20, ["iC"], ["tabI"])
+    iota(T.i256[:], [[256, EXO + 16]], 0, 0, EXO + 16, "i256")
+    dma("s", T.pic_s[:, PAD + 4096:PAD + 8192], T.pic[:], 1 << 20, [("ex", 1)], ["picx1"])
+    dma("s", T.pic_s[:, 0:PAD], T.pic[:, 4096 - PAD:4096], 1 << 17, [("ex", 1)], ["picx0"])
+    dma("s", T.pic_s[:, PAD + 8192:9216], T.pic[:, 0:PAD], 1 << 17, [("ex", 1)], ["picx2"])
+    dve(1, lambda: V.tensor_scalar(T.ci[:, 1:2], T.ci[:, 0:1], 15, None, A.bitwise_and), ["ci"], ["ci1"])
+    dve(1, lambda: V.tensor_scalar(T.ci[:, 2:3], T.ci[:, 0:1], 112, None, A.bitwise_and), ["ci"], ["ci2"])
+    dve(1, lambda: V.tensor_scalar(T.ci[:, 3:4], T.ci[:, 0:1], 4, 1, A.arith_shift_right, A.bitwise_and), ["ci"], ["ci3"])
+    dve(1, lambda: V.tensor_copy(T.cl[:, 0:4], T.ci[:]), ["ci", "ci1", "ci2", "ci3"], ["cl"])
+    dve(1, lambda: V.tensor_scalar(col[4], col[3], -1.0, 1.0, A.mult, A.add), ["cl"], ["cl4"])
+    dve(1, lambda: V.tensor_scalar(col[5], col[1], 16.0, None, A.mult), ["cl"], ["cl5"])
+    for buf, cc_, key in ((T.r16e, 4, "r16e"), (T.r16o, 3, "r16o"), (T.r32e, 4, "r32e"), (T.r32o, 3, "r32o")):
+        dve(160, lambda buf=buf, cc_=cc_: V.tensor_scalar(buf[:], T.cf[:], col[0], col[cc_], A.is_equal, A.mult),
+            ["cf", "cl", "cl4"], [key], k=0.5 if "16" in key else 1)
+    dve(128, lambda: V.tensor_scalar(T.bo[:], T.iG[:], col[2], None, A.is_equal), ["iG", "cl"], ["bo"])
+    dve(1, lambda: V.tensor_scalar(T.oc[:, 0:1], T.ofs_s[:, 0:1], 2048.0, None, A.add), ["ofs"], [("oc", 0)])
+    dve(1, lambda: V.tensor_scalar(T.oc[:, 1:3], T.ofs_s[:, 1:3], 2048.0 + PAD, None, A.add), ["ofs"], [("oc", 1), ("oc", 2)])
+    for t in range(3):
+        dve(256, lambda t=t: V.tensor_scalar(T.rt[:, 256 * t:256 * t + 256], T.iI[:], col[1], T.oc[:, t:t + 1], A.is_equal, A.mult),
+            ["iI", "cl", ("oc", t)], [("rt", t)])
+    for n in sorted(set(NS)):
+        if n == 16:
+            dve(1, lambda: V.tensor_scalar(T.pm16[:], T.cf[:, 16:32], col[5], None, A.add), ["cf", "cl5"], ["pm16"])
+            continue
+        pf, pq = T["pf%d" % n], T["pq%d" % n]
+        dve(1, lambda n=n, pf=pf: V.tensor_scalar(pf[:, 0:n], T.cf[:, 16:16 + n], 16.0, col[1], A.mult, A.add), ["cf", "cl"], [("pf", n)])
+        dve(1, lambda n=n, pf=pf: V.tensor_scalar(pf[:, n:2 * n], pf[:, 0:n], 1.0 / n, 0.5 / n - 0.5, A.mult, A.add), [("pf", n)], [("pg", n)])
+        dve(1, lambda n=n, pf=pf, pq=pq: V.tensor_copy(pq[:], pf[:, n:2 * n]), [("pg", n)], [("pq", n)])
+        dve(1, lambda n=n, pf=pf, pq=pq: V.tensor_scalar(pf[:, n:2 * n], pq[:], (1.0 - 16 * n) / 16, None, A.mult), [("pq", n)], [("pg", n)])
+        dve(1, lambda n=n, pf=pf: V.tensor_tensor(pf[:, 0:n], pf[:, 0:n], pf[:, n:2 * n], A.add), [("pf", n), ("pg", n)], [("pf", n)])
+        dve(1, lambda n=n, pf=pf: V.tensor_scalar(T["pm%d" % n][:], pf[:, 0:n], 16.0, None, A.mult), [("pf", n)], ["pm%d" % n])
+    dve(143, lambda: V.tensor_scalar(T.ub[:, 0:143], T.cf[:, 1:144], col[2], None, A.is_equal), ["cf", "cl"], ["ub"], k=0.5)
+    act(143, lambda: S_.activation(T.uh[:, 0:143], T.ub[:, 0:143], F.Identity, scale=0.5), ["ub"], ["uh"])
+    dve(128, lambda: V.tensor_scalar(W2[1], T.cf[:, 16:144], col[0], None, A.is_equal), ["cf", "cl"], [("w2", 1)], k=0.5)
+    for m in (11, 4, 0, 2, 3, 5, 6, 7, 8, 9, 10, 12, 13):
+        sc = -1.0 if m == 11 else -float(EXO) if m == 12 else -4096.0 if m == 13 else 2.0 ** (m - 1)
+        act(128, lambda m=m, sc=sc: S_.activation(W2[m], W2[1], F.Identity, scale=sc), [("w2", 1)], [("w2", m)])
+    dve(256, lambda: V.tensor_scalar(T.ex16[:], T.iC[:], col[0], None, A.is_equal), ["iC", "cl"], ["ex16"], k=0.5)
+    dve(256, lambda: V.memset(T.ones[:], 1.0), [], ["ones"], k=0.5)
+    dve(128, lambda: V.memset(T.tab[:, SPARE:EXO], 0.0), [], ["tabD"])
+    dve(1, lambda: V.tensor_scalar(T.fid[:], T.iG[:, 0:128:16], col[1], 4096.0, A.add, A.mult), ["iG", "cl"], ["fid"])
+    dve(1, lambda: V.tensor_scalar(T.dum[:], T.iG[:, 0:128:16], col[1], float(SPARE), A.add, A.add), ["iG", "cl"], ["dum"])
+    dve(128, lambda: V.tensor_scalar(T.rep[0:8, :], T.iG[0:8, :], 0.0625, T.cl[0:8, 0:1], A.mult, A.is_equal), ["iG", "cl"], ["rep"])
+    dve(1, lambda: V.tensor_scalar(T.thf[0:8, 0:3], T.thr_s[0:8, 0:3], 2.0, -11.0, A.mult, A.add), ["thr"], ["thf"])
+    pe(256, [lambda: P.matmul(T.ps[:, 0:3], T.rep[0:8, :], T.thf[0:8, 0:3], True, True)], ["rep", "thf"], ["ps"], ["ps"])
+    act(1, lambda: S_.activation(T.thc[:, 0:3], T.ps[:, 0:3], F.Identity), ["ps"], ["thc"], ["ps"])
+    pri[0] = 0.5
+    for k in range(2):
+        dve(1024, lambda k=k: V.tensor_scalar(T.tab[:, EXO + 1024 * k:EXO + 1024 * k + 1024], T.ex_s[:, 1024 * k:1024 * k + 1024], -2048.0, None, A.add),
+            [("ex", k)], [("tabE", k)])
+    if PREF:
+        dve(144, lambda: V.memset(T.pfi[:, SPARE:EXO + 16], 0.0), [], ["pfz", "pfd"], k=0.5)
+        dve(48, lambda: V.tensor_scalar(T.fall[:], T.cf[:, 16:64], 16.0, col[1], A.mult, A.add), ["cf", "cl"], ["fall"])
+        pri[0] = -0.9
+        for k in range(2):
+            send(rank - 3, T.pfi[:, 1024 * k:1024 * k + 1024], T.inc_s[:, 1024 * k:1024 * k + 1024], 1 << 18, ["inc_s"], [("pfi", k)],
+                 (0, 1) if k == 0 else (1,))
+        pri[0] = 0.6
+        for k in range(4):
+            send(rank - 3, T.pfx[:, 768 + 512 * k:1280 + 512 * k], T.tab[:, EXO + 512 * k:EXO + 512 * k + 512], 1 << 18,
+                 [("tabE", k // 2)], [("pfe", k)], (1,))
+    else:
+        dve(128, lambda: V.memset(T.fours[:], 4.0), [], ["fours"], k=0.5)
+    pxk = [("px", 0), ("px", 1)]
+
+    def route(c, src, e, o, cyc, key, const=False):
+        h2 = NS[c] // 2
+        E = [[e[:, 16:144], e[:, 0:128]], [o[:, 32:160], o[:, 16:144]]]
+        for x in range(2):
+            fns = [lambda x=x, y=y: P.matmul(T.px[:, 0:h2, x, :], E[x][y], src[:, :, y, :], y == 0, y == 1 and not const) for y in range(2)]
+            if const:
+                fns.append(lambda x=x: P.matmul(T.px[:, 0:h2, x, :], W2[10], T.fours[:, 0:16 * h2], False, True))
+            pe(2 * max(64, 16 * h2) * cyc + (16 * h2 if const else 0), fns, key, [("px", x)], ["px"])
+        return T.px[:, 0:h2]
+
+    def update(t, c):
+        n, W, f0 = NS[c], 16 * NS[c], 16 * C0[c]
+        aT, st, li = T["aT%d" % c], T["st%d" % c], T["li%d" % c]
+        if t == 0:
+            dve(W, lambda: V.tensor_scalar(T.s16[:, f0:f0 + W], T.shp_s[:, f0:f0 + W], -2048.0, None, A.add), [("shp", c)], [("s16", c)])
+            src, key = T.s16[:, f0:f0 + W], ("s16", c)
+        else:
+            src, key = T.an_i[:, 768 * (t - 1) + f0:768 * (t - 1) + f0 + W], ("an_i", t - 1, c)
+        dve(W, lambda: V.transpose(aT[:], src), [key], [("aT", c)], k=0.5)
+        pa = route(c, aT, T.r16e, T.r16o, 1, [("aT", c), "r16e", "r16o"])
+        if t == 0:
+            act(W, lambda: S_.activation(st[:], pa, F.Identity), pxk, [("st", c)], ["px"])
+        else:
+            dve(W, lambda: V.tensor_tensor(st[:], pa, T["sm%d" % c][:], A.add), pxk + [("sm", c)], [("st", c)], ["px"])
+        o0 = 256 * (t % 2)
+        xi = T.xi[:, f0:f0 + W]
+        dve(W, lambda: V.tensor_tensor(xi, st[:], T.po[:, o0:o0 + W], A.add), [("st", c), ("po", t % 2)], [("xi", c)], ["po"])
+        if t == 0:
+            dve(W, lambda: V.tensor_scalar(xi, xi, 4095, None, A.bitwise_and), [("xi", c)], [("xi", c)])
+        k = ((16 - t) * n + 15) // 16
+        dve(16 * k, lambda: V.tensor_copy(li[:, 0:16 * k], xi.indirect(T["pm%d" % n][:, 0:k])), [("xi", c), "pm%d" % n], [("li", c)], k="g")
+
+    def compute(t, c):
+        n, W, d = NS[c], 16 * NS[c], 5 - t
+        a, a2, b = SPLIT[t]
+        li, mm, cc, bb, su, sT = [T["%s%d" % (s, c)] for s in ("li", "mm", "cc", "bb", "su", "sT")]
+        win, wk = (main, ["pic"]) if t == 0 else (T.pic_s[:, 0:9216], ["pic", "picx0", "picx1", "picx2"])
+        M = lambda i0, i1: mm[:, (i0 - a) * W:(i1 - a) * W]
+        mk = lambda i0, i1: [("mm", c, i - a) for i in range(i0, i1)]
+        ck = lambda m0, m1: [("cc", c, m) for m in range(m0, m1)]
+        e1 = min(a2 + d, b + 1)
+        for j0, j1 in ((d, e1), (e1, b + 1), (a, d)):
+            for i0, i1 in pieces(j0, j1, PA):
+                act((i1 - i0) * W, lambda i0=i0, i1=i1: S_.activation(M(i0, i1), win.indirect(li[:, i0 * n:i1 * n]), F.Identity),
+                    [("li", c)] + wk, mk(i0, i1), k="g")
+        m2 = b - d + 1
+        pv, pvk = T["pv%d" % cnt["pv"]], "pv%d" % cnt["pv"]
+        cnt["pv"] ^= 1
+
+        def votes(m0, m1, signs):
+            u = T.uh if signs else T.ub
+            fns = [lambda j=j: P.matmul(pv[:, m0 * n:m1 * n], u[:, 15 - j:143 - j], cc[:, m0 * W + j:m1 * W:16], j == 0, j == 15 and not signs)
+                   for j in range(16)]
+            if signs:
+                fns.append(lambda: P.matmul(pv[:, m0 * n:m1 * n], W2[4], T.ones[:, 0:(m1 - m0) * n], False, True))
+            pe(len(fns) * max(64, (m1 - m0) * n), fns, ck(m0, m1) + ["ub", "uh", ("w2", 4), "ones"], [(pvk, "v")], [pvk])
+
+        for m0, m1 in pieces(0, a2, PV):
+            dve((m1 - m0) * W, lambda m0=m0, m1=m1: V.tensor_tensor(cc[:, m0 * W:m1 * W], win.indirect(li[:, m0 * n:m1 * n]), M(m0 + d, m1 + d), A.is_gt),
+                [("li", c)] + wk + mk(m0 + d, m1 + d), ck(m0, m1), k="g")
+        votes(0, a2, False)
+        per = 512 // W
+        for m0 in range(a2, m2, per):
+            m1 = min(m0 + per, m2)
+            pd, pk = T["pd%d" % cnt["pd"]], "pd%d" % cnt["pd"]
+            cnt["pd"] ^= 1
+            w = (m1 - m0) * W
+            pe(2 * w, [lambda pd=pd, m0=m0, m1=m1, w=w: P.matmul(pd[:, 0:w], W2[1], M(m0, m1), True, False),
+                       lambda pd=pd, m0=m0, m1=m1, w=w: P.matmul(pd[:, 0:w], W2[11], M(m0 + d, m1 + d), False, True)],
+               mk(m0, m1) + mk(m0 + d, m1 + d) + [("w2", 1), ("w2", 11)], [pk], [pk])
+            act(w, lambda pd=pd, m0=m0, m1=m1, w=w: S_.activation(cc[:, m0 * W:m1 * W], pd[:, 0:w], F.Sign, bias=-2.0 ** -110),
+                [pk], ck(m0, m1), [pk])
+        for m0, m1 in pieces(m2, 11, PV):
+            dve((m1 - m0) * W, lambda m0=m0, m1=m1: V.tensor_tensor(cc[:, m0 * W:m1 * W], win.indirect(li[:, (m0 + d) * n:(m1 + d) * n]), M(m0, m1), A.is_lt),
+                [("li", c)] + wk + mk(m0, m1), ck(m0, m1), k="g")
+        if m2 < 11:
+            votes(m2, 11, False)
+        if m2 > a2:
+            votes(a2, m2, True)
+        q = 11 * n
+        act(q, lambda: S_.activation(bb[:, 2 * q:3 * q], pv[:, 0:q], F.Abs, bias=-7.5), [(pvk, "v")], [("bb", c, 2)], [pvk])
+        act(q, lambda: S_.activation(bb[:, 0:q], pv[:, 0:q], F.Sign, bias=-8.5), [(pvk, "v")], [("bb", c, 0)], [pvk])
+        act(q, lambda: S_.activation(bb[:, q:2 * q], bb[:, 2 * q:3 * q], F.Sign, bias=-4.0), [("bb", c, 2)], [("bb", c, 1)])
+        pe(11 * 64, [lambda m=m: P.matmul(T.ps[:, 0:n], W2[m], bb[:, m * n:(m + 1) * n], m == 0, False) for m in range(11)],
+           [("bb", c, 0)] + [("w2", m) for m in range(11)], ["ps"], ["ps"])
+        pe(11 * 64, [lambda m=m: P.matmul(pv[:, 256:256 + n], W2[1], bb[:, q + m * n:q + (m + 1) * n], m == 0, m == 10) for m in range(11)],
+           [("bb", c, 1), ("w2", 1)], [(pvk, "c")], [pvk])
+        dve(n, lambda: V.tensor_scalar(su[:], pv[:, 256:256 + n], T.thc[:, t:t + 1], None, A.is_ge), [(pvk, "c"), "thc"], [("su", c)], [pvk])
+        last = PREF and t == 2
+        wu = 13 if last else 12
+        pe(64, [lambda: P.matmul(T.ps[:, 0:n], W2[wu], su[:], False, True)], [("su", c), ("w2", wu)], ["ps"], ["ps"])
+        r0, c0 = 48 * t + C0[c], C0[c]
+        if last:
+            dve(n, lambda: V.tensor_scalar(T.la[:, c0:c0 + n], T.ps[:, 0:n], 1023.5 + 768, None, A.add), ["ps"], [("la", c)], ["ps"])
+            dve(n, lambda: V.tensor_scalar(T.l1[:, c0:c0 + n], T.ps[:, 0:n], 1023.5 + 4096, float(EXO), A.add, A.min), ["ps"], [("l1", c)], ["ps"])
+            if c0 < 24 and c0 + n > 16:
+                dve(n, lambda: V.tensor_scalar(T.rq_o[:, r0:r0 + n], T.ps[:, 0:n], 1023.5 + 4096, None, A.add), ["ps"], [("rq_o", t, c)], ["ps"])
+            dve(n, lambda: V.tensor_tensor(T.la[:, c0:c0 + n], T.la[:, c0:c0 + n], T.fall[:, c0:c0 + n], A.max), [("la", c), "fall"], [("la", c)])
+            dve(n, lambda: V.tensor_copy(T.l2[:, c0:c0 + n], T.la[:, c0:c0 + n]), [("la", c)], [("l2", c)])
+            return
+        dve(n, lambda: V.tensor_scalar(T.rq_o[:, r0:r0 + n], T.ps[:, 0:n], 1023.5 + EXO, None, A.add), ["ps"], [("rq_o", t, c)], ["ps"])
+        send(rank + 1 + t, T.rq_i[:, r0:r0 + n], T.rq_o[:, r0:r0 + n], 256 * n, [("rq_o", t, c)], [("rq_i", t, c)], quick)
+        a0 = 768 * t + 16 * c0
+        dve(W, lambda: V.tensor_copy(T.an_o[:, a0:a0 + W], T.tab[:, 0:TABW].indirect(T.rq_i[:, r0:r0 + n])),
+            [("rq_i", t, c), "tabI", "tabD", ("tabE", 0), ("tabE", 1)], [("an_o", t, c)], k="g")
+        send(rank - 1 - t, T.an_i[:, a0:a0 + W], T.an_o[:, a0:a0 + W], 256 * W, [("an_o", t, c)], [("an_i", t, c)], quick)
+        pri[0] += MPRI
+        pe(128, [lambda: P.matmul(pv[0:n, 384:512], su[:], W2[1], True, True)], [("su", c), ("w2", 1)], [(pvk, "t")], [pvk])
+        act(128, lambda: S_.activation(sT[0:n, :], pv[0:n, 384:512], F.Identity), [(pvk, "t")], [("sT", c)], [pvk])
+        pe(W, [lambda: P.matmul(T.pe[:, 0:W], sT[0:n, :], T.ex16[0:n, 0:W], True, True)], [("sT", c), "ex16"], ["pe"], ["pe"])
+        dve(W, lambda: V.tensor_tensor(T["sm%d" % c][:], T["st%d" % c][:], T.pe[:, 0:W], A.mult), [("st", c), "pe"], [("sm", c)], ["pe"])
+
+    def back(c):
+        W, f0 = 16 * NS[c], 16 * C0[c]
+        if PREF:
+            pa = route(c, T["st%d" % c], T.r32e, T.r32o, 4, [("st", c), "r32e", "r32o"])
+            dve(W, lambda: V.transpose(T.pfx[:, f0:f0 + W], pa), pxk, [("pfs", c)], ["px"])
+        else:
+            pa = route(c, T["sm%d" % c], T.r32e, T.r32o, 4, [("sm", c), "r32e", "r32o", ("w2", 10), "fours"], True)
+            dve(W, lambda: V.transpose(T.smn[:, f0:f0 + W], pa), pxk, [("smn", c)], ["px"])
+
+    def finish(c):
+        n, W, f0, c0 = NS[c], 16 * NS[c], 16 * C0[c], C0[c]
+        xi, yo = T.xi[:, f0:f0 + W], T.yo[:, f0:f0 + W]
+        if PREF:
+            dve(W, lambda: V.tensor_scalar(yo, T.pfx[:, 0:2816].indirect(T.l2[:, c0:c0 + n]), 2048.0, None, A.add),
+                [("l2", c)] + [("pfs", k) for k in range(NC)] + [("pfe", k) for k in range(4)], [("yo", c)], k="g")
+            dve(W, lambda: V.tensor_tensor(xi, T.pfi[:, 0:EXO + 16].indirect(T.l1[:, c0:c0 + n]), yo, A.add),
+                [("l1", c), ("yo", c), "pfz", "pfd", ("pfi", 0), ("pfi", 1)], [("xi", c)], k="g")
+        else:
+            back(c)
+            dve(W, lambda: V.tensor_tensor(xi, T.an_i[:, 1536 + f0:1536 + f0 + W], T.smn[:, f0:f0 + W], A.add), [("an_i", 2, c), ("smn", c)], [("xi", c)], k=2)
+        dve(W, lambda: V.tensor_scalar(xi, xi, 4095, None, A.bitwise_and), [("xi", c)], [("xi", c)])
+        dve(W, lambda: V.tensor_copy(yo, xi), [("xi", c)], [("yo", c)])
+        dma("s", T.ys[:, f0:f0 + W], yo, 512 * W, [("yo", c)], [("ys", c)])
+
+    def halve(t):
+        rk = [("rq_i", t, k) for k in range(NC) if C0[k] < 8 * t + 8 and C0[k] + NS[k] > 8 * t]
+        r0, h0 = 56 * t, 144 * t
+        hi, ht = T.hi[:, h0:h0 + 128], T.hi[:, h0 + 128:h0 + 136]
+        if PREF and t == 2:
+            send(rank + 3, T.rq_i[:, r0:r0 + 8], T.rq_o[:, r0:r0 + 8], 2048, [("rq_o",) + x[1:] for x in rk], rk, quick)
+        dve(1, lambda: V.tensor_scalar(T.hl[:], T.rq_i[:, r0:r0 + 8], float(EXO), None, A.min), rk, ["hl"])
+        dve(1, lambda: V.tensor_scalar(T.hf[:], T.rq_i[:, r0:r0 + 8], float(EXO), None, A.min), rk, ["hf"])
+        act(1, lambda: S_.activation(T.nb[:], T.hf[:], F.Identity, scale=-256.0), ["hf"], ["nb"])
+        dve(128, lambda: V.tensor_tensor(T.rr[:], T.i256[:, 0:EXO + 16].indirect(T.hl[:, 0:8]), T.cf[:, 16:144], A.add), ["i256", "hl", "cf"], ["rr"], k="g")
+        dve(128, lambda: V.tensor_scalar(T.hv[:], T.tab[:, 0:EXO + 16].indirect(T.hl[:, 0:8]), 0.5, -0.25, A.mult, A.add),
+            ["tabI", "tabD", ("tabE", 0), "hl"], ["hv"], k="g")
+        dve(128, lambda: V.tensor_copy(hi, T.hv[:]), ["hv"], [("hi", t)])
+        for k in range(8):
+            o, w = 8 * k * (k + 1), 16 * (k + 1)
+            act(w, lambda k=k, o=o, w=w: S_.activation(T.dd[:, o:o + w], T.rr[:, 0:w], F.Abs, bias=T.nb[:, k:k + 1]), ["rr", "nb"], [("dd", k)])
+        for k in range(8):
+            o, w = 8 * k * (k + 1), 16 * (k + 1)
+            act(w, lambda k=k, o=o, w=w: S_.activation(T.dd[:, o:o + w], T.dd[:, o:o + w], F.Relu, bias=T.fid[:, k:k + 1], scale=-4096.0,
+                                                       accum_out=T.mn[:, k:k + 1]), [("dd", k), "fid"], [("dd", k), ("mn", k)])
+        dve(1, lambda: V.tensor_tensor(T.hg[:], T.mn[:], T.hf[:], A.max), [("mn", k) for k in range(8)] + ["hf"], ["hg"])
+        dve(1, lambda: V.tensor_tensor(ht, T.hg[:], T.dum[:], A.min), ["hg", "dum"], [("ht", t)])
+        dve(1, lambda: V.tensor_copy(T.tl[:], ht), [("ht", t)], ["tl"])
+        if t < 2:
+            dve(128, lambda: V.tensor_copy(T.tab[:, 0:EXO].indirect(T.tl[:, 0:8]), hi), ["tl", ("hi", t)], ["tabI", "tabD"], k="s")
+        else:
+            dve(128, lambda: V.tensor_copy(T.yit[:, 0:EXO].indirect(T.tl[:, 0:8]), hi), ["tl", ("hi", t)], ["yit"], k="s")
+            dma("s", T.yi[:], T.yit[:, 0:2048], 1 << 19, ["yit"], ["yi"])
+        if t == 1:
+            dma("q", T.yit[:, 0:2048], T.tab[:, 0:2048], 1 << 19, ["tabI"], ["yit"])
+        if PREF and t < 2:
+            send(rank - 3, T.hx[:, h0:h0 + 136], T.hi[:, h0:h0 + 136], 512 * 136, [("hi", t), ("ht", t)], [("hx", t)], quick)
+            pri[0] = 2 * NC - 0.5
+            dve(1, lambda: V.tensor_copy(T.tx[:], T.hx[:, h0 + 128:h0 + 136]), [("hx", t)], ["tx"])
+            dve(128, lambda: V.tensor_copy(T.pfi[:, 0:EXO].indirect(T.tx[:, 0:8]), T.hx[:, h0:h0 + 128]), ["tx", ("hx", t)],
+                [("pfi", 0), ("pfi", 1), "pfd"], k="s")
+
+    for t in range(3):
+        o0 = 256 * (t % 2)
+        pri[0] = -0.5 if t == 0 else NC * t - 0.5
+        pe(1024, [lambda t=t, o0=o0: P.matmul(T.po[:, o0:o0 + 256], T.bo[:], T.rt[:, 256 * t:256 * t + 256], True, True)],
+           ["bo", ("rt", t)], [("po", t % 2)], ["po"])
+        for c in range(NC):
+            pri[0] = -0.5 if t == 0 else NC * t + c
+            update(t, c)
+        if PREF and t == 2:
+            for c in range(NC):
+                pri[0] = NC * t + c + 0.7
+                back(c)
+        for c in range(NC):
+            pri[0] = NC * t + c
+            compute(t, c)
+        pri[0] = NC * t + NC - 1 + HPRI
+        halve(t)
+    for c in range(NC):
+        pri[0] = 2 * NC + c + 0.5
+        finish(c)
+    return ops
+
+
+def depend(ops):
+    last_w, readers, bank = {}, {}, {}
+    for k, o in enumerate(ops):
+        dep = set()
+        for x in o["r"]:
+            if x in last_w:
+                dep.add(last_w[x])
+        for x in o["w"]:
+            if x in last_w:
+                dep.add(last_w[x])
+            dep.update(readers.get(x, []))
+        for b in o["banks"]:
+            e, cur, prev = bank.get(b, (o["eng"], [], []))
+            if e != o["eng"]:
+                cur, prev = [], cur
+            dep.update(prev)
+            if o["eng"] == "p":
+                dep.update(cur[-1:])
+            bank[b] = (o["eng"], cur + [k], prev)
+        for x in o["r"]:
+            readers.setdefault(x, []).append(k)
+        for x in o["w"]:
+            last_w[x] = k
+            readers[x] = []
+        dep.discard(k)
+        o["dep"] = sorted(dep)
+
+
+def costs(ops, m):
+    cy, gam, sca, pcy, rfix, rbw, riss, dbw = m[:8]
+    out = []
+    for o in ops:
+        e, n, k = o["eng"], o["n"], o["k"]
+        if o["kind"] == "d":
+            out.append((1000.0 if e == "q" else 100.0, n / dbw))
+        elif o["kind"] == "r":
+            out.append((riss, n / (rbw if len(k) == 2 else 0.6 * rbw)))
+        elif e == "p":
+            out.append((n * pcy, 60.0))
+        elif e == "q":
+            out.append((130 + 2 * n * cy, 0.0))
+        elif k in ("g", "s"):
+            out.append((55 + n * cy * (gam if k == "g" else sca), 0.0))
+        else:
+            out.append((40 + max(64, n * k) * cy, 0.0))
+    return out
+
+
+def replay(ops, order, cost, m, why=None):
+    hop, first = m[8], m[9]
+    free = {"v": 0.0, "a": 0.0, "p": 0.0, "q": 0.0, "s": 0.0}
+    prev, port = {}, [0.0, 0.0]
+    end = [0.0] * len(ops)
+    wire, seen, last, lastk = 0.0, set(), 0.0, 0
+    for k in order:
+        e, kind, dep = ops[k]["key"]
+        t, w = free[e], prev.get(e, -1)
+        for j in dep:
+            if end[j] > t:
+                t, w = end[j] + hop, -2 - j
+        occ, lat = cost[k]
+        t += occ
+        if kind != "c":
+            if e == "q" and kind not in seen:
+                seen.add(kind)
+                t += first
+            if kind == "d":
+                wire = max(wire, t) + lat
+                lat = wire - t + 2000.0
+            else:
+                out = max([t] + [port[h] for h in ops[k]["k"]]) + lat
+                for h in ops[k]["k"]:
+                    port[h] = out
+                lat = out - t + m[4] - m[6]
+        free[e], prev[e], end[k] = t, k, t + lat
+        if why is not None:
+            why[k] = w
+        if t + lat > last:
+            last, lastk = t + lat, k
+    return last, lastk
+
+
+def schedule(ops):
+    n = len(ops)
+    for o in ops:
+        o["key"] = (o["eng"], o["kind"], [j for j in o["dep"] if o["eng"] != "p" or ops[j]["eng"] != "p"])
+    cost = [costs(ops, m) for m in MODELS]
+    succ = [[] for _ in range(n)]
+    for k, o in enumerate(ops):
+        for j in o["dep"]:
+            succ[j].append(k)
+    left = [len(o["dep"]) for o in ops]
+    lim, start, cum = [0.0] * n, [0.0] * n, 0.0
+    busy = {e: [] for e in "vapqs"}
+    pool = [k for k in range(n) if left[k] == 0]
+    while pool:
+        k = min(pool, key=lambda j: (ops[j]["pri"], j))
+        pool.remove(k)
+        occ, lat = cost[0][k]
+        if ops[k]["kind"] == "d":
+            cum = cum + lat if ops[k]["pri"] < 0 else lat
+            lat = cum + 2000.0
+        if ops[k]["kind"] == "r":
+            lat += MODELS[0][4] - MODELS[0][6]
+        t = lim[k]
+        for lo, hi in busy[ops[k]["eng"]]:
+            if t + occ <= lo:
+                break
+            t = max(t, hi)
+        busy[ops[k]["eng"]].append((t, t + occ))
+        busy[ops[k]["eng"]].sort()
+        start[k] = t
+        for j in succ[k]:
+            lim[j] = max(lim[j], t + occ + lat + MODELS[0][8])
+            left[j] -= 1
+            if left[j] == 0:
+                pool.append(j)
+    order = sorted(range(n), key=lambda k: (start[k], k))
+    base = [replay(ops, order, c, m)[0] for c, m in zip(cost, MODELS)]
+    score = lambda od: sum(replay(ops, od, c, m)[0] / b_ for c, m, b_ in zip(cost, MODELS, base))
+    seed = [SEED]
+
+    def rnd():
+        seed[0] = (seed[0] * 1103515245 + 12345) % 2147483648
+        return seed[0] / 2147483648.0
+
+    cur = best = score(order)
+    best_order = order
+    why = [0] * n
+    for it in range(ITERS):
+        i = int(rnd() * len(MODELS))
+        k = replay(ops, order, cost[i], MODELS[i], why)[1]
+        pairs = []
+        while k != -1:
+            w = why[k]
+            if w >= 0 and w not in ops[k]["dep"] and ops[w]["kind"] != "d":
+                pairs.append((w, k))
+            k = w if w >= -1 else -2 - w
+        if not pairs:
+            continue
+        j, k = pairs[int(rnd() * len(pairs))]
+        seg = order[order.index(j):order.index(k) + 1]
+        if rnd() < 0.5:
+            take = {k}
+            for x in reversed(seg[:-1]):
+                if any(y in take for y in succ[x]):
+                    take.add(x)
+            if j in take:
+                continue
+            new = [x for x in seg if x in take] + [x for x in seg if x not in take]
+        else:
+            take = {j}
+            for x in seg[1:]:
+                if any(y in take for y in ops[x]["dep"]):
+                    take.add(x)
+            if k in take:
+                continue
+            new = [x for x in seg if x not in take] + [x for x in seg if x in take]
+        p0 = order.index(j)
+        cand = order[:p0] + new + order[p0 + len(seg):]
+        val = score(cand)
+        if val < cur + TEMP * (1.0 - it / ITERS) * rnd():
+            order, cur = cand, val
+            if val < best:
+                best, best_order = val, cand
+    return best_order
+
+
+ORDER = {}
+
+
+def rank_program(g, core, T, topo):
+    if T.rank_of(core) is None:
+        return
+    ops = build(g, core, T, topo)
+    depend(ops)
+    if "order" not in ORDER:
+        ORDER["order"] = schedule(ops)
+    Q = {"v": g.vector, "a": g.scalar, "p": g.tensor, "q": g, "s": g.sync}
+    count = {"v": 0, "a": 0, "p": 0, "q": 0}
+    known = {e: {} for e in Q}
+    done, total = {}, {}
+    nd, loc = 0, 0
+    for k in ORDER["order"]:
+        o = ops[k]
+        e = o["eng"]
+        need = {}
+        for j in o["dep"]:
+            if e == "p" and ops[j]["eng"] == "p":
+                continue
+            s, val = done[j]
+            need[s] = max(need.get(s, 0), val)
+        for s, val in need.items():
+            if known[e].get(s, 0) < val:
+                Q[e].wait_ge(T.sem[s], val)
+                known[e][s] = val
+        ins = [fn() for fn in o["fns"]][-1]
+        if o["kind"] == "c":
+            count[e] += 1
+            ins.then_inc(T.sem[e], 1)
+            done[k] = (e, count[e])
+        elif o["kind"] == "d":
+            done[k] = ("d%d" % nd, 16)
+            ins.then_inc(T.sem["d%d" % nd], 16)
+            nd += 1
+        else:
+            done[k] = o["sem"]
+            loc += o["sem"][1]
+        total[done[k][0]] = done[k][1]
+    total["loc"] = loc
+    for s, val in total.items():
+        if all(known[e].get(s, 0) < val for e in Q):
+            g.sync.wait_ge(T.sem[s], val)

@@ -1,11 +1,11 @@
 from concourse.mybir import AluOpType as A, ActivationFunctionType as F
 
 NS = [16, 16, 16]
-SPLIT = [(4, 4, 11), (4, 4, 11), (3, 3, 10)]
-PA, PV = 2, 2
-PREF = True
+CO = [1, 0, 2]
+SPLIT = [(4, 4, 11), (4, 4, 10), (3, 4, 10)]
+PA, PV = 4, 4
 HPRI, MPRI = 0.5, 1.5
-SEED, ITERS, TEMP = 1, 22000, 0.05
+SEED, ITERS, TEMP = 1, 52000, 0.03
 MODELS = [(1.04, 1.5, 3.8, 0.53, 2700, 60.0, 700, 250.0, 100, 2000), (0.85, 1.15, 2.0, 0.43, 2000, 100.0, 400, 350.0, 70, 1200),
           (1.2, 1.95, 5.5, 0.62, 3500, 40.0, 1000, 180.0, 150, 3000)]
 NC = len(NS)
@@ -25,23 +25,20 @@ SCRATCH = {
     "iC": _sb(256, "bfloat16"), "i256": _sb(EXO + 16, "float32"),
     "r16e": _sb(160, "float16"), "r16o": _sb(160, "float16"), "r32e": _sb(160, "float32"), "r32o": _sb(160, "float32"),
     "bo": _sb(128, "float32"), "rep": _sb(128, "float32"), "rt": _sb(768, "float32"), "ub": _sb(144, "bfloat16"), "uh": _sb(144, "bfloat16"),
-    "w2": _sb(14 * 128, "bfloat16"), "ex16": _sb(256, "bfloat16"), "ones": _sb(256, "bfloat16"), "fours": _sb(128, "bfloat16"),
+    "w2": _sb(14 * 128, "bfloat16"), "ex16": _sb(256, "bfloat16"), "ones": _sb(256, "bfloat16"),
     "fid": _sb(8, "float32"), "dum": _sb(8, "float32"), "fall": _sb(48, "float32"), "s16": _sb(768, "float16"),
-    "rq_o": _sb(144, "uint16"), "rq_i": _sb(144, "uint16"), "an_o": _sb(2304, "float16"), "an_i": _sb(2304, "float16"),
-    "xi": _sb(768, "int32"), "smn": _sb(768, "float32"), "yo": _sb(768, "float32"),
+    "rq_o": _sb(144, "uint16"), "rq_i": _sb(144, "uint16"), "an_o": _sb(1536, "float16"), "an_i": _sb(1536, "float16"),
+    "xi": _sb(768, "int32"), "yo": _sb(768, "float32"),
     "hf": _sb(8, "float32"), "hg": _sb(8, "float32"), "nb": _sb(8, "float32"), "mn": _sb(8, "float32"),
     "hl": _sb(8, "uint16"), "tl": _sb(8, "uint16"), "tx": _sb(8, "uint16"),
     "rr": _sb(128, "float32"), "dd": _sb(576, "float32"), "hv": _sb(128, "float32"), "hi": _sb(432, "int32"), "hx": _sb(288, "int32"),
-    "la": _sb(48, "float32"), "l1": _sb(48, "uint16"), "l2": _sb(48, "uint16"),
+    "la": _sb(48, "float32"), "l1": _sb(48, "uint16"), "l2": _sb(48, "uint16"), "pm16": _sb(16, "uint16"),
     "px": ("psum", [128, 16, 2, 16], "float32"),
 }
 for _k in ("po", "ps", "pe", "pv0", "pv1", "pd0", "pd1"):
     SCRATCH[_k] = ("psum", [128, 512], "float32")
 for _c in range(NC):
     _n = NS[_c]
-    SCRATCH["pm%d" % _n] = _sb(_n, "uint16")
-    SCRATCH["pf%d" % _n] = _sb(2 * _n, "float32")
-    SCRATCH["pq%d" % _n] = _sb(_n, "int32")
     SCRATCH["aT%d" % _c] = ("sbuf", [128, _n // 2, 2, 16], "float16")
     SCRATCH["sm%d" % _c] = ("sbuf", [128, _n // 2, 2, 16], "float32")
     SCRATCH["st%d" % _c] = ("sbuf", [128, _n // 2, 2, 16], "float32")
@@ -57,6 +54,15 @@ SEMAPHORES = ["v", "a", "p", "q", "loc"] + ["d%d" % k for k in range(24)] + ["r%
 def pieces(lo, hi, k):
     m = -(-(hi - lo) // k)
     return [(lo + (hi - lo) * j // m, lo + (hi - lo) * (j + 1) // m) for j in range(m)] if hi > lo else []
+
+
+def relays(core, T, topo):
+    dst = T.cores[(T.rank_of(core) - 3) % len(T.cores)]
+    return dst, [h for h in topo.cores_of(core) if T.rank_of(h) is None and topo.die(h) != topo.die(core) and topo.may_write(h, dst)]
+
+
+def landing(T):
+    return [T.pfi[:, 1024 * k:1024 * k + 1024] for k in range(2)] + [T.pfx[:, 768 + 512 * k:1280 + 512 * k] for k in range(4)]
 
 
 def build(g, core, T, topo):
@@ -84,33 +90,34 @@ def build(g, core, T, topo):
         Q = {"s": g.sync, "a": S_, "q": g}[q]
         add(q, nbytes, [lambda: Q.dma_start(out, in_)], r, w, kind="d")
 
-    def send(dst_rank, out, in_, nbytes, r, w, lanes):
+    def send(dst_rank, out, in_, nbytes, r, w, relay=False):
         dst = T.cores[dst_rank % N]
-        rid, pid, _ = topo.addr(dst)
-        eng = topo.engines(core, dst)
-        half = len(eng) // 2
-        eng = eng[half * lanes[0]:half * (lanes[-1] + 1)]
         k = cnt["r"]
         cnt["r"] += 1
+        eng = topo.engines(core, dst)
+        arrive = len(eng)
+        if relay:
+            hs = relays(core, T, topo)[1]
+            h = hs[k % len(hs)]
+            eng = [e for e in topo.engines(core, h) if e not in eng]
+            arrive = len(topo.engines(h, dst))
+            dst = h
+        rid, pid, _ = topo.addr(dst)
         add("q", nbytes, [lambda: g.remote_dma(out, in_, T.sem["r%d" % k], T.sem.loc, pid, rid, sum(1 << e for e in eng))],
-            r, w, k=lanes, kind="r", sem=("r%d" % k, len(eng)))
+            r, w, k=(2,) if relay else (0, 1), kind="r", sem=("r%d" % k, arrive, len(eng)))
 
     def iota(out, pat, base, cm, n, key):
         add("q", n, [lambda: g.iota(out, pat, base, cm, allow_small_or_imprecise_dtypes=True)], [], [key])
 
-    quick = (0,) if PREF else (0, 1)
     W2 = [T.w2[:, 128 * m:128 * (m + 1)] for m in range(14)]
     col = [T.cl[:, k:k + 1] for k in range(6)]
     main = T.pic_s[:, PAD:PAD + 4096]
 
-    W0 = 16 * NS[0]
-    dma("s", T.shp_s[:, 0:W0], T.shp[:, 0:W0], 512 * W0, [], [("shp", 0)])
+    dma("s", T.shp_s[:], T.shp[:], 512 * 768, [], [("shp", c) for c in range(NC)])
     dma("a", T.ofs_s[:, 0:3], T.ofs[:], 1536, [], ["ofs"])
-    dma("s", T.shp_s[:, W0:768], T.shp[:, W0:768], 512 * (768 - W0), [], [("shp", c) for c in range(1, NC)])
     dma("s", main, T.pic[:], 1 << 20, [], ["pic"])
     dma("a", T.thr_s[0:8, 0:3], T.thr[:], 96, [], ["thr"])
-    if PREF:
-        dma("s", T.inc_s[:], T.inc[:], 1 << 19, [], ["inc_s"])
+    dma("s", T.inc_s[:], T.inc[:], 1 << 19, [], ["inc_s"])
     dma("s", T.ex_s[:, 0:1024], T.ex[:, 0:1024], 1 << 19, [], [("ex", 0)])
     dma("s", T.ex_s[:, 1024:2048], T.ex[:, 1024:2048], 1 << 19, [], [("ex", 1)])
 
@@ -119,7 +126,7 @@ def build(g, core, T, topo):
     iota(T.iI[:], [[0, 16], [1, 16]], 0, 0, 256, "iI")
     iota(T.iG[:], [[16, 8], [0, 16]], 0, 0, 128, "iG")
     iota(T.iC[:], [[1, 16], [0, 16]], 0, 0, 256, "iC")
-    dma("q", T.tab[:, 0:2048], T.inc[:], 1 << 20, ["iC"], ["tabI"])
+    dma("q", T.tab[:, 0:2048], T.inc[:], 1 << 20, ["pic"], ["tabI"])
     iota(T.i256[:], [[256, EXO + 16]], 0, 0, EXO + 16, "i256")
     dma("s", T.pic_s[:, PAD + 4096:PAD + 8192], T.pic[:], 1 << 20, [("ex", 1)], ["picx1"])
     dma("s", T.pic_s[:, 0:PAD], T.pic[:, 4096 - PAD:4096], 1 << 17, [("ex", 1)], ["picx0"])
@@ -139,22 +146,12 @@ def build(g, core, T, topo):
     for t in range(3):
         dve(256, lambda t=t: V.tensor_scalar(T.rt[:, 256 * t:256 * t + 256], T.iI[:], col[1], T.oc[:, t:t + 1], A.is_equal, A.mult),
             ["iI", "cl", ("oc", t)], [("rt", t)])
-    for n in sorted(set(NS)):
-        if n == 16:
-            dve(1, lambda: V.tensor_scalar(T.pm16[:], T.cf[:, 16:32], col[5], None, A.add), ["cf", "cl5"], ["pm16"])
-            continue
-        pf, pq = T["pf%d" % n], T["pq%d" % n]
-        dve(1, lambda n=n, pf=pf: V.tensor_scalar(pf[:, 0:n], T.cf[:, 16:16 + n], 16.0, col[1], A.mult, A.add), ["cf", "cl"], [("pf", n)])
-        dve(1, lambda n=n, pf=pf: V.tensor_scalar(pf[:, n:2 * n], pf[:, 0:n], 1.0 / n, 0.5 / n - 0.5, A.mult, A.add), [("pf", n)], [("pg", n)])
-        dve(1, lambda n=n, pf=pf, pq=pq: V.tensor_copy(pq[:], pf[:, n:2 * n]), [("pg", n)], [("pq", n)])
-        dve(1, lambda n=n, pf=pf, pq=pq: V.tensor_scalar(pf[:, n:2 * n], pq[:], (1.0 - 16 * n) / 16, None, A.mult), [("pq", n)], [("pg", n)])
-        dve(1, lambda n=n, pf=pf: V.tensor_tensor(pf[:, 0:n], pf[:, 0:n], pf[:, n:2 * n], A.add), [("pf", n), ("pg", n)], [("pf", n)])
-        dve(1, lambda n=n, pf=pf: V.tensor_scalar(T["pm%d" % n][:], pf[:, 0:n], 16.0, None, A.mult), [("pf", n)], ["pm%d" % n])
+    dve(1, lambda: V.tensor_scalar(T.pm16[:], T.cf[:, 16:32], col[5], None, A.add), ["cf", "cl5"], ["pm16"])
     dve(143, lambda: V.tensor_scalar(T.ub[:, 0:143], T.cf[:, 1:144], col[2], None, A.is_equal), ["cf", "cl"], ["ub"], k=0.5)
     act(143, lambda: S_.activation(T.uh[:, 0:143], T.ub[:, 0:143], F.Identity, scale=0.5), ["ub"], ["uh"])
     dve(128, lambda: V.tensor_scalar(W2[1], T.cf[:, 16:144], col[0], None, A.is_equal), ["cf", "cl"], [("w2", 1)], k=0.5)
     for m in (11, 4, 0, 2, 3, 5, 6, 7, 8, 9, 10, 12, 13):
-        sc = -1.0 if m == 11 else -float(EXO) if m == 12 else -4096.0 if m == 13 else 2.0 ** (m - 1)
+        sc = -1.0 if m == 11 else -EXO / 2.0 if m == 12 else -2048.0 if m == 13 else 2.0 ** (m - 1)
         act(128, lambda m=m, sc=sc: S_.activation(W2[m], W2[1], F.Identity, scale=sc), [("w2", 1)], [("w2", m)])
     dve(256, lambda: V.tensor_scalar(T.ex16[:], T.iC[:], col[0], None, A.is_equal), ["iC", "cl"], ["ex16"], k=0.5)
     dve(256, lambda: V.memset(T.ones[:], 1.0), [], ["ones"], k=0.5)
@@ -162,36 +159,30 @@ def build(g, core, T, topo):
     dve(1, lambda: V.tensor_scalar(T.fid[:], T.iG[:, 0:128:16], col[1], 4096.0, A.add, A.mult), ["iG", "cl"], ["fid"])
     dve(1, lambda: V.tensor_scalar(T.dum[:], T.iG[:, 0:128:16], col[1], float(SPARE), A.add, A.add), ["iG", "cl"], ["dum"])
     dve(128, lambda: V.tensor_scalar(T.rep[0:8, :], T.iG[0:8, :], 0.0625, T.cl[0:8, 0:1], A.mult, A.is_equal), ["iG", "cl"], ["rep"])
-    dve(1, lambda: V.tensor_scalar(T.thf[0:8, 0:3], T.thr_s[0:8, 0:3], 2.0, -11.0, A.mult, A.add), ["thr"], ["thf"])
+    dve(1, lambda: V.tensor_scalar(T.thf[0:8, 0:3], T.thr_s[0:8, 0:3], -2.0, 11.5, A.mult, A.add), ["thr"], ["thf"])
     pe(256, [lambda: P.matmul(T.ps[:, 0:3], T.rep[0:8, :], T.thf[0:8, 0:3], True, True)], ["rep", "thf"], ["ps"], ["ps"])
     act(1, lambda: S_.activation(T.thc[:, 0:3], T.ps[:, 0:3], F.Identity), ["ps"], ["thc"], ["ps"])
     pri[0] = 0.5
     for k in range(2):
         dve(1024, lambda k=k: V.tensor_scalar(T.tab[:, EXO + 1024 * k:EXO + 1024 * k + 1024], T.ex_s[:, 1024 * k:1024 * k + 1024], -2048.0, None, A.add),
             [("ex", k)], [("tabE", k)])
-    if PREF:
-        dve(144, lambda: V.memset(T.pfi[:, SPARE:EXO + 16], 0.0), [], ["pfz", "pfd"], k=0.5)
-        dve(48, lambda: V.tensor_scalar(T.fall[:], T.cf[:, 16:64], 16.0, col[1], A.mult, A.add), ["cf", "cl"], ["fall"])
-        pri[0] = -0.9
-        for k in range(2):
-            send(rank - 3, T.pfi[:, 1024 * k:1024 * k + 1024], T.inc_s[:, 1024 * k:1024 * k + 1024], 1 << 18, ["inc_s"], [("pfi", k)],
-                 (0, 1) if k == 0 else (1,))
-        pri[0] = 0.6
-        for k in range(4):
-            send(rank - 3, T.pfx[:, 768 + 512 * k:1280 + 512 * k], T.tab[:, EXO + 512 * k:EXO + 512 * k + 512], 1 << 18,
-                 [("tabE", k // 2)], [("pfe", k)], (1,))
-    else:
-        dve(128, lambda: V.memset(T.fours[:], 4.0), [], ["fours"], k=0.5)
+    dve(144, lambda: V.memset(T.pfi[:, SPARE:EXO + 16], 0.0), [], ["pfz", "pfd"], k=0.5)
+    dve(48, lambda: V.tensor_scalar(T.fall[:], T.cf[:, 16:64], 16.0, col[1], A.mult, A.add), ["cf", "cl"], ["fall"])
+    land = landing(T)
+    pri[0] = -0.9
+    for k in range(2):
+        send(rank - 3, land[k], T.inc_s[:, 1024 * k:1024 * k + 1024], 1 << 18, ["inc_s"], [("pfi", k)], True)
+    pri[0] = 0.6
+    for k in range(4):
+        send(rank - 3, land[2 + k], T.tab[:, EXO + 512 * k:EXO + 512 * k + 512], 1 << 18, [("tabE", k // 2)], [("pfe", k)], True)
     pxk = [("px", 0), ("px", 1)]
 
-    def route(c, src, e, o, cyc, key, const=False):
+    def route(c, src, e, o, cyc, key):
         h2 = NS[c] // 2
         E = [[e[:, 16:144], e[:, 0:128]], [o[:, 32:160], o[:, 16:144]]]
         for x in range(2):
-            fns = [lambda x=x, y=y: P.matmul(T.px[:, 0:h2, x, :], E[x][y], src[:, :, y, :], y == 0, y == 1 and not const) for y in range(2)]
-            if const:
-                fns.append(lambda x=x: P.matmul(T.px[:, 0:h2, x, :], W2[10], T.fours[:, 0:16 * h2], False, True))
-            pe(2 * max(64, 16 * h2) * cyc + (16 * h2 if const else 0), fns, key, [("px", x)], ["px"])
+            pe(2 * max(64, 16 * h2) * cyc, [lambda x=x, y=y: P.matmul(T.px[:, 0:h2, x, :], E[x][y], src[:, :, y, :], y == 0, y == 1) for y in range(2)],
+               key, [("px", x)], ["px"])
         return T.px[:, 0:h2]
 
     def update(t, c):
@@ -213,8 +204,8 @@ def build(g, core, T, topo):
         dve(W, lambda: V.tensor_tensor(xi, st[:], T.po[:, o0:o0 + W], A.add), [("st", c), ("po", t % 2)], [("xi", c)], ["po"])
         if t == 0:
             dve(W, lambda: V.tensor_scalar(xi, xi, 4095, None, A.bitwise_and), [("xi", c)], [("xi", c)])
-        k = ((16 - t) * n + 15) // 16
-        dve(16 * k, lambda: V.tensor_copy(li[:, 0:16 * k], xi.indirect(T["pm%d" % n][:, 0:k])), [("xi", c), "pm%d" % n], [("li", c)], k="g")
+        k = 16 - t
+        dve(16 * k, lambda: V.tensor_copy(li[:, 0:16 * k], xi.indirect(T.pm16[:, 0:k])), [("xi", c), "pm16"], [("li", c)], k="g")
 
     def compute(t, c):
         n, W, d = NS[c], 16 * NS[c], 5 - t
@@ -271,51 +262,42 @@ def build(g, core, T, topo):
            [("bb", c, 0)] + [("w2", m) for m in range(11)], ["ps"], ["ps"])
         pe(11 * 64, [lambda m=m: P.matmul(pv[:, 256:256 + n], W2[1], bb[:, q + m * n:q + (m + 1) * n], m == 0, m == 10) for m in range(11)],
            [("bb", c, 1), ("w2", 1)], [(pvk, "c")], [pvk])
-        dve(n, lambda: V.tensor_scalar(su[:], pv[:, 256:256 + n], T.thc[:, t:t + 1], None, A.is_ge), [(pvk, "c"), "thc"], [("su", c)], [pvk])
-        last = PREF and t == 2
-        wu = 13 if last else 12
+        act(n, lambda: S_.activation(su[:], pv[:, 256:256 + n], F.Sign, bias=T.thc[:, t:t + 1]), [(pvk, "c"), "thc"], [("su", c)], [pvk])
+        wu = 13 if t == 2 else 12
         pe(64, [lambda: P.matmul(T.ps[:, 0:n], W2[wu], su[:], False, True)], [("su", c), ("w2", wu)], ["ps"], ["ps"])
         r0, c0 = 48 * t + C0[c], C0[c]
-        if last:
-            dve(n, lambda: V.tensor_scalar(T.la[:, c0:c0 + n], T.ps[:, 0:n], 1023.5 + 768, None, A.add), ["ps"], [("la", c)], ["ps"])
-            dve(n, lambda: V.tensor_scalar(T.l1[:, c0:c0 + n], T.ps[:, 0:n], 1023.5 + 4096, float(EXO), A.add, A.min), ["ps"], [("l1", c)], ["ps"])
+        if t == 2:
+            dve(n, lambda: V.tensor_scalar(T.la[:, c0:c0 + n], T.ps[:, 0:n], 1023.5 + 768 - 2048, None, A.add), ["ps"], [("la", c)], ["ps"])
+            dve(n, lambda: V.tensor_scalar(T.l1[:, c0:c0 + n], T.ps[:, 0:n], 1023.5 + 2048, float(EXO), A.add, A.min), ["ps"], [("l1", c)], ["ps"])
             if c0 < 24 and c0 + n > 16:
-                dve(n, lambda: V.tensor_scalar(T.rq_o[:, r0:r0 + n], T.ps[:, 0:n], 1023.5 + 4096, None, A.add), ["ps"], [("rq_o", t, c)], ["ps"])
+                dve(n, lambda: V.tensor_scalar(T.rq_o[:, r0:r0 + n], T.ps[:, 0:n], 1023.5 + 2048, None, A.add), ["ps"], [("rq_o", t, c)], ["ps"])
             dve(n, lambda: V.tensor_tensor(T.la[:, c0:c0 + n], T.la[:, c0:c0 + n], T.fall[:, c0:c0 + n], A.max), [("la", c), "fall"], [("la", c)])
             dve(n, lambda: V.tensor_copy(T.l2[:, c0:c0 + n], T.la[:, c0:c0 + n]), [("la", c)], [("l2", c)])
             return
-        dve(n, lambda: V.tensor_scalar(T.rq_o[:, r0:r0 + n], T.ps[:, 0:n], 1023.5 + EXO, None, A.add), ["ps"], [("rq_o", t, c)], ["ps"])
-        send(rank + 1 + t, T.rq_i[:, r0:r0 + n], T.rq_o[:, r0:r0 + n], 256 * n, [("rq_o", t, c)], [("rq_i", t, c)], quick)
+        dve(n, lambda: V.tensor_scalar(T.rq_o[:, r0:r0 + n], T.ps[:, 0:n], 1023.5 + EXO / 2, None, A.add), ["ps"], [("rq_o", t, c)], ["ps"])
+        send(rank + 1 + t, T.rq_i[:, r0:r0 + n], T.rq_o[:, r0:r0 + n], 256 * n, [("rq_o", t, c)], [("rq_i", t, c)])
         a0 = 768 * t + 16 * c0
         dve(W, lambda: V.tensor_copy(T.an_o[:, a0:a0 + W], T.tab[:, 0:TABW].indirect(T.rq_i[:, r0:r0 + n])),
             [("rq_i", t, c), "tabI", "tabD", ("tabE", 0), ("tabE", 1)], [("an_o", t, c)], k="g")
-        send(rank - 1 - t, T.an_i[:, a0:a0 + W], T.an_o[:, a0:a0 + W], 256 * W, [("an_o", t, c)], [("an_i", t, c)], quick)
+        send(rank - 1 - t, T.an_i[:, a0:a0 + W], T.an_o[:, a0:a0 + W], 256 * W, [("an_o", t, c)], [("an_i", t, c)])
         pri[0] += MPRI
         pe(128, [lambda: P.matmul(pv[0:n, 384:512], su[:], W2[1], True, True)], [("su", c), ("w2", 1)], [(pvk, "t")], [pvk])
-        act(128, lambda: S_.activation(sT[0:n, :], pv[0:n, 384:512], F.Identity), [(pvk, "t")], [("sT", c)], [pvk])
+        act(128, lambda: S_.activation(sT[0:n, :], pv[0:n, 384:512], F.Relu), [(pvk, "t")], [("sT", c)], [pvk])
         pe(W, [lambda: P.matmul(T.pe[:, 0:W], sT[0:n, :], T.ex16[0:n, 0:W], True, True)], [("sT", c), "ex16"], ["pe"], ["pe"])
         dve(W, lambda: V.tensor_tensor(T["sm%d" % c][:], T["st%d" % c][:], T.pe[:, 0:W], A.mult), [("st", c), "pe"], [("sm", c)], ["pe"])
 
     def back(c):
         W, f0 = 16 * NS[c], 16 * C0[c]
-        if PREF:
-            pa = route(c, T["st%d" % c], T.r32e, T.r32o, 4, [("st", c), "r32e", "r32o"])
-            dve(W, lambda: V.transpose(T.pfx[:, f0:f0 + W], pa), pxk, [("pfs", c)], ["px"])
-        else:
-            pa = route(c, T["sm%d" % c], T.r32e, T.r32o, 4, [("sm", c), "r32e", "r32o", ("w2", 10), "fours"], True)
-            dve(W, lambda: V.transpose(T.smn[:, f0:f0 + W], pa), pxk, [("smn", c)], ["px"])
+        pa = route(c, T["st%d" % c], T.r32e, T.r32o, 4, [("st", c), "r32e", "r32o"])
+        dve(W, lambda: V.transpose(T.pfx[:, f0:f0 + W], pa), pxk, [("pfs", c)], ["px"])
 
     def finish(c):
         n, W, f0, c0 = NS[c], 16 * NS[c], 16 * C0[c], C0[c]
         xi, yo = T.xi[:, f0:f0 + W], T.yo[:, f0:f0 + W]
-        if PREF:
-            dve(W, lambda: V.tensor_scalar(yo, T.pfx[:, 0:2816].indirect(T.l2[:, c0:c0 + n]), 2048.0, None, A.add),
-                [("l2", c)] + [("pfs", k) for k in range(NC)] + [("pfe", k) for k in range(4)], [("yo", c)], k="g")
-            dve(W, lambda: V.tensor_tensor(xi, T.pfi[:, 0:EXO + 16].indirect(T.l1[:, c0:c0 + n]), yo, A.add),
-                [("l1", c), ("yo", c), "pfz", "pfd", ("pfi", 0), ("pfi", 1)], [("xi", c)], k="g")
-        else:
-            back(c)
-            dve(W, lambda: V.tensor_tensor(xi, T.an_i[:, 1536 + f0:1536 + f0 + W], T.smn[:, f0:f0 + W], A.add), [("an_i", 2, c), ("smn", c)], [("xi", c)], k=2)
+        dve(W, lambda: V.tensor_scalar(yo, T.pfx[:, 0:2816].indirect(T.l2[:, c0:c0 + n]), 2048.0, None, A.add),
+            [("l2", c)] + [("pfs", k) for k in range(NC)] + [("pfe", k) for k in range(4)], [("yo", c)], k="g")
+        dve(W, lambda: V.tensor_tensor(xi, T.pfi[:, 0:EXO + 16].indirect(T.l1[:, c0:c0 + n]), yo, A.add),
+            [("l1", c), ("yo", c), "pfz", "pfd", ("pfi", 0), ("pfi", 1)], [("xi", c)], k="g")
         dve(W, lambda: V.tensor_scalar(xi, xi, 4095, None, A.bitwise_and), [("xi", c)], [("xi", c)])
         dve(W, lambda: V.tensor_copy(yo, xi), [("xi", c)], [("yo", c)])
         dma("s", T.ys[:, f0:f0 + W], yo, 512 * W, [("yo", c)], [("ys", c)])
@@ -324,13 +306,13 @@ def build(g, core, T, topo):
         rk = [("rq_i", t, k) for k in range(NC) if C0[k] < 8 * t + 8 and C0[k] + NS[k] > 8 * t]
         r0, h0 = 56 * t, 144 * t
         hi, ht = T.hi[:, h0:h0 + 128], T.hi[:, h0 + 128:h0 + 136]
-        if PREF and t == 2:
-            send(rank + 3, T.rq_i[:, r0:r0 + 8], T.rq_o[:, r0:r0 + 8], 2048, [("rq_o",) + x[1:] for x in rk], rk, quick)
+        if t == 2:
+            send(rank + 3, T.rq_i[:, r0:r0 + 8], T.rq_o[:, r0:r0 + 8], 2048, [("rq_o",) + x[1:] for x in rk], rk)
         dve(1, lambda: V.tensor_scalar(T.hl[:], T.rq_i[:, r0:r0 + 8], float(EXO), None, A.min), rk, ["hl"])
         dve(1, lambda: V.tensor_scalar(T.hf[:], T.rq_i[:, r0:r0 + 8], float(EXO), None, A.min), rk, ["hf"])
         act(1, lambda: S_.activation(T.nb[:], T.hf[:], F.Identity, scale=-256.0), ["hf"], ["nb"])
         dve(128, lambda: V.tensor_tensor(T.rr[:], T.i256[:, 0:EXO + 16].indirect(T.hl[:, 0:8]), T.cf[:, 16:144], A.add), ["i256", "hl", "cf"], ["rr"], k="g")
-        dve(128, lambda: V.tensor_scalar(T.hv[:], T.tab[:, 0:EXO + 16].indirect(T.hl[:, 0:8]), 0.5, -0.25, A.mult, A.add),
+        act(128, lambda: S_.activation(T.hv[:], T.tab[:, 0:EXO + 16].indirect(T.hl[:, 0:8]), F.Identity, bias=-0.25, scale=0.5),
             ["tabI", "tabD", ("tabE", 0), "hl"], ["hv"], k="g")
         dve(128, lambda: V.tensor_copy(hi, T.hv[:]), ["hv"], [("hi", t)])
         for k in range(8):
@@ -350,8 +332,8 @@ def build(g, core, T, topo):
             dma("s", T.yi[:], T.yit[:, 0:2048], 1 << 19, ["yit"], ["yi"])
         if t == 1:
             dma("q", T.yit[:, 0:2048], T.tab[:, 0:2048], 1 << 19, ["tabI"], ["yit"])
-        if PREF and t < 2:
-            send(rank - 3, T.hx[:, h0:h0 + 136], T.hi[:, h0:h0 + 136], 512 * 136, [("hi", t), ("ht", t)], [("hx", t)], quick)
+        if t < 2:
+            send(rank - 3, T.hx[:, h0:h0 + 136], T.hi[:, h0:h0 + 136], 512 * 136, [("hi", t), ("ht", t)], [("hx", t)])
             pri[0] = 2 * NC - 0.5
             dve(1, lambda: V.tensor_copy(T.tx[:], T.hx[:, h0 + 128:h0 + 136]), [("hx", t)], ["tx"])
             dve(128, lambda: V.tensor_copy(T.pfi[:, 0:EXO].indirect(T.tx[:, 0:8]), T.hx[:, h0:h0 + 128]), ["tx", ("hx", t)],
@@ -362,20 +344,20 @@ def build(g, core, T, topo):
         pri[0] = -0.5 if t == 0 else NC * t - 0.5
         pe(1024, [lambda t=t, o0=o0: P.matmul(T.po[:, o0:o0 + 256], T.bo[:], T.rt[:, 256 * t:256 * t + 256], True, True)],
            ["bo", ("rt", t)], [("po", t % 2)], ["po"])
-        for c in range(NC):
-            pri[0] = -0.5 if t == 0 else NC * t + c
+        for k, c in enumerate(CO):
+            pri[0] = -0.5 if t == 0 else NC * t + k
             update(t, c)
-        if PREF and t == 2:
-            for c in range(NC):
-                pri[0] = NC * t + c + 0.7
+        if t == 2:
+            for k, c in enumerate(CO):
+                pri[0] = NC * t + k + 0.7
                 back(c)
-        for c in range(NC):
-            pri[0] = NC * t + c
+        for k, c in enumerate(CO):
+            pri[0] = NC * t + k
             compute(t, c)
         pri[0] = NC * t + NC - 1 + HPRI
         halve(t)
-    for c in range(NC):
-        pri[0] = 2 * NC + c + 0.5
+    for k, c in enumerate(CO):
+        pri[0] = 2 * NC + k + 0.5
         finish(c)
     return ops
 
@@ -431,7 +413,7 @@ def costs(ops, m):
 def replay(ops, order, cost, m, why=None):
     hop, first = m[8], m[9]
     free = {"v": 0.0, "a": 0.0, "p": 0.0, "q": 0.0, "s": 0.0}
-    prev, port = {}, [0.0, 0.0]
+    prev, port = {}, [0.0, 0.0, 0.0]
     end = [0.0] * len(ops)
     wire, seen, last, lastk = 0.0, set(), 0.0, 0
     for k in order:
@@ -551,8 +533,27 @@ def schedule(ops):
 ORDER = {}
 
 
+def hand_on(g, core, T, topo):
+    for owner in topo.cores_of(core):
+        if T.rank_of(owner) is None:
+            continue
+        dst, hs = relays(owner, T, topo)
+        if core not in hs:
+            continue
+        rid, pid, _ = topo.addr(dst)
+        came = len([e for e in topo.engines(owner, core) if e not in topo.engines(owner, dst)])
+        sent = 0
+        for k, piece in enumerate(landing(T)):
+            if hs[k % len(hs)] == core:
+                g.wait_ge(T.sem["r%d" % k], came)
+                g.remote_dma(piece, piece, T.sem["r%d" % k], T.sem.loc, pid, rid, topo.mask(core, dst))
+                sent += len(topo.engines(core, dst))
+        g.wait_ge(T.sem.loc, sent)
+
+
 def rank_program(g, core, T, topo):
     if T.rank_of(core) is None:
+        hand_on(g, core, T, topo)
         return
     ops = build(g, core, T, topo)
     depend(ops)
@@ -586,8 +587,8 @@ def rank_program(g, core, T, topo):
             ins.then_inc(T.sem["d%d" % nd], 16)
             nd += 1
         else:
-            done[k] = o["sem"]
-            loc += o["sem"][1]
+            done[k] = o["sem"][:2]
+            loc += o["sem"][2]
         total[done[k][0]] = done[k][1]
     total["loc"] = loc
     for s, val in total.items():

@@ -2,15 +2,36 @@ from concourse.mybir import AluOpType as A, ActivationFunctionType as F
 
 NS = [16, 16, 16]
 CO = [1, 0, 2]
-SPLIT = [(4, 4, 11), (4, 4, 10), (3, 4, 10)]
-PA, PV = 4, 4
-HPRI, MPRI = 0.5, 1.5
-SEED, ITERS, TEMP = 1, 52000, 0.03
-MODELS = [(1.04, 1.5, 3.8, 0.53, 2700, 60.0, 700, 250.0, 100, 2000), (0.85, 1.15, 2.0, 0.43, 2000, 100.0, 400, 350.0, 70, 1200),
-          (1.2, 1.95, 5.5, 0.62, 3500, 40.0, 1000, 180.0, 150, 3000)]
+PLANS = {
+    "5a": ([(6, 10, 1), (0, 16, 5)], [((1, 5, 1), "L", 0), ((11, 15, 1), "R", 0)], [(1, 0, 1, 1, 3)]),
+    "5b": ([(5, 10, 1), (10, 16, 5)], [((0, 5, 1), "L", 0), ((10, 15, 1), "R", 0)], [(1, 0, 1, 1, 1)]),
+    "4a": ([(4, 8, 1), (7, 11, 1)], [((0, 4, 1), "L", 0), ((11, 15, 1), "R", 1)], [(0, 0, 1, 1, 3)]),
+    "4b": ([(4, 8, 1), (12, 15, 1)], [((0, 4, 1), "L", 0), ((8, 12, 1), "R", 0), ((8, 11, 1), "L", 1)], []),
+    "5c": ([(5, 10, 1), (15, 16, 1)], [((0, 5, 1), "L", 0), ((10, 15, 1), "R", 0), ((10, 11, 1), "L", 1)], []),
+    "3a": ([(3, 7, 1), (7, 11, 1)], [((0, 4, 1), "L", 0), ((10, 14, 1), "R", 1)], [(0, 1, 1, 0, 3)]),
+    "3b": ([(3, 7, 1), (7, 11, 1), (10, 14, 1)], [((0, 4, 1), "L", 0)], [(0, 1, 1, 0, 3), (1, 0, 2, 0, 4)]),
+    "3c": ([(3, 6, 1), (9, 12, 1), (12, 14, 1)], [((0, 3, 1), "L", 0), ((6, 9, 1), "R", 0), ((6, 9, 1), "L", 1), ((9, 11, 1), "L", 2)], []),
+}
+PLAN = [["5b", "5b", "5b"], ["4a", "4b", "4a"], ["3a", "3a", "3a"]]
+PA, PV = 900, 900
+CONFV = [False, False, False]
+ANSA, TABA = True, True
+SEED, STARTS, ROUNDS, NOISE, ITERS, TEMP, SOFT = 1, 30, 4, 0.05, 40000, 0.01, 0.1
+MODELS = [(0.95, 1.4, 3.2, 0.48, 2400, 70.0, 600, 280.0, 90, 1700), (0.85, 1.15, 2.0, 0.43, 2000, 100.0, 400, 350.0, 70, 1200),
+          (1.15, 1.85, 5.0, 0.6, 3300, 45.0, 900, 200.0, 140, 2800)]
 NC = len(NS)
 C0 = [sum(NS[:c]) for c in range(NC)]
+WM = 16 * max(NS)
 SPARE, EXO, TABW, PAD = 2048, 2176, 4224, 512
+LIFT, DROP = 3072.0, 8192.0
+
+
+def plan(t, c):
+    return PLANS[PLAN[t][CO.index(c)]]
+
+
+def size(x):
+    return len(range(*x))
 
 
 def _sb(n, dtype):
@@ -19,41 +40,46 @@ def _sb(n, dtype):
 
 SCRATCH = {
     "pic_s": _sb(9216, "bfloat16"), "shp_s": _sb(768, "int32"), "ex_s": _sb(2048, "int32"), "inc_s": _sb(2048, "bfloat16"),
-    "tab": _sb(TABW, "float32"), "yit": _sb(EXO, "bfloat16"), "pfi": _sb(EXO + 16, "bfloat16"), "pfx": _sb(2816, "float32"),
+    "tab": _sb(TABW, "float32"), "pft": _sb(TABW, "float32"), "pfi": _sb(2048, "bfloat16"),
     "ofs_s": _sb(4, "int32"), "thr_s": _sb(4, "int32"), "thf": _sb(4, "float32"), "thc": _sb(4, "float32"), "oc": _sb(4, "float32"),
-    "ci": _sb(4, "int32"), "cl": _sb(8, "float32"), "cf": _sb(160, "bfloat16"), "iI": _sb(256, "bfloat16"), "iG": _sb(128, "bfloat16"),
-    "iC": _sb(256, "bfloat16"), "i256": _sb(EXO + 16, "float32"),
+    "ci": _sb(4, "int32"), "cl": _sb(8, "float32"), "cf": _sb(160, "bfloat16"), "iI": _sb(WM, "bfloat16"), "iG": _sb(128, "bfloat16"),
+    "iC": _sb(WM, "bfloat16"), "idn": _sb(EXO + 16, "float32"), "wh": _sb(2048, "bfloat16"), "drop": _sb(128, "bfloat16"),
     "r16e": _sb(160, "float16"), "r16o": _sb(160, "float16"), "r32e": _sb(160, "float32"), "r32o": _sb(160, "float32"),
-    "bo": _sb(128, "float32"), "rep": _sb(128, "float32"), "rt": _sb(768, "float32"), "ub": _sb(144, "bfloat16"), "uh": _sb(144, "bfloat16"),
-    "w2": _sb(14 * 128, "bfloat16"), "ex16": _sb(256, "bfloat16"), "ones": _sb(256, "bfloat16"),
-    "fid": _sb(8, "float32"), "dum": _sb(8, "float32"), "fall": _sb(48, "float32"), "s16": _sb(768, "float16"),
+    "bo": _sb(128, "float16"), "i32": _sb(128, "float32"), "rep": _sb(128, "float32"), "rt": _sb(3 * WM, "float16"),
+    "ub": _sb(144, "bfloat16"), "uh": _sb(144, "bfloat16"),
+    "w2": _sb(14 * 128, "bfloat16"), "exa": _sb(WM, "bfloat16"), "exb": _sb(WM, "bfloat16"), "ones": _sb(WM, "bfloat16"),
+    "tri": _sb(128, "bfloat16"), "kl": _sb(8, "uint16"), "s16": _sb(768, "float16"),
     "rq_o": _sb(144, "uint16"), "rq_i": _sb(144, "uint16"), "an_o": _sb(1536, "float16"), "an_i": _sb(1536, "float16"),
-    "xi": _sb(768, "int32"), "yo": _sb(768, "float32"),
-    "hf": _sb(8, "float32"), "hg": _sb(8, "float32"), "nb": _sb(8, "float32"), "mn": _sb(8, "float32"),
-    "hl": _sb(8, "uint16"), "tl": _sb(8, "uint16"), "tx": _sb(8, "uint16"),
-    "rr": _sb(128, "float32"), "dd": _sb(576, "float32"), "hv": _sb(128, "float32"), "hi": _sb(432, "int32"), "hx": _sb(288, "int32"),
-    "la": _sb(48, "float32"), "l1": _sb(48, "uint16"), "l2": _sb(48, "uint16"), "pm16": _sb(16, "uint16"),
-    "px": ("psum", [128, 16, 2, 16], "float32"),
+    "xi": _sb(768, "int32"), "zz": _sb(768, "float32"), "yo": _sb(768, "float32"),
+    "hf": _sb(8, "float32"), "hg": _sb(8, "float32"), "hl": _sb(8, "uint16"), "tl": _sb(16, "uint16"), "tx": _sb(32, "uint16"),
+    "rr": _sb(128, "float32"), "eq": _sb(128, "bfloat16"), "sc": _sb(128, "bfloat16"), "hi": _sb(432, "int32"), "hx": _sb(288, "int32"),
 }
-for _k in ("po", "ps", "pe", "pv0", "pv1", "pd0", "pd1"):
-    SCRATCH[_k] = ("psum", [128, 512], "float32")
+for _k in ("ps", "pv0", "pv1", "pd0", "pd1")[:8 - NC]:
+    SCRATCH[_k] = ("psum", [128, 8, 4, 16] if _k[1] == "d" else [128, 512], "float32")
+NPD = 5 - NC
 for _c in range(NC):
     _n = NS[_c]
-    SCRATCH["aT%d" % _c] = ("sbuf", [128, _n // 2, 2, 16], "float16")
-    SCRATCH["sm%d" % _c] = ("sbuf", [128, _n // 2, 2, 16], "float32")
-    SCRATCH["st%d" % _c] = ("sbuf", [128, _n // 2, 2, 16], "float32")
-    SCRATCH["li%d" % _c] = _sb(16 * _n, "uint16")
-    SCRATCH["mm%d" % _c] = _sb(10 * 16 * _n, "bfloat16")
+    SCRATCH["px%d" % _c] = ("psum", [128, 32, 16], "float32")
+    SCRATCH["aT%d" % _c] = ("sbuf", [128, _n, 16], "float16")
+    SCRATCH["x0%d" % _c] = ("sbuf", [128, _n, 16], "int32")
+    SCRATCH["tp%d" % _c] = ("sbuf", [128, _n, 16], "float32")
+    SCRATCH["li%d" % _c] = _sb(20 * _n, "uint16")
     SCRATCH["cc%d" % _c] = _sb(11 * 16 * _n, "bfloat16")
     SCRATCH["bb%d" % _c] = _sb(3 * 11 * _n, "bfloat16")
     SCRATCH["su%d" % _c] = _sb(_n, "bfloat16")
-    SCRATCH["sT%d" % _c] = _sb(128, "bfloat16")
+    SCRATCH["sT%d" % _c] = _sb(256, "bfloat16")
+    for _t in range(2):
+        SCRATCH["sm%d_%d" % (_t, _c)] = _sb(16 * _n, "float32")
+    for _t in range(3):
+        for _s, _r in enumerate(plan(_t, _c)[0]):
+            SCRATCH["mm%d_%d_%d" % (_t, _c, _s)] = _sb(_n * 16 * size(_r), "bfloat16")
 SEMAPHORES = ["v", "a", "p", "q", "loc"] + ["d%d" % k for k in range(24)] + ["r%d" % k for k in range(6 * NC + 8)]
 
 
-def pieces(lo, hi, k):
-    m = -(-(hi - lo) // k)
-    return [(lo + (hi - lo) * j // m, lo + (hi - lo) * (j + 1) // m) for j in range(m)] if hi > lo else []
+def pieces(n, k, most):
+    m = -(-(16 * n * k) // most)
+    cut = [2 * ((n // 2) * j // m) for j in range(m + 1)]
+    return [(a, b) for a, b in zip(cut, cut[1:]) if b > a]
 
 
 def relays(core, T, topo):
@@ -62,7 +88,7 @@ def relays(core, T, topo):
 
 
 def landing(T):
-    return [T.pfi[:, 1024 * k:1024 * k + 1024] for k in range(2)] + [T.pfx[:, 768 + 512 * k:1280 + 512 * k] for k in range(4)]
+    return [T.pfi[:, 1024 * k:1024 * k + 1024] for k in range(2)] + [T.pft[:, EXO + 512 * k:EXO + 512 * k + 512] for k in range(4)]
 
 
 def build(g, core, T, topo):
@@ -70,12 +96,12 @@ def build(g, core, T, topo):
     N = len(T.cores)
     V, S_, P = g.vector, g.scalar, g.tensor
     ops = []
-    cnt = {"pd": 0, "pv": 0, "r": 0}
+    cnt = {"pd": 0, "pv": 0, "h": 0, "r": 6}
     pri = [-1.0]
 
-    def add(eng, n, fns, r, w, banks=(), k=1.0, kind="c", sem=None):
+    def add(eng, n, fns, r, w, banks=(), k=1.0, kind="c", sem=None, after=()):
         ops.append({"pri": pri[0], "eng": eng, "n": n, "k": k, "fns": fns, "r": list(r), "w": list(w), "banks": list(banks),
-                    "kind": kind, "sem": sem})
+                    "kind": kind, "sem": sem, "after": list(after)})
 
     def dve(n, fn, r, w, banks=(), k=1.0):
         add("v", n, [fn], r, w, banks, k)
@@ -86,14 +112,14 @@ def build(g, core, T, topo):
     def pe(cyc, fns, r, w, banks):
         add("p", cyc, fns, r, w, banks)
 
-    def dma(q, out, in_, nbytes, r, w):
+    def dma(q, out, in_, nbytes, r, w, after=()):
         Q = {"s": g.sync, "a": S_, "q": g}[q]
-        add(q, nbytes, [lambda: Q.dma_start(out, in_)], r, w, kind="d")
+        add(q, nbytes, [lambda: Q.dma_start(out, in_)], r, w, kind="d", after=after)
 
     def send(dst_rank, out, in_, nbytes, r, w, relay=False):
         dst = T.cores[dst_rank % N]
-        k = cnt["r"]
-        cnt["r"] += 1
+        k = cnt["h" if relay else "r"]
+        cnt["h" if relay else "r"] += 1
         eng = topo.engines(core, dst)
         arrive = len(eng)
         if relay:
@@ -104,7 +130,7 @@ def build(g, core, T, topo):
             dst = h
         rid, pid, _ = topo.addr(dst)
         add("q", nbytes, [lambda: g.remote_dma(out, in_, T.sem["r%d" % k], T.sem.loc, pid, rid, sum(1 << e for e in eng))],
-            r, w, k=(2,) if relay else (0, 1), kind="r", sem=("r%d" % k, arrive, len(eng)))
+            r, w + [("h", k)], k=(2,) if relay else (0, 1), kind="r", sem=("r%d" % k, arrive, len(eng)), after=[("h", k - 1)] if relay and k else [])
 
     def iota(out, pat, base, cm, n, key):
         add("q", n, [lambda: g.iota(out, pat, base, cm, allow_small_or_imprecise_dtypes=True)], [], [key])
@@ -113,194 +139,262 @@ def build(g, core, T, topo):
     col = [T.cl[:, k:k + 1] for k in range(6)]
     main = T.pic_s[:, PAD:PAD + 4096]
 
-    dma("s", T.shp_s[:], T.shp[:], 512 * 768, [], [("shp", c) for c in range(NC)])
+    for k, c in enumerate(CO):
+        f0, W = 16 * C0[c], 16 * NS[c]
+        dma("s", T.shp_s[:, f0:f0 + W], T.shp[:, f0:f0 + W], 512 * W, [], [("shp", c)], [("shp", x) for x in CO[:k]])
     dma("a", T.ofs_s[:, 0:3], T.ofs[:], 1536, [], ["ofs"])
-    dma("s", main, T.pic[:], 1 << 20, [], ["pic"])
-    dma("a", T.thr_s[0:8, 0:3], T.thr[:], 96, [], ["thr"])
-    dma("s", T.inc_s[:], T.inc[:], 1 << 19, [], ["inc_s"])
-    dma("s", T.ex_s[:, 0:1024], T.ex[:, 0:1024], 1 << 19, [], [("ex", 0)])
-    dma("s", T.ex_s[:, 1024:2048], T.ex[:, 1024:2048], 1 << 19, [], [("ex", 1)])
+    dma("s", main, T.pic[:], 1 << 20, [], ["pic"], [("shp", x) for x in CO])
+    dma("a", T.thr_s[0:8, 0:3], T.thr[:], 96, [], ["thr"], ["ofs"])
+    dma("s", T.ex_s[:, 0:1024], T.ex[:, 0:1024], 1 << 19, [], [("ex", 0)], ["pic"])
+    dma("s", T.ex_s[:, 1024:2048], T.ex[:, 1024:2048], 1 << 19, [], [("ex", 1)], [("ex", 0)])
 
     add("q", 4, [lambda: g.iota(T.ci[:], [[0, 4]], 0, 1)], [], ["ci"])
     iota(T.cf[:], [[1, 160]], -16, 0, 160, "cf")
-    iota(T.iI[:], [[0, 16], [1, 16]], 0, 0, 256, "iI")
+    iota(T.iI[:], [[0, WM // 16], [1, 16]], 0, 0, WM, "iI")
     iota(T.iG[:], [[16, 8], [0, 16]], 0, 0, 128, "iG")
-    iota(T.iC[:], [[1, 16], [0, 16]], 0, 0, 256, "iC")
-    dma("q", T.tab[:, 0:2048], T.inc[:], 1 << 20, ["pic"], ["tabI"])
-    iota(T.i256[:], [[256, EXO + 16]], 0, 0, EXO + 16, "i256")
-    dma("s", T.pic_s[:, PAD + 4096:PAD + 8192], T.pic[:], 1 << 20, [("ex", 1)], ["picx1"])
-    dma("s", T.pic_s[:, 0:PAD], T.pic[:, 4096 - PAD:4096], 1 << 17, [("ex", 1)], ["picx0"])
-    dma("s", T.pic_s[:, PAD + 8192:9216], T.pic[:, 0:PAD], 1 << 17, [("ex", 1)], ["picx2"])
+    iota(T.iC[:], [[1, WM // 16], [0, 16]], 0, 0, WM, "iC")
+    dma("q", T.tab[:, 0:2048], T.inc[:], 1 << 20, [("shp", CO[-1])], ["tabI"], ["ci", "cf", "iI", "iG", "iC"])
+    for k in range(2):
+        iota(T.idn[:, 1096 * k:1096 * k + 1096], [[1, 1096]], 1096 * k, 0, 1096, ("idn", k))
+    dma("s", T.inc_s[:], T.inc[:], 1 << 19, [("ex", 1)], ["inc_s"])
+    dma("s", T.pic_s[:, PAD + 4096:PAD + 6144], T.pic[:, 0:2048], 1 << 19, ["tabI"], ["picx1"], ["inc_s"])
+    dma("s", T.pic_s[:, PAD + 6144:PAD + 8192], T.pic[:, 2048:4096], 1 << 19, ["inc_s"], ["picx3"], ["picx1"])
+    dma("s", T.pic_s[:, 0:PAD], T.pic[:, 4096 - PAD:4096], 1 << 17, [], ["picx0"], ["picx3"])
+    dma("s", T.pic_s[:, PAD + 8192:9216], T.pic[:, 0:PAD], 1 << 17, [], ["picx2"], ["picx0"])
     dve(1, lambda: V.tensor_scalar(T.ci[:, 1:2], T.ci[:, 0:1], 15, None, A.bitwise_and), ["ci"], ["ci1"])
     dve(1, lambda: V.tensor_scalar(T.ci[:, 2:3], T.ci[:, 0:1], 112, None, A.bitwise_and), ["ci"], ["ci2"])
     dve(1, lambda: V.tensor_scalar(T.ci[:, 3:4], T.ci[:, 0:1], 4, 1, A.arith_shift_right, A.bitwise_and), ["ci"], ["ci3"])
     dve(1, lambda: V.tensor_copy(T.cl[:, 0:4], T.ci[:]), ["ci", "ci1", "ci2", "ci3"], ["cl"])
-    dve(1, lambda: V.tensor_scalar(col[4], col[3], -1.0, 1.0, A.mult, A.add), ["cl"], ["cl4"])
-    dve(1, lambda: V.tensor_scalar(col[5], col[1], 16.0, None, A.mult), ["cl"], ["cl5"])
-    for buf, cc_, key in ((T.r16e, 4, "r16e"), (T.r16o, 3, "r16o"), (T.r32e, 4, "r32e"), (T.r32o, 3, "r32o")):
-        dve(160, lambda buf=buf, cc_=cc_: V.tensor_scalar(buf[:], T.cf[:], col[0], col[cc_], A.is_equal, A.mult),
-            ["cf", "cl", "cl4"], [key], k=0.5 if "16" in key else 1)
-    dve(128, lambda: V.tensor_scalar(T.bo[:], T.iG[:], col[2], None, A.is_equal), ["iG", "cl"], ["bo"])
-    dve(1, lambda: V.tensor_scalar(T.oc[:, 0:1], T.ofs_s[:, 0:1], 2048.0, None, A.add), ["ofs"], [("oc", 0)])
-    dve(1, lambda: V.tensor_scalar(T.oc[:, 1:3], T.ofs_s[:, 1:3], 2048.0 + PAD, None, A.add), ["ofs"], [("oc", 1), ("oc", 2)])
-    for t in range(3):
-        dve(256, lambda t=t: V.tensor_scalar(T.rt[:, 256 * t:256 * t + 256], T.iI[:], col[1], T.oc[:, t:t + 1], A.is_equal, A.mult),
-            ["iI", "cl", ("oc", t)], [("rt", t)])
-    dve(1, lambda: V.tensor_scalar(T.pm16[:], T.cf[:, 16:32], col[5], None, A.add), ["cf", "cl5"], ["pm16"])
+    act(1, lambda: S_.activation(col[4], col[3], F.Identity, bias=1.0, scale=-1.0), ["cl"], ["cl4"])
+    act(1, lambda: S_.activation(col[5], col[1], F.Identity, bias=float(SPARE)), ["cl"], ["cl5"])
+    for buf, cc_, key in ((T.r16e, 4, "r16e"), (T.r16o, 3, "r16o")):
+        dve(160, lambda buf=buf, cc_=cc_: V.tensor_scalar(buf[:], T.cf[:], col[0], col[cc_], A.is_equal, A.mult), ["cf", "cl", "cl4"], [key], k=0.5)
+    dve(128, lambda: V.tensor_scalar(T.bo[:], T.iG[:], col[2], None, A.is_equal), ["iG", "cl"], ["bo"], k=0.5)
+    dve(1, lambda: V.tensor_scalar(T.oc[:, 0:3], T.ofs_s[:, 0:3], -2048.0, None, A.add), ["ofs"], ["oc"])
+    dve(WM, lambda: V.tensor_scalar(T.rt[:, 0:WM], T.iI[:], col[1], T.oc[:, 0:1], A.is_equal, A.mult), ["iI", "cl", "oc"], [("rt", 0)], k=0.5)
+    dve(128, lambda: V.tensor_scalar(W2[1], T.cf[:, 16:144], col[0], None, A.is_equal), ["cf", "cl"], [("w2", 1)], k=0.5)
+    act(WM, lambda: S_.activation(T.ones[:], T.iI[:], F.Identity, bias=1.0, scale=0.0), ["iI"], ["ones"])
+    for m in (13, 11, 4, 0, 2, 3, 5, 6, 7, 8, 9, 10, 12):
+        sc = -1.0 if m == 11 else -EXO / 2.0 if m == 12 else LIFT if m == 13 else 2.0 ** (m - 1)
+        act(128, lambda m=m, sc=sc: S_.activation(W2[m], W2[1], F.Identity, scale=sc), [("w2", 1)], [("w2", m)])
+    pri[0] = -0.4
     dve(143, lambda: V.tensor_scalar(T.ub[:, 0:143], T.cf[:, 1:144], col[2], None, A.is_equal), ["cf", "cl"], ["ub"], k=0.5)
     act(143, lambda: S_.activation(T.uh[:, 0:143], T.ub[:, 0:143], F.Identity, scale=0.5), ["ub"], ["uh"])
-    dve(128, lambda: V.tensor_scalar(W2[1], T.cf[:, 16:144], col[0], None, A.is_equal), ["cf", "cl"], [("w2", 1)], k=0.5)
-    for m in (11, 4, 0, 2, 3, 5, 6, 7, 8, 9, 10, 12, 13):
-        sc = -1.0 if m == 11 else -EXO / 2.0 if m == 12 else -2048.0 if m == 13 else 2.0 ** (m - 1)
-        act(128, lambda m=m, sc=sc: S_.activation(W2[m], W2[1], F.Identity, scale=sc), [("w2", 1)], [("w2", m)])
-    dve(256, lambda: V.tensor_scalar(T.ex16[:], T.iC[:], col[0], None, A.is_equal), ["iC", "cl"], ["ex16"], k=0.5)
-    dve(256, lambda: V.memset(T.ones[:], 1.0), [], ["ones"], k=0.5)
-    dve(128, lambda: V.memset(T.tab[:, SPARE:EXO], 0.0), [], ["tabD"])
-    dve(1, lambda: V.tensor_scalar(T.fid[:], T.iG[:, 0:128:16], col[1], 4096.0, A.add, A.mult), ["iG", "cl"], ["fid"])
-    dve(1, lambda: V.tensor_scalar(T.dum[:], T.iG[:, 0:128:16], col[1], float(SPARE), A.add, A.add), ["iG", "cl"], ["dum"])
+    act(128, lambda: S_.activation(T.i32[:], W2[1], F.Identity), [("w2", 1)], ["i32"])
+    for t in (1, 2):
+        dve(WM, lambda t=t: V.tensor_scalar(T.rt[:, WM * t:WM * t + WM], T.iI[:], col[1], T.oc[:, t:t + 1], A.is_equal, A.mult),
+            ["iI", "cl", "oc"], [("rt", t)], k=0.5)
+    dve(WM, lambda: V.tensor_scalar(T.exa[:], T.iC[:], col[0], -DROP, A.is_equal, A.mult), ["iC", "cl"], ["exa"], k=0.5)
+    act(WM, lambda: S_.activation(T.exb[:], T.exa[:], F.Identity, scale=-LIFT / DROP), ["exa"], ["exb"])
+    act(128, lambda: S_.activation(T.tab[:, SPARE:EXO], T.iG[:], F.Identity, scale=0.0), ["iG"], ["tabD"])
+    act(128, lambda: S_.activation(T.pft[:, SPARE:EXO], T.iG[:], F.Identity, scale=0.0), ["iG"], ["pfD"])
+    act(128, lambda: S_.activation(T.drop[:], T.iG[:], F.Identity, bias=DROP, scale=0.0), ["iG"], ["drop"])
+    for k, (e16, e32) in enumerate(((T.r16e, T.r32e), (T.r16o, T.r32o))):
+        act(160, lambda e16=e16, e32=e32: S_.activation(e32[:], e16[:], F.Identity), ["r16e", "r16o"], [("r32", k)])
+    dve(128, lambda: V.tensor_scalar(T.tri[:], T.iI[:, 0:128], col[1], None, A.is_gt), ["iI", "cl"], ["tri"], k=0.5)
+    act(8, lambda: S_.activation(T.tri[:, 15:128:16], T.tri[:, 15:128:16], F.Identity, scale=4096.0), ["tri"], ["tri"])
+    dve(8, lambda: V.tensor_copy(T.kl[:], T.cf[:, 16:24]), ["cf"], ["kl"])
+    act(1, lambda: S_.activation(T.oc[:, 3:4], T.oc[:, 2:3], F.Identity, bias=6144.0 - 2 * LIFT - DROP, scale=-1.0), ["oc"], ["oc3"])
     dve(128, lambda: V.tensor_scalar(T.rep[0:8, :], T.iG[0:8, :], 0.0625, T.cl[0:8, 0:1], A.mult, A.is_equal), ["iG", "cl"], ["rep"])
-    dve(1, lambda: V.tensor_scalar(T.thf[0:8, 0:3], T.thr_s[0:8, 0:3], -2.0, 11.5, A.mult, A.add), ["thr"], ["thf"])
+    for t in range(3):
+        a_, b_ = (-1.0, 0.5) if CONFV[t] else (-2.0, 11.5)
+        if t == 0 or CONFV[t] != CONFV[t - 1]:
+            dve(1, lambda t=t, a_=a_, b_=b_: V.tensor_scalar(T.thf[0:8, t:3], T.thr_s[0:8, t:3], a_, b_, A.mult, A.add), ["thr"], ["thf"])
     pe(256, [lambda: P.matmul(T.ps[:, 0:3], T.rep[0:8, :], T.thf[0:8, 0:3], True, True)], ["rep", "thf"], ["ps"], ["ps"])
     act(1, lambda: S_.activation(T.thc[:, 0:3], T.ps[:, 0:3], F.Identity), ["ps"], ["thc"], ["ps"])
     pri[0] = 0.5
-    for k in range(2):
-        dve(1024, lambda k=k: V.tensor_scalar(T.tab[:, EXO + 1024 * k:EXO + 1024 * k + 1024], T.ex_s[:, 1024 * k:1024 * k + 1024], -2048.0, None, A.add),
-            [("ex", k)], [("tabE", k)])
-    dve(144, lambda: V.memset(T.pfi[:, SPARE:EXO + 16], 0.0), [], ["pfz", "pfd"], k=0.5)
-    dve(48, lambda: V.tensor_scalar(T.fall[:], T.cf[:, 16:64], 16.0, col[1], A.mult, A.add), ["cf", "cl"], ["fall"])
+    for k in range(4):
+        o_, i_ = T.tab[:, EXO + 512 * k:EXO + 512 * k + 512], T.ex_s[:, 512 * k:512 * k + 512]
+        if TABA:
+            act(512, lambda o_=o_, i_=i_: S_.activation(o_, i_, F.Identity, bias=-2048.0), [("ex", k // 2)], [("tabE", k)])
+        else:
+            dve(512, lambda o_=o_, i_=i_: V.tensor_scalar(o_, i_, -2048.0, None, A.add), [("ex", k // 2)], [("tabE", k)])
+    tabk = ["tabI", "tabD"] + [("tabE", k) for k in range(4)]
     land = landing(T)
-    pri[0] = -0.9
+    pri[0] = 0.6
     for k in range(2):
         send(rank - 3, land[k], T.inc_s[:, 1024 * k:1024 * k + 1024], 1 << 18, ["inc_s"], [("pfi", k)], True)
-    pri[0] = 0.6
     for k in range(4):
-        send(rank - 3, land[2 + k], T.tab[:, EXO + 512 * k:EXO + 512 * k + 512], 1 << 18, [("tabE", k // 2)], [("pfe", k)], True)
-    pxk = [("px", 0), ("px", 1)]
+        send(rank - 3, land[2 + k], T.tab[:, EXO + 512 * k:EXO + 512 * k + 512], 1 << 18, [("tabE", k)], [("pfe", k)], True)
+    pri[0] = NC
+    for h in range(16):
+        add("q", 148, [lambda h=h: g.affine_select(T.wh[:, 128 * h:128 * h + 128], T.drop[:], [[-16, 8], [0, 16]], A.is_equal, 0.0, -h, 1)],
+            ["drop"], [("wh", h)])
 
-    def route(c, src, e, o, cyc, key):
-        h2 = NS[c] // 2
+    def route(c, src, e, o, cyc, key, stop):
+        n, px = NS[c], T["px%d" % c]
         E = [[e[:, 16:144], e[:, 0:128]], [o[:, 32:160], o[:, 16:144]]]
-        for x in range(2):
-            pe(2 * max(64, 16 * h2) * cyc, [lambda x=x, y=y: P.matmul(T.px[:, 0:h2, x, :], E[x][y], src[:, :, y, :], y == 0, y == 1) for y in range(2)],
-               key, [("px", x)], ["px"])
-        return T.px[:, 0:h2]
+        pe(4 * max(64, 8 * n) * cyc, [lambda x=x, y=y: P.matmul(px[:, x:n:2, :], E[x][y], src[:, y:n:2, :], False, stop and x == 1 and y == 1)
+                                      for x in range(2) for y in range(2)], key + [("px", c)], [("px", c)], ["px%d" % c])
+
+    def kept(t, c, offsets):
+        n, W, px = NS[c], 16 * NS[c], T["px%d" % c]
+        if t == 0:
+            fns, cyc, r = [lambda: P.matmul(px[:, 0:n, :], W2[13], T.ones[:, 0:W], True, False)], W, [("w2", 13), "ones"]
+        else:
+            fns = [lambda: P.matmul(px[:, 0:n, :], T.i32[:], T["sm%d_%d" % (t - 1, c)][:], True, False),
+                   lambda: P.matmul(px[:, 0:n, :], T["sT%d" % c][0:n, 128 * t - 128:128 * t], T.exb[0:n, 0:W], False, False)]
+            cyc, r = 5 * W, ["i32", ("sm", t - 1, c), ("sT", t - 1, c), "exb"]
+        if offsets:
+            fns.append(lambda: P.matmul(px[:, 0:n, :], T.bo[:], T.rt[:, WM * t:WM * t + W], False, False))
+            cyc, r = cyc + W, r + ["bo", ("rt", t)]
+        pe(cyc, fns, r, [("px", c)], ["px%d" % c])
+
+    def sets(t, c):
+        out = []
+        for x in plan(t, c)[0] + [y[0] for y in plan(t, c)[1]]:
+            if x not in out:
+                out.append(x)
+        return out
 
     def update(t, c):
         n, W, f0 = NS[c], 16 * NS[c], 16 * C0[c]
-        aT, st, li = T["aT%d" % c], T["st%d" % c], T["li%d" % c]
+        aT, px, li, x0, pk = T["aT%d" % c], T["px%d" % c], T["li%d" % c], T["x0%d" % c], "px%d" % c
         if t == 0:
             dve(W, lambda: V.tensor_scalar(T.s16[:, f0:f0 + W], T.shp_s[:, f0:f0 + W], -2048.0, None, A.add), [("shp", c)], [("s16", c)])
             src, key = T.s16[:, f0:f0 + W], ("s16", c)
         else:
             src, key = T.an_i[:, 768 * (t - 1) + f0:768 * (t - 1) + f0 + W], ("an_i", t - 1, c)
+        kept(t, c, True)
         dve(W, lambda: V.transpose(aT[:], src), [key], [("aT", c)], k=0.5)
-        pa = route(c, aT, T.r16e, T.r16o, 1, [("aT", c), "r16e", "r16o"])
+        route(c, aT, T.r16e, T.r16o, 1, [("aT", c), "r16e", "r16o"], True)
         if t == 0:
-            act(W, lambda: S_.activation(st[:], pa, F.Identity), pxk, [("st", c)], ["px"])
-        else:
-            dve(W, lambda: V.tensor_tensor(st[:], pa, T["sm%d" % c][:], A.add), pxk + [("sm", c)], [("st", c)], ["px"])
-        o0 = 256 * (t % 2)
-        xi = T.xi[:, f0:f0 + W]
-        dve(W, lambda: V.tensor_tensor(xi, st[:], T.po[:, o0:o0 + W], A.add), [("st", c), ("po", t % 2)], [("xi", c)], ["po"])
-        if t == 0:
-            dve(W, lambda: V.tensor_scalar(xi, xi, 4095, None, A.bitwise_and), [("xi", c)], [("xi", c)])
-        k = 16 - t
-        dve(16 * k, lambda: V.tensor_copy(li[:, 0:16 * k], xi.indirect(T.pm16[:, 0:k])), [("xi", c), "pm16"], [("li", c)], k="g")
+            dve(W, lambda: V.tensor_scalar(x0[:], px[:, 0:n, :], 4096.0 - LIFT, None, A.add), [("px", c)], [("x0", c)], [pk])
+            dve(W, lambda: V.tensor_scalar(x0[:], x0[:], 4095, None, A.bitwise_and), [("x0", c)], [("x0", c)])
+        o = 0
+        for j, (lo, hi, st) in enumerate(sets(t, c)):
+            w = n * size((lo, hi, st))
+            if t == 0:
+                dve(w, lambda o=o, w=w, lo=lo, hi=hi, st=st: V.tensor_copy(li[:, o:o + w], x0[:, :, lo:hi:st]), [("x0", c)], [("li", c, j)])
+            else:
+                dve(w, lambda o=o, w=w, lo=lo, hi=hi, st=st: V.tensor_scalar(li[:, o:o + w], px[:, 0:n, lo:hi:st], 4096.0 - LIFT + PAD, None, A.add),
+                    [("px", c)], [("li", c, j)], [pk])
+            o += w
 
     def compute(t, c):
         n, W, d = NS[c], 16 * NS[c], 5 - t
-        a, a2, b = SPLIT[t]
-        li, mm, cc, bb, su, sT = [T["%s%d" % (s, c)] for s in ("li", "mm", "cc", "bb", "su", "sT")]
-        win, wk = (main, ["pic"]) if t == 0 else (T.pic_s[:, 0:9216], ["pic", "picx0", "picx1", "picx2"])
-        M = lambda i0, i1: mm[:, (i0 - a) * W:(i1 - a) * W]
-        mk = lambda i0, i1: [("mm", c, i - a) for i in range(i0, i1)]
-        ck = lambda m0, m1: [("cc", c, m) for m in range(m0, m1)]
-        e1 = min(a2 + d, b + 1)
-        for j0, j1 in ((d, e1), (e1, b + 1), (a, d)):
-            for i0, i1 in pieces(j0, j1, PA):
-                act((i1 - i0) * W, lambda i0=i0, i1=i1: S_.activation(M(i0, i1), win.indirect(li[:, i0 * n:i1 * n]), F.Identity),
-                    [("li", c)] + wk, mk(i0, i1), k="g")
-        m2 = b - d + 1
+        li, cc, bb, su, sT, px = [T["%s%d" % (s, c)] for s in ("li", "cc", "bb", "su", "sT", "px")]
+        win, wk = (main, ["pic"]) if t == 0 else (T.pic_s[:, 0:9216], ["pic", "picx0", "picx1", "picx2", "picx3"])
+        sr, vr, dr = plan(t, c)
+        rs = sets(t, c)
+        lo_ = [n * sum(size(x) for x in rs[:j]) for j in range(len(rs))]
+        mm = [T["mm%d_%d_%d" % (t, c, s)] for s in range(len(sr))]
+        mk = lambda s, a, b: [("mm", t, c, s, x) for x in range(a, b, 2)]
+        ck = lambda o, a, b: [("cc", c, o, x) for x in range(a, b, 2)]
+        lst = lambda j, k, a, b: li[:, lo_[j] + a * k:lo_[j] + b * k]
+        M = lambda s, a, b: mm[s][:, 16 * size(sr[s]) * a:16 * size(sr[s]) * b]
+        for s, x in enumerate(sr):
+            k = size(x)
+            for a, b in pieces(n, k, PA):
+                act(16 * (b - a) * k, lambda s=s, a=a, b=b, k=k: S_.activation(M(s, a, b), win.indirect(lst(s, k, a, b)), F.Identity),
+                    [("li", c, s)] + wk, mk(s, a, b), k="g")
         pv, pvk = T["pv%d" % cnt["pv"]], "pv%d" % cnt["pv"]
         cnt["pv"] ^= 1
+        at, vk = {}, []
 
-        def votes(m0, m1, signs):
+        def votes(o0, o1, keys, signs):
             u = T.uh if signs else T.ub
-            fns = [lambda j=j: P.matmul(pv[:, m0 * n:m1 * n], u[:, 15 - j:143 - j], cc[:, m0 * W + j:m1 * W:16], j == 0, j == 15 and not signs)
+            fns = [lambda j=j: P.matmul(pv[:, o0:o1], u[:, 15 - j:143 - j], cc[:, 16 * o0 + j:16 * o1:16], j == 0, j == 15 and not signs)
                    for j in range(16)]
             if signs:
-                fns.append(lambda: P.matmul(pv[:, m0 * n:m1 * n], W2[4], T.ones[:, 0:(m1 - m0) * n], False, True))
-            pe(len(fns) * max(64, (m1 - m0) * n), fns, ck(m0, m1) + ["ub", "uh", ("w2", 4), "ones"], [(pvk, "v")], [pvk])
+                fns.append(lambda: P.matmul(pv[:, o0:o1], W2[4], T.ones[:, 0:o1 - o0], False, True))
+            vk.append((pvk, "v", len(vk)))
+            pe(len(fns) * max(64, o1 - o0), fns, keys + ["ub", "uh", ("w2", 4), "ones"], vk[-1:], [pvk])
 
-        for m0, m1 in pieces(0, a2, PV):
-            dve((m1 - m0) * W, lambda m0=m0, m1=m1: V.tensor_tensor(cc[:, m0 * W:m1 * W], win.indirect(li[:, m0 * n:m1 * n]), M(m0 + d, m1 + d), A.is_gt),
-                [("li", c)] + wk + mk(m0 + d, m1 + d), ck(m0, m1), k="g")
-        votes(0, a2, False)
-        per = 512 // W
-        for m0 in range(a2, m2, per):
-            m1 = min(m0 + per, m2)
-            pd, pk = T["pd%d" % cnt["pd"]], "pd%d" % cnt["pd"]
-            cnt["pd"] ^= 1
-            w = (m1 - m0) * W
-            pe(2 * w, [lambda pd=pd, m0=m0, m1=m1, w=w: P.matmul(pd[:, 0:w], W2[1], M(m0, m1), True, False),
-                       lambda pd=pd, m0=m0, m1=m1, w=w: P.matmul(pd[:, 0:w], W2[11], M(m0 + d, m1 + d), False, True)],
-               mk(m0, m1) + mk(m0 + d, m1 + d) + [("w2", 1), ("w2", 11)], [pk], [pk])
-            act(w, lambda pd=pd, m0=m0, m1=m1, w=w: S_.activation(cc[:, m0 * W:m1 * W], pd[:, 0:w], F.Sign, bias=-2.0 ** -110),
-                [pk], ck(m0, m1), [pk])
-        for m0, m1 in pieces(m2, 11, PV):
-            dve((m1 - m0) * W, lambda m0=m0, m1=m1: V.tensor_tensor(cc[:, m0 * W:m1 * W], win.indirect(li[:, (m0 + d) * n:(m1 + d) * n]), M(m0, m1), A.is_lt),
-                [("li", c)] + wk + mk(m0, m1), ck(m0, m1), k="g")
-        if m2 < 11:
-            votes(m2, 11, False)
-        if m2 > a2:
-            votes(a2, m2, True)
+        o = 0
+        for x, side, s in vr:
+            k, j = size(x), rs.index(x)
+            for z, i in enumerate(range(*x)):
+                at[i if side == "L" else i - d] = (o + z, o + n * k, k)
+            for a, b in pieces(n, k, PV):
+                dve(16 * (b - a) * k, lambda o=o, a=a, b=b, k=k, j=j, s=s, side=side: V.tensor_tensor(
+                    cc[:, 16 * (o + a * k):16 * (o + b * k)], win.indirect(lst(j, k, a, b)), M(s, a, b), A.is_gt if side == "L" else A.is_lt),
+                    [("li", c, j)] + wk + mk(s, a, b), ck(o // n, a, b), k="g")
+            votes(o, o + n * k, ck(o // n, 0, n), False)
+            o += n * k
+        o0, keys = o, []
+        for s0, i0, s1, i1, k in dr:
+            for z, i in enumerate(list(range(*sr[s0]))[i0:i0 + k]):
+                at[i] = (o + z, o + n * k, k)
+            ks = size(sr[s0])
+            for a, b in pieces(n, 2 if ks == 2 else 4, 512):
+                pd, pk = T["pd%d" % cnt["pd"]], "pd%d" % cnt["pd"]
+                cnt["pd"] = (cnt["pd"] + 1) % NPD
+                rows = (b - a) // 2 if ks == 2 else b - a
+                seen = pd[:, 0:rows, 0:4:2, :] if ks == 2 and k == 1 else pd[:, 0:rows, 0:(4 if ks == 2 else k), :]
+                if k == ks:
+                    parts = [(seen, M(s0, a, b), M(s1, a, b), 16 * k * (b - a))]
+                else:
+                    z0, z1, e, e1 = 16 * (ks * a + i0), 16 * (ks * a + i1), 64 * (rows - 1), 4 - ks + k
+                    parts = [(pd[:, 0:rows - 1], mm[s0][:, z0:z0 + e], mm[s1][:, z1:z1 + e], e),
+                             (pd[:, rows - 1, 0:e1, :], mm[s0][:, z0 + e:z0 + e + 16 * e1], mm[s1][:, z1 + e:z1 + e + 16 * e1], 64)]
+                pe(2 * sum(x[3] for x in parts), [lambda x=x, z=z: P.matmul(x[0], W2[(1, 11)[z]], x[1 + z], z == 0, z == 1) for x in parts for z in range(2)],
+                   mk(s0, a, b) + mk(s1, a, b) + [("w2", 1), ("w2", 11)], [pk], [pk])
+                act(16 * k * (b - a), lambda seen=seen, o=o, a=a, b=b, k=k: S_.activation(cc[:, 16 * (o + a * k):16 * (o + b * k)], seen, F.Sign, bias=-2.0 ** -110),
+                    [pk], ck(o // n, a, b), [pk])
+            keys += ck(o // n, 0, n)
+            o += n * k
+        if dr:
+            votes(o0, o, keys, True)
         q = 11 * n
-        act(q, lambda: S_.activation(bb[:, 2 * q:3 * q], pv[:, 0:q], F.Abs, bias=-7.5), [(pvk, "v")], [("bb", c, 2)], [pvk])
-        act(q, lambda: S_.activation(bb[:, 0:q], pv[:, 0:q], F.Sign, bias=-8.5), [(pvk, "v")], [("bb", c, 0)], [pvk])
-        act(q, lambda: S_.activation(bb[:, q:2 * q], bb[:, 2 * q:3 * q], F.Sign, bias=-4.0), [("bb", c, 2)], [("bb", c, 1)])
-        pe(11 * 64, [lambda m=m: P.matmul(T.ps[:, 0:n], W2[m], bb[:, m * n:(m + 1) * n], m == 0, False) for m in range(11)],
-           [("bb", c, 0)] + [("w2", m) for m in range(11)], ["ps"], ["ps"])
-        pe(11 * 64, [lambda m=m: P.matmul(pv[:, 256:256 + n], W2[1], bb[:, q + m * n:q + (m + 1) * n], m == 0, m == 10) for m in range(11)],
+        act(q, lambda: S_.activation(bb[:, 2 * q:3 * q], pv[:, 0:q], F.Abs, bias=-7.5), vk, [("bb", c, 2)], [pvk])
+        if CONFV[t]:
+            dve(q, lambda: V.tensor_scalar(bb[:, q:2 * q], bb[:, 2 * q:3 * q], 4.0, None, A.is_ge), [("bb", c, 2)], [("bb", c, 1)], k=0.5)
+        else:
+            act(q, lambda: S_.activation(bb[:, q:2 * q], bb[:, 2 * q:3 * q], F.Sign, bias=-4.0), [("bb", c, 2)], [("bb", c, 1)])
+        act(q, lambda: S_.activation(bb[:, 0:q], pv[:, 0:q], F.Sign, bias=-8.5), vk, [("bb", c, 0)], [pvk])
+        B = lambda z, m: bb[:, z + at[m][0]:z + at[m][1]:at[m][2]]
+        pe(11 * 64, [lambda m=m: P.matmul(pv[:, 256:256 + n], W2[1], B(q, m), m == 0, m == 10) for m in range(11)],
            [("bb", c, 1), ("w2", 1)], [(pvk, "c")], [pvk])
+        pe(11 * 64, [lambda m=m: P.matmul(T.ps[:, 0:n], W2[m], B(0, m), m == 0, False) for m in range(11)],
+           [("bb", c, 0)] + [("w2", m) for m in range(11)], ["ps"], ["ps"])
         act(n, lambda: S_.activation(su[:], pv[:, 256:256 + n], F.Sign, bias=T.thc[:, t:t + 1]), [(pvk, "c"), "thc"], [("su", c)], [pvk])
-        wu = 13 if t == 2 else 12
-        pe(64, [lambda: P.matmul(T.ps[:, 0:n], W2[wu], su[:], False, True)], [("su", c), ("w2", wu)], ["ps"], ["ps"])
-        r0, c0 = 48 * t + C0[c], C0[c]
-        if t == 2:
-            dve(n, lambda: V.tensor_scalar(T.la[:, c0:c0 + n], T.ps[:, 0:n], 1023.5 + 768 - 2048, None, A.add), ["ps"], [("la", c)], ["ps"])
-            dve(n, lambda: V.tensor_scalar(T.l1[:, c0:c0 + n], T.ps[:, 0:n], 1023.5 + 2048, float(EXO), A.add, A.min), ["ps"], [("l1", c)], ["ps"])
-            if c0 < 24 and c0 + n > 16:
-                dve(n, lambda: V.tensor_scalar(T.rq_o[:, r0:r0 + n], T.ps[:, 0:n], 1023.5 + 2048, None, A.add), ["ps"], [("rq_o", t, c)], ["ps"])
-            dve(n, lambda: V.tensor_tensor(T.la[:, c0:c0 + n], T.la[:, c0:c0 + n], T.fall[:, c0:c0 + n], A.max), [("la", c), "fall"], [("la", c)])
-            dve(n, lambda: V.tensor_copy(T.l2[:, c0:c0 + n], T.la[:, c0:c0 + n]), [("la", c)], [("l2", c)])
-            return
+        pe(64, [lambda: P.matmul(T.ps[:, 0:n], W2[12], su[:], False, True)], [("su", c), ("w2", 12), "ps"], ["ps"], ["ps"])
+        r0, c0, pk = 48 * t + C0[c], C0[c], "px%d" % c
         dve(n, lambda: V.tensor_scalar(T.rq_o[:, r0:r0 + n], T.ps[:, 0:n], 1023.5 + EXO / 2, None, A.add), ["ps"], [("rq_o", t, c)], ["ps"])
+        if t == 2:
+            pe(16 * 64, [lambda h=h: P.matmul(px[:, 0:n, h], T.wh[:, 128 * h:128 * h + 128], su[:], False, h == 15) for h in range(16)],
+               [("su", c), ("px", c)] + [("wh", h) for h in range(16)], [("px", c)], [pk])
+            return
         send(rank + 1 + t, T.rq_i[:, r0:r0 + n], T.rq_o[:, r0:r0 + n], 256 * n, [("rq_o", t, c)], [("rq_i", t, c)])
+        if t == 1 and c == CO[0]:
+            dma("q", T.pft[:, 0:2048], T.pfi[:], 1 << 20, [("pfi", 0), ("pfi", 1)], ["pfI"], [("rq_i", t, c)])
         a0 = 768 * t + 16 * c0
-        dve(W, lambda: V.tensor_copy(T.an_o[:, a0:a0 + W], T.tab[:, 0:TABW].indirect(T.rq_i[:, r0:r0 + n])),
-            [("rq_i", t, c), "tabI", "tabD", ("tabE", 0), ("tabE", 1)], [("an_o", t, c)], k="g")
+        if ANSA:
+            act(W, lambda: S_.activation(T.an_o[:, a0:a0 + W], T.tab[:, 0:TABW].indirect(T.rq_i[:, r0:r0 + n]), F.Identity),
+                [("rq_i", t, c)] + tabk, [("an_o", t, c)], k="g")
+        else:
+            dve(W, lambda: V.tensor_copy(T.an_o[:, a0:a0 + W], T.tab[:, 0:TABW].indirect(T.rq_i[:, r0:r0 + n])),
+                [("rq_i", t, c)] + tabk, [("an_o", t, c)], k="g")
         send(rank - 1 - t, T.an_i[:, a0:a0 + W], T.an_o[:, a0:a0 + W], 256 * W, [("an_o", t, c)], [("an_i", t, c)])
-        pri[0] += MPRI
+        pri[0] += 1.5
         pe(128, [lambda: P.matmul(pv[0:n, 384:512], su[:], W2[1], True, True)], [("su", c), ("w2", 1)], [(pvk, "t")], [pvk])
-        act(128, lambda: S_.activation(sT[0:n, :], pv[0:n, 384:512], F.Relu), [(pvk, "t")], [("sT", c)], [pvk])
-        pe(W, [lambda: P.matmul(T.pe[:, 0:W], sT[0:n, :], T.ex16[0:n, 0:W], True, True)], [("sT", c), "ex16"], ["pe"], ["pe"])
-        dve(W, lambda: V.tensor_tensor(T["sm%d" % c][:], T["st%d" % c][:], T.pe[:, 0:W], A.mult), [("st", c), "pe"], [("sm", c)], ["pe"])
+        act(128, lambda: S_.activation(sT[0:n, 128 * t:128 * t + 128], pv[0:n, 384:512], F.Relu, scale=-1.0), [(pvk, "t")], [("sT", t, c)], [pvk])
+        kept(t, c, False)
+        route(c, T["aT%d" % c], T.r16e, T.r16o, 1, [("aT", c), "r16e", "r16o"], False)
+        pe(W, [lambda: P.matmul(px[:, 0:n, :], sT[0:n, 128 * t:128 * t + 128], T.exa[0:n, 0:W], False, True)],
+           [("sT", t, c), "exa", ("px", c)], [("px", c)], [pk])
+        act(W, lambda: S_.activation(T["sm%d_%d" % (t, c)][:], px[:, 0:n, :], F.Relu), [("px", c)], [("sm", t, c)], [pk])
 
     def back(c):
-        W, f0 = 16 * NS[c], 16 * C0[c]
-        pa = route(c, T["st%d" % c], T.r32e, T.r32o, 4, [("st", c), "r32e", "r32o"])
-        dve(W, lambda: V.transpose(T.pfx[:, f0:f0 + W], pa), pxk, [("pfs", c)], ["px"])
+        n, W, px, tp, pk = NS[c], 16 * NS[c], T["px%d" % c], T["tp%d" % c], "px%d" % c
+        dve(W, lambda: V.transpose(tp[:], px[:, 0:n, :]), [("px", c)], [("tp", c)], [pk])
+        pe(W, [lambda: P.matmul(px[:, 0:n, :], W2[13], T.ones[:, 0:W], True, False)], [("w2", 13), "ones"], [("px", c)], [pk])
+        route(c, tp, T.r32e, T.r32o, 4, [("tp", c), ("r32", 0), ("r32", 1)], False)
 
     def finish(c):
-        n, W, f0, c0 = NS[c], 16 * NS[c], 16 * C0[c], C0[c]
-        xi, yo = T.xi[:, f0:f0 + W], T.yo[:, f0:f0 + W]
-        dve(W, lambda: V.tensor_scalar(yo, T.pfx[:, 0:2816].indirect(T.l2[:, c0:c0 + n]), 2048.0, None, A.add),
-            [("l2", c)] + [("pfs", k) for k in range(NC)] + [("pfe", k) for k in range(4)], [("yo", c)], k="g")
-        dve(W, lambda: V.tensor_tensor(xi, T.pfi[:, 0:EXO + 16].indirect(T.l1[:, c0:c0 + n]), yo, A.add),
-            [("l1", c), ("yo", c), "pfz", "pfd", ("pfi", 0), ("pfi", 1)], [("xi", c)], k="g")
+        n, W, f0, r0 = NS[c], 16 * NS[c], 16 * C0[c], 96 + C0[c]
+        xi, zz, yo, px = T.xi[:, f0:f0 + W], T.zz[:, f0:f0 + W], T.yo[:, f0:f0 + W], T["px%d" % c]
+        dve(W, lambda: V.tensor_scalar(zz, px[:, 0:n, :], T.oc[:, 3:4], 2048.0, A.add, A.max), [("px", c), "oc3"], [("zz", c)], ["px%d" % c])
+        dve(W, lambda: V.tensor_tensor(xi, T.pft[:, 0:TABW].indirect(T.rq_o[:, r0:r0 + n]), zz, A.add),
+            [("rq_o", 2, c), ("zz", c), "pfI", "pfD"] + [("pfe", k) for k in range(4)], [("xi", c)], k="g")
         dve(W, lambda: V.tensor_scalar(xi, xi, 4095, None, A.bitwise_and), [("xi", c)], [("xi", c)])
         dve(W, lambda: V.tensor_copy(yo, xi), [("xi", c)], [("yo", c)])
         dma("s", T.ys[:, f0:f0 + W], yo, 512 * W, [("yo", c)], [("ys", c)])
+
+    def scatter(win, tl, l0, src, h0, r, w):
+        for k in range(8):
+            dve(16, lambda k=k: V.tensor_copy(win[:, 0:EXO].indirect(tl[:, l0 + 2 * k:l0 + 2 * k + 1]), src[:, h0 + 16 * k:h0 + 16 * k + 16]), r, w, k="s")
 
     def halve(t):
         rk = [("rq_i", t, k) for k in range(NC) if C0[k] < 8 * t + 8 and C0[k] + NS[k] > 8 * t]
@@ -309,43 +403,32 @@ def build(g, core, T, topo):
         if t == 2:
             send(rank + 3, T.rq_i[:, r0:r0 + 8], T.rq_o[:, r0:r0 + 8], 2048, [("rq_o",) + x[1:] for x in rk], rk)
         dve(1, lambda: V.tensor_scalar(T.hl[:], T.rq_i[:, r0:r0 + 8], float(EXO), None, A.min), rk, ["hl"])
-        dve(1, lambda: V.tensor_scalar(T.hf[:], T.rq_i[:, r0:r0 + 8], float(EXO), None, A.min), rk, ["hf"])
-        act(1, lambda: S_.activation(T.nb[:], T.hf[:], F.Identity, scale=-256.0), ["hf"], ["nb"])
-        dve(128, lambda: V.tensor_tensor(T.rr[:], T.i256[:, 0:EXO + 16].indirect(T.hl[:, 0:8]), T.cf[:, 16:144], A.add), ["i256", "hl", "cf"], ["rr"], k="g")
-        act(128, lambda: S_.activation(T.hv[:], T.tab[:, 0:EXO + 16].indirect(T.hl[:, 0:8]), F.Identity, bias=-0.25, scale=0.5),
-            ["tabI", "tabD", ("tabE", 0), "hl"], ["hv"], k="g")
-        dve(128, lambda: V.tensor_copy(hi, T.hv[:]), ["hv"], [("hi", t)])
-        for k in range(8):
-            o, w = 8 * k * (k + 1), 16 * (k + 1)
-            act(w, lambda k=k, o=o, w=w: S_.activation(T.dd[:, o:o + w], T.rr[:, 0:w], F.Abs, bias=T.nb[:, k:k + 1]), ["rr", "nb"], [("dd", k)])
-        for k in range(8):
-            o, w = 8 * k * (k + 1), 16 * (k + 1)
-            act(w, lambda k=k, o=o, w=w: S_.activation(T.dd[:, o:o + w], T.dd[:, o:o + w], F.Relu, bias=T.fid[:, k:k + 1], scale=-4096.0,
-                                                       accum_out=T.mn[:, k:k + 1]), [("dd", k), "fid"], [("dd", k), ("mn", k)])
-        dve(1, lambda: V.tensor_tensor(T.hg[:], T.mn[:], T.hf[:], A.max), [("mn", k) for k in range(8)] + ["hf"], ["hg"])
-        dve(1, lambda: V.tensor_tensor(ht, T.hg[:], T.dum[:], A.min), ["hg", "dum"], [("ht", t)])
-        dve(1, lambda: V.tensor_copy(T.tl[:], ht), [("ht", t)], ["tl"])
+        dve(1, lambda: V.tensor_copy(T.hf[:], T.hl[:]), ["hl"], ["hf"])
+        act(128, lambda: S_.activation(T.rr[:], T.idn[:, 0:EXO + 16].indirect(T.hl[:, 0:8]), F.Identity), [("idn", 0), ("idn", 1), "hl"], ["rr"], k="g")
         if t < 2:
-            dve(128, lambda: V.tensor_copy(T.tab[:, 0:EXO].indirect(T.tl[:, 0:8]), hi), ["tl", ("hi", t)], ["tabI", "tabD"], k="s")
+            a0 = 896 * t
+            dve(128, lambda: V.tensor_scalar(hi, T.an_o[:, a0:a0 + 128], 0.5, -0.25, A.mult, A.add), [("an_o",) + x[1:] for x in rk], [("hi", t)])
         else:
-            dve(128, lambda: V.tensor_copy(T.yit[:, 0:EXO].indirect(T.tl[:, 0:8]), hi), ["tl", ("hi", t)], ["yit"], k="s")
-            dma("s", T.yi[:], T.yit[:, 0:2048], 1 << 19, ["yit"], ["yi"])
-        if t == 1:
-            dma("q", T.yit[:, 0:2048], T.tab[:, 0:2048], 1 << 19, ["tabI"], ["yit"])
-        if t < 2:
-            send(rank - 3, T.hx[:, h0:h0 + 136], T.hi[:, h0:h0 + 136], 512 * 136, [("hi", t), ("ht", t)], [("hx", t)])
-            pri[0] = 2 * NC - 0.5
-            dve(1, lambda: V.tensor_copy(T.tx[:], T.hx[:, h0 + 128:h0 + 136]), [("hx", t)], ["tx"])
-            dve(128, lambda: V.tensor_copy(T.pfi[:, 0:EXO].indirect(T.tx[:, 0:8]), T.hx[:, h0:h0 + 128]), ["tx", ("hx", t)],
-                [("pfi", 0), ("pfi", 1), "pfd"], k="s")
+            dve(128, lambda: V.tensor_scalar(hi, T.tab[:, 0:EXO + 16].indirect(T.hl[:, 0:8]), 0.5, -0.25, A.mult, A.add), tabk + ["hl"], [("hi", t)], k="g")
+        dve(128, lambda: V.tensor_tensor(T.eq[:], T.hf[:, 0:8].indirect(T.kl[:, 0:8]), T.rr[:], A.is_equal), ["hf", "kl", "rr"], ["eq"], k="g")
+        dve(128, lambda: V.tensor_tensor_scan(T.sc[:], T.eq[:], T.tri[:], 0.0, A.max, A.mult), ["eq", "tri"], ["sc"], k=0.5)
+        dve(1, lambda: V.tensor_tensor(T.hg[:], T.sc[:, 15:128:16], T.hf[:], A.max), ["sc", "hf"], ["hg"])
+        dve(1, lambda: V.tensor_scalar(T.tl[:, 0:16:2], T.hg[:], col[5], None, A.min), ["hg", "cl5"], ["tl"])
+        scatter(T.tab, T.tl, 0, T.hi, h0, ["tl", ("hi", t)], ["tabI", "tabD"])
+        if t == 2:
+            dma("q", T.yi[:], T.tab[:, 0:2048], 1 << 19, ["tabI"], ["yi"])
+            return
+        dve(1, lambda: V.tensor_scalar(ht, T.hg[:], col[5], None, A.min), ["hg", "cl5"], [("ht", t)])
+        send(rank - 3, T.hx[:, h0:h0 + 136], T.hi[:, h0:h0 + 136], 512 * 136, [("hi", t), ("ht", t)], [("hx", t)])
+
+    def mirror(t):
+        h0 = 144 * t
+        dve(1, lambda: V.tensor_copy(T.tx[:, 16 * t:16 * t + 16:2], T.hx[:, h0 + 128:h0 + 136]), [("hx", t)], [("tx", t)])
+        scatter(T.pft, T.tx, 16 * t, T.hx, h0, [("tx", t), ("hx", t)], ["pfI", "pfD"])
 
     for t in range(3):
-        o0 = 256 * (t % 2)
-        pri[0] = -0.5 if t == 0 else NC * t - 0.5
-        pe(1024, [lambda t=t, o0=o0: P.matmul(T.po[:, o0:o0 + 256], T.bo[:], T.rt[:, 256 * t:256 * t + 256], True, True)],
-           ["bo", ("rt", t)], [("po", t % 2)], ["po"])
         for k, c in enumerate(CO):
-            pri[0] = -0.5 if t == 0 else NC * t + k
+            pri[0] = -0.5 + 0.01 * k if t == 0 else NC * t + k
             update(t, c)
         if t == 2:
             for k, c in enumerate(CO):
@@ -354,8 +437,11 @@ def build(g, core, T, topo):
         for k, c in enumerate(CO):
             pri[0] = NC * t + k
             compute(t, c)
-        pri[0] = NC * t + NC - 1 + HPRI
+        pri[0] = NC * t + NC - 0.5
         halve(t)
+        if t == 1:
+            mirror(0)
+            mirror(1)
     for k, c in enumerate(CO):
         pri[0] = 2 * NC + k + 0.5
         finish(c)
@@ -369,6 +455,7 @@ def depend(ops):
         for x in o["r"]:
             if x in last_w:
                 dep.add(last_w[x])
+        o["raw"] = set(dep)
         for x in o["w"]:
             if x in last_w:
                 dep.add(last_w[x])
@@ -381,13 +468,14 @@ def depend(ops):
             if o["eng"] == "p":
                 dep.update(cur[-1:])
             bank[b] = (o["eng"], cur + [k], prev)
+        dep.discard(k)
+        o["dep"] = sorted(dep)
+        o["pre"] = sorted(dep | set(last_w[x] for x in o["after"]))
         for x in o["r"]:
             readers.setdefault(x, []).append(k)
         for x in o["w"]:
             last_w[x] = k
             readers[x] = []
-        dep.discard(k)
-        o["dep"] = sorted(dep)
 
 
 def costs(ops, m):
@@ -396,9 +484,9 @@ def costs(ops, m):
     for o in ops:
         e, n, k = o["eng"], o["n"], o["k"]
         if o["kind"] == "d":
-            out.append((1000.0 if e == "q" else 100.0, n / dbw))
+            out.append((1000.0 if e == "q" else 100.0, 60 + n / dbw))
         elif o["kind"] == "r":
-            out.append((riss, n / (rbw if len(k) == 2 else 0.6 * rbw)))
+            out.append((riss, 150 + n / rbw))
         elif e == "p":
             out.append((n * pcy, 60.0))
         elif e == "q":
@@ -410,38 +498,73 @@ def costs(ops, m):
     return out
 
 
-def replay(ops, order, cost, m, why=None):
-    hop, first = m[8], m[9]
+def step(o, e, kind, t, cost, m, wire):
+    occ, lat = cost
+    t += occ
+    if kind == "c":
+        return t, t + lat
+    if e == "q" and kind not in wire[3]:
+        wire[3] += kind
+        t += m[9]
+    if kind == "d":
+        wire[0], wire[1] = max(wire[0], t) + lat, max(wire[1], t) + lat
+        return t, max(wire[0], wire[1]) + 2000.0
+    if len(o["k"]) == 2:
+        wire[0] = max(wire[0], t) + lat
+        return t, wire[0] + m[4] - m[6]
+    wire[1] = max(wire[1], t) + 0.6 * lat
+    wire[2] = max(wire[2], wire[1] + m[4]) + lat
+    return t, wire[2] + m[4] - m[6]
+
+
+def replay(ops, order, cost, m, why=None, ends=None):
+    hop = m[8]
     free = {"v": 0.0, "a": 0.0, "p": 0.0, "q": 0.0, "s": 0.0}
-    prev, port = {}, [0.0, 0.0, 0.0]
-    end = [0.0] * len(ops)
-    wire, seen, last, lastk = 0.0, set(), 0.0, 0
+    prev, wire = {}, [0.0, 0.0, 0.0, ""]
+    end = [0.0] * len(ops) if ends is None else ends
+    last, lastk = 0.0, 0
     for k in order:
         e, kind, dep = ops[k]["key"]
         t, w = free[e], prev.get(e, -1)
         for j in dep:
             if end[j] > t:
                 t, w = end[j] + hop, -2 - j
-        occ, lat = cost[k]
-        t += occ
-        if kind != "c":
-            if e == "q" and kind not in seen:
-                seen.add(kind)
-                t += first
-            if kind == "d":
-                wire = max(wire, t) + lat
-                lat = wire - t + 2000.0
-            else:
-                out = max([t] + [port[h] for h in ops[k]["k"]]) + lat
-                for h in ops[k]["k"]:
-                    port[h] = out
-                lat = out - t + m[4] - m[6]
-        free[e], prev[e], end[k] = t, k, t + lat
+        if kind == "c":
+            t += cost[k][0]
+            free[e], t = t, t + cost[k][1]
+        else:
+            free[e], t = step(ops[k], e, kind, t, cost[k], m, wire)
+        prev[e], end[k] = k, t
         if why is not None:
             why[k] = w
-        if t + lat > last:
-            last, lastk = t + lat, k
+        if t > last:
+            last, lastk = t, k
     return last, lastk
+
+
+def listed(ops, succ, cost, m, key):
+    n = len(ops)
+    left = [len(o["pre"]) for o in ops]
+    lim = [0.0] * n
+    free = {e: 0.0 for e in "vapqs"}
+    wire = [0.0, 0.0, 0.0, ""]
+    pool = [k for k in range(n) if left[k] == 0]
+    order = []
+    while pool:
+        j = min(pool, key=lambda x: max(lim[x], free[ops[x]["eng"]]) + cost[x][0])
+        e = ops[j]["eng"]
+        first = max(lim[j], free[e]) + cost[j][0]
+        k = min((x for x in pool if ops[x]["eng"] == e and (x == j or lim[x] < first)), key=key)
+        pool.remove(k)
+        order.append(k)
+        free[e], end = step(ops[k], e, ops[k]["kind"], max(lim[k], free[e]), cost[k], m, wire)
+        for x in succ[k]:
+            if k in ops[x]["key"][2]:
+                lim[x] = max(lim[x], end + m[8])
+            left[x] -= 1
+            if left[x] == 0:
+                pool.append(x)
+    return order
 
 
 def schedule(ops):
@@ -451,43 +574,27 @@ def schedule(ops):
     cost = [costs(ops, m) for m in MODELS]
     succ = [[] for _ in range(n)]
     for k, o in enumerate(ops):
-        for j in o["dep"]:
+        for j in o["pre"]:
             succ[j].append(k)
-    left = [len(o["dep"]) for o in ops]
-    lim, start, cum = [0.0] * n, [0.0] * n, 0.0
-    busy = {e: [] for e in "vapqs"}
-    pool = [k for k in range(n) if left[k] == 0]
-    while pool:
-        k = min(pool, key=lambda j: (ops[j]["pri"], j))
-        pool.remove(k)
-        occ, lat = cost[0][k]
-        if ops[k]["kind"] == "d":
-            cum = cum + lat if ops[k]["pri"] < 0 else lat
-            lat = cum + 2000.0
-        if ops[k]["kind"] == "r":
-            lat += MODELS[0][4] - MODELS[0][6]
-        t = lim[k]
-        for lo, hi in busy[ops[k]["eng"]]:
-            if t + occ <= lo:
-                break
-            t = max(t, hi)
-        busy[ops[k]["eng"]].append((t, t + occ))
-        busy[ops[k]["eng"]].sort()
-        start[k] = t
-        for j in succ[k]:
-            lim[j] = max(lim[j], t + occ + lat + MODELS[0][8])
-            left[j] -= 1
-            if left[j] == 0:
-                pool.append(j)
-    order = sorted(range(n), key=lambda k: (start[k], k))
-    base = [replay(ops, order, c, m)[0] for c, m in zip(cost, MODELS)]
-    score = lambda od: sum(replay(ops, od, c, m)[0] / b_ for c, m, b_ in zip(cost, MODELS, base))
+    tail = [0.0] * n
+    for k in range(n - 1, -1, -1):
+        tail[k] = sum(cost[0][k]) + (0.0 if ops[k]["kind"] == "c" else 2000.0) + max([0.0] + [tail[x] + MODELS[0][8] for x in succ[k]])
     seed = [SEED]
 
     def rnd():
         seed[0] = (seed[0] * 1103515245 + 12345) % 2147483648
         return seed[0] / 2147483648.0
 
+    base = [replay(ops, range(n), c, m)[0] for c, m in zip(cost, MODELS)]
+    score = lambda od: sum(replay(ops, od, c, m)[0] / b_ for c, m, b_ in zip(cost, MODELS, base))
+    starts = []
+    for it in range(STARTS):
+        w = 2000.0 * (it % 4)
+        urge = [w * ops[k]["pri"] - tail[k] * (1.0 + NOISE * rnd() * (it >= 4)) for k in range(n)]
+        order = listed(ops, succ, cost[0], MODELS[0], lambda x: urge[x])
+        starts.append((score(order), order))
+    cur, order = min(starts)
+    base = [b_ * cur / len(MODELS) for b_ in base]
     cur = best = score(order)
     best_order = order
     why = [0] * n
@@ -497,7 +604,7 @@ def schedule(ops):
         pairs = []
         while k != -1:
             w = why[k]
-            if w >= 0 and w not in ops[k]["dep"] and ops[w]["kind"] != "d":
+            if w >= 0 and w not in ops[k]["pre"]:
                 pairs.append((w, k))
             k = w if w >= -1 else -2 - w
         if not pairs:
@@ -515,7 +622,7 @@ def schedule(ops):
         else:
             take = {j}
             for x in seg[1:]:
-                if any(y in take for y in ops[x]["dep"]):
+                if any(y in take for y in ops[x]["pre"]):
                     take.add(x)
             if k in take:
                 continue
@@ -525,6 +632,180 @@ def schedule(ops):
         val = score(cand)
         if val < cur + TEMP * (1.0 - it / ITERS) * rnd():
             order, cur = cand, val
+            if val < best:
+                best, best_order = val, cand
+    return best_order
+
+
+def book(busy, t, lat):
+    for i, (lo, hi) in enumerate(busy):
+        if t + lat <= lo:
+            busy.insert(i, (t, t + lat))
+            return t + lat
+        if hi > t:
+            t = hi
+    busy.append((t, t + lat))
+    return t + lat
+
+
+def step(o, e, kind, t, cost, m, wire):
+    occ, lat = cost
+    t += occ
+    if kind == "c":
+        return t, t + lat
+    if e == "q" and kind not in wire[3]:
+        wire[3] += kind
+        t += m[9]
+    if kind == "d":
+        return t, max(book(wire[0], t, lat), book(wire[1], t, lat)) + 2000.0
+    if len(o["k"]) == 2:
+        return t, book(wire[0], t, lat) + m[4] - m[6]
+    return t, book(wire[2], book(wire[1], t, 0.6 * lat) + m[4], lat) + m[4] - m[6]
+
+
+def replay(ops, order, cost, m, why=None, ends=None):
+    hop = m[8]
+    free = {"v": 0.0, "a": 0.0, "p": 0.0, "q": 0.0, "s": 0.0}
+    prev, wire = {}, [[], [], [], ""]
+    end = [0.0] * len(ops) if ends is None else ends
+    for k in order:
+        e, kind, dep = ops[k]["key"]
+        t, w = free[e], prev.get(e, -1)
+        for j in dep:
+            if end[j] + hop > t:
+                t, w = end[j] + hop, -2 - j
+        if kind == "c":
+            t += cost[k][0]
+            free[e] = t
+            t += cost[k][1]
+        else:
+            free[e], t = step(ops[k], e, kind, t, cost[k], m, wire)
+        prev[e], end[k] = k, t
+        if why is not None:
+            why[k] = w
+    last = max(end)
+    return last, end.index(last), sum(end) / len(end)
+
+
+def listed(ops, pre, succ, hard, cost, m, urge, back=False):
+    n = len(ops)
+    left = [len(x) for x in pre]
+    lim = [0.0] * n
+    free = {e: 0.0 for e in "vapqs"}
+    wire = [[], [], [], ""]
+    pool = [k for k in range(n) if left[k] == 0]
+    order, at = [], [0.0] * n
+    while pool:
+        j = min(pool, key=lambda x: max(lim[x], free[ops[x]["eng"]]) + cost[x][0])
+        e = ops[j]["eng"]
+        first = max(lim[j], free[e]) + cost[j][0]
+        k = min((x for x in pool if ops[x]["eng"] == e and (x == j or lim[x] < first)), key=lambda x: urge[x])
+        pool.remove(k)
+        order.append(k)
+        if back:
+            free[e] = end = max(lim[k], free[e]) + cost[k][0]
+        else:
+            free[e], end = step(ops[k], e, ops[k]["kind"], max(lim[k], free[e]), cost[k], m, wire)
+        at[k] = free[e]
+        for x in succ[k]:
+            if (x, k) in hard:
+                lim[x] = max(lim[x], end + m[8] + (cost[x][1] if back else 0.0))
+            left[x] -= 1
+            if left[x] == 0:
+                pool.append(x)
+    return order, at
+
+
+def schedule(ops):
+    n = len(ops)
+    for o in ops:
+        o["key"] = (o["eng"], o["kind"], [j for j in o["dep"] if o["eng"] != "p" or ops[j]["eng"] != "p"])
+    cost = [costs(ops, m) for m in MODELS]
+    pre = [o["pre"] for o in ops]
+    succ = [[] for _ in range(n)]
+    for k, o in enumerate(ops):
+        for j in o["pre"]:
+            succ[j].append(k)
+    hard = set((k, j) for k in range(n) for j in ops[k]["key"][2])
+    drah = set((j, k) for k, j in hard)
+    seed = [SEED]
+
+    def rnd():
+        seed[0] = (seed[0] * 1103515245 + 12345) % 2147483648
+        return seed[0] / 2147483648.0
+
+    base = [replay(ops, range(n), c, m)[0] for c, m in zip(cost, MODELS)]
+
+    def score(od):
+        s = 0.0
+        for c, m, b_ in zip(cost, MODELS, base):
+            r = replay(ops, od, c, m)
+            s += (r[0] + SOFT * r[2]) / b_
+        return s
+
+    m0, c0 = MODELS[0], cost[0]
+    starts = []
+    for it in range(STARTS):
+        tail = [0.0] * n
+        for k in range(n - 1, -1, -1):
+            tail[k] = sum(c0[k]) * (1 + NOISE * rnd()) + (0.0 if ops[k]["kind"] == "c" else 2000.0) + max([0.0] + [tail[x] + m0[8] for x in succ[k]])
+        urge = [-x for x in tail]
+        for r in range(ROUNDS):
+            order, at = listed(ops, pre, succ, hard, c0, m0, urge)
+            starts.append((score(order), order))
+            ends = [0.0] * n
+            replay(ops, order, c0, m0, None, ends)
+            cb = [(c0[k][0], ends[k] - at[k]) for k in range(n)]
+            urge = [-x for x in listed(ops, succ, pre, drah, cb, m0, [-x for x in at], True)[1]]
+    cur, order = min(starts)
+    base = [b_ * cur / len(MODELS) for b_ in base]
+    cur = best = score(order)
+    best_order, moved, pairs = order, True, []
+    why = [0] * n
+    for it in range(ITERS):
+        if it % 8 == 0 or moved:
+            i = int(rnd() * len(MODELS))
+            k = replay(ops, order, cost[i], MODELS[i], why)[1]
+            pairs = []
+            while k != -1:
+                w = why[k]
+                if w >= 0 and w not in pre[k]:
+                    pairs.append((w, k))
+                k = w if w >= -1 else -2 - w
+        moved = False
+        if pairs and rnd() < 0.7:
+            j, k = pairs[int(rnd() * len(pairs))]
+            p0, p1 = order.index(j), order.index(k)
+        else:
+            p0 = int(rnd() * (n - 1))
+            j = order[p0]
+            p1 = p0 + 1
+            while p1 < n and ops[order[p1]]["eng"] != ops[j]["eng"]:
+                p1 += 1
+            if p1 == n:
+                continue
+            k = order[p1]
+        seg = order[p0:p1 + 1]
+        if rnd() < 0.5:
+            take = {k}
+            for x in reversed(seg[:-1]):
+                if any(y in take for y in succ[x]):
+                    take.add(x)
+            if j in take:
+                continue
+            new = [x for x in seg if x in take] + [x for x in seg if x not in take]
+        else:
+            take = {j}
+            for x in seg[1:]:
+                if any(y in take for y in pre[x]):
+                    take.add(x)
+            if k in take:
+                continue
+            new = [x for x in seg if x not in take] + [x for x in seg if x in take]
+        cand = order[:p0] + new + order[p1 + 1:]
+        val = score(cand)
+        if val < cur + TEMP * (1.0 - it / ITERS) * rnd():
+            order, cur, moved = cand, val, True
             if val < best:
                 best, best_order = val, cand
     return best_order

@@ -5,25 +5,35 @@ CO = [1, 0, 2]
 PLANS = {
     "5a": ([(6, 10, 1), (0, 16, 5)], [((1, 5, 1), "L", 0), ((11, 15, 1), "R", 0)], [(1, 0, 1, 1, 3)]),
     "5b": ([(5, 10, 1), (10, 16, 5)], [((0, 5, 1), "L", 0), ((10, 15, 1), "R", 0)], [(1, 0, 1, 1, 1)]),
+    "5c": ([(5, 10, 1), (15, 16, 1)], [((10, 11, 1), "L", 1), ((0, 5, 1), "L", 0), ((10, 15, 1), "R", 0)], []),
     "4a": ([(4, 8, 1), (7, 11, 1)], [((0, 4, 1), "L", 0), ((11, 15, 1), "R", 1)], [(0, 0, 1, 1, 3)]),
-    "4b": ([(4, 8, 1), (12, 15, 1)], [((0, 4, 1), "L", 0), ((8, 12, 1), "R", 0), ((8, 11, 1), "L", 1)], []),
-    "5c": ([(5, 10, 1), (15, 16, 1)], [((0, 5, 1), "L", 0), ((10, 15, 1), "R", 0), ((10, 11, 1), "L", 1)], []),
+    "4b": ([(4, 8, 1), (12, 15, 1)], [((8, 11, 1), "L", 1), ((0, 4, 1), "L", 0), ((8, 12, 1), "R", 0)], []),
     "3a": ([(3, 7, 1), (7, 11, 1)], [((0, 4, 1), "L", 0), ((10, 14, 1), "R", 1)], [(0, 1, 1, 0, 3)]),
+    "3d": ([(3, 6, 1), (9, 12, 1)], [((0, 3, 1), "L", 0), ((6, 9, 1), "R", 0), ((6, 9, 1), "L", 1), ((12, 15, 1), "R", 1)], []),
     "3b": ([(3, 7, 1), (7, 11, 1), (10, 14, 1)], [((0, 4, 1), "L", 0)], [(0, 1, 1, 0, 3), (1, 0, 2, 0, 4)]),
-    "3c": ([(3, 6, 1), (9, 12, 1), (12, 14, 1)], [((0, 3, 1), "L", 0), ((6, 9, 1), "R", 0), ((6, 9, 1), "L", 1), ((9, 11, 1), "L", 2)], []),
 }
-PLAN = [["5b", "5b", "5b"], ["4a", "4b", "4a"], ["3a", "3a", "3a"]]
-PA, PV = 900, 900
-CONFV = [False, False, False]
-ANSA, TABA = True, True
-SEED, STARTS, ROUNDS, NOISE, ITERS, TEMP, SOFT = 1, 30, 4, 0.05, 40000, 0.01, 0.1
-MODELS = [(0.95, 1.4, 3.2, 0.48, 2400, 70.0, 600, 280.0, 90, 1700), (0.85, 1.15, 2.0, 0.43, 2000, 100.0, 400, 350.0, 70, 1200),
-          (1.15, 1.85, 5.0, 0.6, 3300, 45.0, 900, 200.0, 140, 2800)]
+PLAN = [["5c", "5c", "5c"], ["4a", "4b", "4b"], ["3a", "3a", "3a"]]
+ONA = {"an", "rq", "tab", "tx", "yo", "li", "hi", "ht", "s0", "st0", "st2"}
+EARLY = 2
+GATE = (0, [], [])
+OWNT = False
+PA = 900
+PV = 900
+VMIN = 64
+LOOK = 51.0
+AT = {'lag': -2.58, 'sign': -2.15, 'thr': 1.42, 'su': -4.52, 'rq': -2.34, 'sT': 31.17, 'sm': -1.2, 'an': 2.68, 'up': -3.25, 'back': 0.85, 'dedup0': 8.23, 'dedup1': 3.03, 'dedup2': -11.02, 'scat0': -0.33, 'scat1': -3.7, 'fin': 13.52, 'tab': -4.39, 'mir0': 2.79, 'mir1': -9.61, 'kept': 2.67, 'tabs': 10.88, 'relay': -2.43, 'sc': 2.34, 'vote': -4.62, 'fin2': -5.91, 'st': 13.7}
+SEED = 212
+ITERS = 165000
+HURRY = 0.01
+TEMP, SOFT, CRIT, GAP = 0.0035, 0.1, 0.7, 24
+MODELS = [(0.95, 1.4, 3.2, 0.48, 2100, 85.0, 550, 370.0, 90, 1600), (0.85, 1.25, 2.5, 0.43, 2700, 55.0, 750, 330.0, 120, 2200),
+          (1.15, 1.25, 4.0, 0.6, 1800, 100.0, 450, 400.0, 80, 1400), (1.1, 1.9, 5.0, 0.55, 2300, 70.0, 600, 300.0, 110, 1800)]
 NC = len(NS)
 C0 = [sum(NS[:c]) for c in range(NC)]
 WM = 16 * max(NS)
 SPARE, EXO, TABW, PAD = 2048, 2176, 4224, 512
 LIFT, DROP = 3072.0, 8192.0
+PIECES = [("e", 0), ("i", 0), ("i", 1), ("e", 1), ("e", 2), ("e", 3)]
 
 
 def plan(t, c):
@@ -43,16 +53,16 @@ SCRATCH = {
     "tab": _sb(TABW, "float32"), "pft": _sb(TABW, "float32"), "pfi": _sb(2048, "bfloat16"),
     "ofs_s": _sb(4, "int32"), "thr_s": _sb(4, "int32"), "thf": _sb(4, "float32"), "thc": _sb(4, "float32"), "oc": _sb(4, "float32"),
     "ci": _sb(4, "int32"), "cl": _sb(8, "float32"), "cf": _sb(160, "bfloat16"), "iI": _sb(WM, "bfloat16"), "iG": _sb(128, "bfloat16"),
-    "iC": _sb(WM, "bfloat16"), "idn": _sb(EXO + 16, "float32"), "wh": _sb(2048, "bfloat16"), "drop": _sb(128, "bfloat16"),
+    "iC": _sb(WM, "bfloat16"), "wh": _sb(2048, "float16"), "drop": _sb(128, "float16"), "nd": _sb(128, "float16"),
     "r16e": _sb(160, "float16"), "r16o": _sb(160, "float16"), "r32e": _sb(160, "float32"), "r32o": _sb(160, "float32"),
-    "bo": _sb(128, "float16"), "i32": _sb(128, "float32"), "rep": _sb(128, "float32"), "rt": _sb(3 * WM, "float16"),
-    "ub": _sb(144, "bfloat16"), "uh": _sb(144, "bfloat16"),
-    "w2": _sb(14 * 128, "bfloat16"), "exa": _sb(WM, "bfloat16"), "exb": _sb(WM, "bfloat16"), "ones": _sb(WM, "bfloat16"),
-    "tri": _sb(128, "bfloat16"), "kl": _sb(8, "uint16"), "s16": _sb(768, "float16"),
+    "bo": _sb(128, "float16"), "i32": _sb(128, "float32"), "i16": _sb(128, "float16"), "exo": _sb(128, "float16"), "rep": _sb(128, "float32"), "rt": _sb(3 * WM, "float16"),
+    "ub": _sb(144, "bfloat16"), "uh": _sb(144, "bfloat16"), "w2": _sb(14 * 128, "bfloat16"),
+    "exa": _sb(WM, "bfloat16"), "exb": _sb(WM, "bfloat16"), "exc": _sb(WM, "bfloat16"), "ones": _sb(WM, "bfloat16"),
+    "tri": _sb(128, "bfloat16"), "s16": _sb(768, "float16"),
     "rq_o": _sb(144, "uint16"), "rq_i": _sb(144, "uint16"), "an_o": _sb(1536, "float16"), "an_i": _sb(1536, "float16"),
     "xi": _sb(768, "int32"), "zz": _sb(768, "float32"), "yo": _sb(768, "float32"),
-    "hf": _sb(8, "float32"), "hg": _sb(8, "float32"), "hl": _sb(8, "uint16"), "tl": _sb(16, "uint16"), "tx": _sb(32, "uint16"),
-    "rr": _sb(128, "float32"), "eq": _sb(128, "bfloat16"), "sc": _sb(128, "bfloat16"), "hi": _sb(432, "int32"), "hx": _sb(288, "int32"),
+    "hf": _sb(8, "float16"), "hg": _sb(8, "float32"), "tl": _sb(16, "uint16"), "tx": _sb(32, "uint16"),
+    "eq": _sb(128, "bfloat16"), "sc": _sb(128, "bfloat16"), "hi": _sb(432, "int32"), "hx": _sb(288, "int32"),
 }
 for _k in ("ps", "pv0", "pv1", "pd0", "pd1")[:8 - NC]:
     SCRATCH[_k] = ("psum", [128, 8, 4, 16] if _k[1] == "d" else [128, 512], "float32")
@@ -60,20 +70,23 @@ NPD = 5 - NC
 for _c in range(NC):
     _n = NS[_c]
     SCRATCH["px%d" % _c] = ("psum", [128, 32, 16], "float32")
-    SCRATCH["aT%d" % _c] = ("sbuf", [128, _n, 16], "float16")
     SCRATCH["x0%d" % _c] = ("sbuf", [128, _n, 16], "int32")
     SCRATCH["tp%d" % _c] = ("sbuf", [128, _n, 16], "float32")
     SCRATCH["li%d" % _c] = _sb(20 * _n, "uint16")
-    SCRATCH["cc%d" % _c] = _sb(11 * 16 * _n, "bfloat16")
-    SCRATCH["bb%d" % _c] = _sb(3 * 11 * _n, "bfloat16")
-    SCRATCH["su%d" % _c] = _sb(_n, "bfloat16")
+    SCRATCH["cc%d" % _c] = _sb(12 * 16 * _n, "bfloat16")
+    SCRATCH["bb%d" % _c] = _sb(3 * 12 * _n, "bfloat16")
+    SCRATCH["su%d" % _c] = _sb(_n, "float16")
     SCRATCH["sT%d" % _c] = _sb(256, "bfloat16")
+    SCRATCH["st%d" % _c] = _sb(16 * _n, "float16")
     for _t in range(2):
-        SCRATCH["sm%d_%d" % (_t, _c)] = _sb(16 * _n, "float32")
+        SCRATCH["sm%d_%d" % (_t, _c)] = _sb(16 * _n, ("float16", "float32")[_t])
+        if OWNT:
+            SCRATCH["oT%d_%d" % (_t, _c)] = ("sbuf", [128, _n, 16], "float16")
     for _t in range(3):
+        SCRATCH["aT%d_%d" % (_t, _c)] = ("sbuf", [128, _n, 16], "float16")
         for _s, _r in enumerate(plan(_t, _c)[0]):
             SCRATCH["mm%d_%d_%d" % (_t, _c, _s)] = _sb(_n * 16 * size(_r), "bfloat16")
-SEMAPHORES = ["v", "a", "p", "q", "loc"] + ["d%d" % k for k in range(24)] + ["r%d" % k for k in range(6 * NC + 8)]
+SEMAPHORES = ["v", "a", "p", "q", "loc"] + ["d%d" % k for k in range(24)] + ["r%d" % k for k in range(4 * NC + 9)]
 
 
 def pieces(n, k, most):
@@ -87,8 +100,12 @@ def relays(core, T, topo):
     return dst, [h for h in topo.cores_of(core) if T.rank_of(h) is None and topo.die(h) != topo.die(core) and topo.may_write(h, dst)]
 
 
+def inward(core, h, dst, k, topo):
+    return [e for e in topo.engines(core, h) if k == 0 or e not in topo.engines(core, dst)]
+
+
 def landing(T):
-    return [T.pfi[:, 1024 * k:1024 * k + 1024] for k in range(2)] + [T.pft[:, EXO + 512 * k:EXO + 512 * k + 512] for k in range(4)]
+    return [T.pfi[:, 1024 * j:1024 * j + 1024] if what == "i" else T.pft[:, EXO + 512 * j:EXO + 512 * j + 512] for what, j in PIECES]
 
 
 def build(g, core, T, topo):
@@ -96,7 +113,7 @@ def build(g, core, T, topo):
     N = len(T.cores)
     V, S_, P = g.vector, g.scalar, g.tensor
     ops = []
-    cnt = {"pd": 0, "pv": 0, "h": 0, "r": 6}
+    cnt = {"pd": 0, "pv": 0, "h": 0, "r": len(PIECES), "wh": 0}
     pri = [-1.0]
 
     def add(eng, n, fns, r, w, banks=(), k=1.0, kind="c", sem=None, after=()):
@@ -109,6 +126,12 @@ def build(g, core, T, topo):
     def act(n, fn, r, w, banks=(), k=1.0):
         add("a", n, [fn], r, w, banks, k)
 
+    def shift(tag, n, out, in_, c, r, w, banks=(), k=1.0, times=1.0):
+        if tag in ONA or tag.rstrip("0123456789") in ONA:
+            act(n, lambda: S_.activation(out, in_, F.Identity, bias=c, scale=times), r, w, banks, k)
+        else:
+            dve(n, lambda: V.tensor_scalar(out, in_, times, c, A.mult, A.add), r, w, banks, k)
+
     def pe(cyc, fns, r, w, banks):
         add("p", cyc, fns, r, w, banks)
 
@@ -116,7 +139,7 @@ def build(g, core, T, topo):
         Q = {"s": g.sync, "a": S_, "q": g}[q]
         add(q, nbytes, [lambda: Q.dma_start(out, in_)], r, w, kind="d", after=after)
 
-    def send(dst_rank, out, in_, nbytes, r, w, relay=False):
+    def send(dst_rank, out, in_, nbytes, r, w, relay=False, left=None):
         dst = T.cores[dst_rank % N]
         k = cnt["h" if relay else "r"]
         cnt["h" if relay else "r"] += 1
@@ -125,12 +148,13 @@ def build(g, core, T, topo):
         if relay:
             hs = relays(core, T, topo)[1]
             h = hs[k % len(hs)]
-            eng = [e for e in topo.engines(core, h) if e not in eng]
-            arrive = len(topo.engines(h, dst))
-            dst = h
+            eng, arrive, dst = inward(core, h, dst, k, topo), len(topo.engines(h, dst)), h
         rid, pid, _ = topo.addr(dst)
-        add("q", nbytes, [lambda: g.remote_dma(out, in_, T.sem["r%d" % k], T.sem.loc, pid, rid, sum(1 << e for e in eng))],
-            r, w + [("h", k)], k=(2,) if relay else (0, 1), kind="r", sem=("r%d" % k, arrive, len(eng)), after=[("h", k - 1)] if relay and k else [])
+        add("q", nbytes, [lambda: g.remote_dma(out, in_, T.sem["r%d" % k], T.sem[left or "loc"], pid, rid, sum(1 << e for e in eng))],
+            r, w + [("h", k)], k=(2,) if relay else (0, 1), kind="r", sem=("r%d" % k, arrive, 0 if left else len(eng)),
+            after=[("h", k - 1)] if relay and k else [])
+        if left:
+            add("l", 0, [], [("h", k)], [left], kind="l", sem=(left, len(eng)))
 
     def iota(out, pat, base, cm, n, key):
         add("q", n, [lambda: g.iota(out, pat, base, cm, allow_small_or_imprecise_dtypes=True)], [], [key])
@@ -139,13 +163,18 @@ def build(g, core, T, topo):
     col = [T.cl[:, k:k + 1] for k in range(6)]
     main = T.pic_s[:, PAD:PAD + 4096]
 
-    for k, c in enumerate(CO):
+    def marks(c, after):
         f0, W = 16 * C0[c], 16 * NS[c]
-        dma("s", T.shp_s[:, f0:f0 + W], T.shp[:, f0:f0 + W], 512 * W, [], [("shp", c)], [("shp", x) for x in CO[:k]])
+        dma("s", T.shp_s[:, f0:f0 + W], T.shp[:, f0:f0 + W], 512 * W, [], [("shp", c)], after)
+
+    for k, c in enumerate(CO[:EARLY]):
+        marks(c, [("shp", x) for x in CO[:k]])
     dma("a", T.ofs_s[:, 0:3], T.ofs[:], 1536, [], ["ofs"])
-    dma("s", main, T.pic[:], 1 << 20, [], ["pic"], [("shp", x) for x in CO])
+    dma("s", main, T.pic[:], 1 << 20, [], ["pic"], [("shp", x) for x in CO[:EARLY]])
+    for k, c in enumerate(CO[EARLY:]):
+        marks(c, ["pic"] + [("shp", x) for x in CO[:EARLY + k]])
     dma("a", T.thr_s[0:8, 0:3], T.thr[:], 96, [], ["thr"], ["ofs"])
-    dma("s", T.ex_s[:, 0:1024], T.ex[:, 0:1024], 1 << 19, [], [("ex", 0)], ["pic"])
+    dma("s", T.ex_s[:, 0:1024], T.ex[:, 0:1024], 1 << 19, [], [("ex", 0)], ["pic", ("shp", CO[-1])])
     dma("s", T.ex_s[:, 1024:2048], T.ex[:, 1024:2048], 1 << 19, [], [("ex", 1)], [("ex", 0)])
 
     add("q", 4, [lambda: g.iota(T.ci[:], [[0, 4]], 0, 1)], [], ["ci"])
@@ -153,12 +182,10 @@ def build(g, core, T, topo):
     iota(T.iI[:], [[0, WM // 16], [1, 16]], 0, 0, WM, "iI")
     iota(T.iG[:], [[16, 8], [0, 16]], 0, 0, 128, "iG")
     iota(T.iC[:], [[1, WM // 16], [0, 16]], 0, 0, WM, "iC")
-    dma("q", T.tab[:, 0:2048], T.inc[:], 1 << 20, [("shp", CO[-1])], ["tabI"], ["ci", "cf", "iI", "iG", "iC"])
-    for k in range(2):
-        iota(T.idn[:, 1096 * k:1096 * k + 1096], [[1, 1096]], 1096 * k, 0, 1096, ("idn", k))
-    dma("s", T.inc_s[:], T.inc[:], 1 << 19, [("ex", 1)], ["inc_s"])
-    dma("s", T.pic_s[:, PAD + 4096:PAD + 6144], T.pic[:, 0:2048], 1 << 19, ["tabI"], ["picx1"], ["inc_s"])
-    dma("s", T.pic_s[:, PAD + 6144:PAD + 8192], T.pic[:, 2048:4096], 1 << 19, ["inc_s"], ["picx3"], ["picx1"])
+    dma("q", T.tab[:, 0:2048], T.inc[:], 1 << 20, [("shp", CO[EARLY - 1])], ["tabI"], ["ci", "cf", "iI", "iG", "iC"])
+    dma("s", T.inc_s[:], T.inc[:], 1 << 19, [("ex", GATE[0])], ["inc_s"], [("ex", 1)])
+    dma("s", T.pic_s[:, PAD + 4096:PAD + 6144], T.pic[:, 0:2048], 1 << 19, GATE[1], ["picx1"], ["inc_s"])
+    dma("s", T.pic_s[:, PAD + 6144:PAD + 8192], T.pic[:, 2048:4096], 1 << 19, GATE[2], ["picx3"], ["picx1"])
     dma("s", T.pic_s[:, 0:PAD], T.pic[:, 4096 - PAD:4096], 1 << 17, [], ["picx0"], ["picx3"])
     dma("s", T.pic_s[:, PAD + 8192:9216], T.pic[:, 0:PAD], 1 << 17, [], ["picx2"], ["picx0"])
     dve(1, lambda: V.tensor_scalar(T.ci[:, 1:2], T.ci[:, 0:1], 15, None, A.bitwise_and), ["ci"], ["ci1"])
@@ -166,7 +193,7 @@ def build(g, core, T, topo):
     dve(1, lambda: V.tensor_scalar(T.ci[:, 3:4], T.ci[:, 0:1], 4, 1, A.arith_shift_right, A.bitwise_and), ["ci"], ["ci3"])
     dve(1, lambda: V.tensor_copy(T.cl[:, 0:4], T.ci[:]), ["ci", "ci1", "ci2", "ci3"], ["cl"])
     act(1, lambda: S_.activation(col[4], col[3], F.Identity, bias=1.0, scale=-1.0), ["cl"], ["cl4"])
-    act(1, lambda: S_.activation(col[5], col[1], F.Identity, bias=float(SPARE)), ["cl"], ["cl5"])
+    act(1, lambda: S_.activation(col[5], col[1], F.Identity, bias=SPARE - EXO / 2), ["cl"], ["cl5"])
     for buf, cc_, key in ((T.r16e, 4, "r16e"), (T.r16o, 3, "r16o")):
         dve(160, lambda buf=buf, cc_=cc_: V.tensor_scalar(buf[:], T.cf[:], col[0], col[cc_], A.is_equal, A.mult), ["cf", "cl", "cl4"], [key], k=0.5)
     dve(128, lambda: V.tensor_scalar(T.bo[:], T.iG[:], col[2], None, A.is_equal), ["iG", "cl"], ["bo"], k=0.5)
@@ -174,8 +201,9 @@ def build(g, core, T, topo):
     dve(WM, lambda: V.tensor_scalar(T.rt[:, 0:WM], T.iI[:], col[1], T.oc[:, 0:1], A.is_equal, A.mult), ["iI", "cl", "oc"], [("rt", 0)], k=0.5)
     dve(128, lambda: V.tensor_scalar(W2[1], T.cf[:, 16:144], col[0], None, A.is_equal), ["cf", "cl"], [("w2", 1)], k=0.5)
     act(WM, lambda: S_.activation(T.ones[:], T.iI[:], F.Identity, bias=1.0, scale=0.0), ["iI"], ["ones"])
-    for m in (13, 11, 4, 0, 2, 3, 5, 6, 7, 8, 9, 10, 12):
-        sc = -1.0 if m == 11 else -EXO / 2.0 if m == 12 else LIFT if m == 13 else 2.0 ** (m - 1)
+    pri[0] = -0.5
+    for m in (13, 11, 4, 0, 2, 3, 5, 6, 7, 8, 9, 10):
+        sc = -1.0 if m == 11 else LIFT if m == 13 else 2.0 ** (m - 1)
         act(128, lambda m=m, sc=sc: S_.activation(W2[m], W2[1], F.Identity, scale=sc), [("w2", 1)], [("w2", m)])
     pri[0] = -0.4
     dve(143, lambda: V.tensor_scalar(T.ub[:, 0:143], T.cf[:, 1:144], col[2], None, A.is_equal), ["cf", "cl"], ["ub"], k=0.5)
@@ -186,6 +214,9 @@ def build(g, core, T, topo):
             ["iI", "cl", "oc"], [("rt", t)], k=0.5)
     dve(WM, lambda: V.tensor_scalar(T.exa[:], T.iC[:], col[0], -DROP, A.is_equal, A.mult), ["iC", "cl"], ["exa"], k=0.5)
     act(WM, lambda: S_.activation(T.exb[:], T.exa[:], F.Identity, scale=-LIFT / DROP), ["exa"], ["exb"])
+    act(WM, lambda: S_.activation(T.exc[:], T.exa[:], F.Identity, scale=-1.0 / DROP), ["exa"], ["exc"])
+    act(128, lambda: S_.activation(T.exo[:], W2[1], F.Identity, scale=-EXO / 2.0), [("w2", 1)], ["exo"])
+    act(128, lambda: S_.activation(T.i16[:], W2[1], F.Identity), [("w2", 1)], ["i16"])
     act(128, lambda: S_.activation(T.tab[:, SPARE:EXO], T.iG[:], F.Identity, scale=0.0), ["iG"], ["tabD"])
     act(128, lambda: S_.activation(T.pft[:, SPARE:EXO], T.iG[:], F.Identity, scale=0.0), ["iG"], ["pfD"])
     act(128, lambda: S_.activation(T.drop[:], T.iG[:], F.Identity, bias=DROP, scale=0.0), ["iG"], ["drop"])
@@ -193,51 +224,56 @@ def build(g, core, T, topo):
         act(160, lambda e16=e16, e32=e32: S_.activation(e32[:], e16[:], F.Identity), ["r16e", "r16o"], [("r32", k)])
     dve(128, lambda: V.tensor_scalar(T.tri[:], T.iI[:, 0:128], col[1], None, A.is_gt), ["iI", "cl"], ["tri"], k=0.5)
     act(8, lambda: S_.activation(T.tri[:, 15:128:16], T.tri[:, 15:128:16], F.Identity, scale=4096.0), ["tri"], ["tri"])
-    dve(8, lambda: V.tensor_copy(T.kl[:], T.cf[:, 16:24]), ["cf"], ["kl"])
+    act(128, lambda: S_.activation(T.nd[:], W2[1], F.Identity, scale=-DROP), [("w2", 1)], ["nd"])
     act(1, lambda: S_.activation(T.oc[:, 3:4], T.oc[:, 2:3], F.Identity, bias=6144.0 - 2 * LIFT - DROP, scale=-1.0), ["oc"], ["oc3"])
     dve(128, lambda: V.tensor_scalar(T.rep[0:8, :], T.iG[0:8, :], 0.0625, T.cl[0:8, 0:1], A.mult, A.is_equal), ["iG", "cl"], ["rep"])
-    for t in range(3):
-        a_, b_ = (-1.0, 0.5) if CONFV[t] else (-2.0, 11.5)
-        if t == 0 or CONFV[t] != CONFV[t - 1]:
-            dve(1, lambda t=t, a_=a_, b_=b_: V.tensor_scalar(T.thf[0:8, t:3], T.thr_s[0:8, t:3], a_, b_, A.mult, A.add), ["thr"], ["thf"])
+    dve(1, lambda: V.tensor_scalar(T.thf[0:8, 0:3], T.thr_s[0:8, 0:3], -2.0, 11.5, A.mult, A.add), ["thr"], ["thf"])
     pe(256, [lambda: P.matmul(T.ps[:, 0:3], T.rep[0:8, :], T.thf[0:8, 0:3], True, True)], ["rep", "thf"], ["ps"], ["ps"])
     act(1, lambda: S_.activation(T.thc[:, 0:3], T.ps[:, 0:3], F.Identity), ["ps"], ["thc"], ["ps"])
-    pri[0] = 0.5
     for k in range(4):
-        o_, i_ = T.tab[:, EXO + 512 * k:EXO + 512 * k + 512], T.ex_s[:, 512 * k:512 * k + 512]
-        if TABA:
-            act(512, lambda o_=o_, i_=i_: S_.activation(o_, i_, F.Identity, bias=-2048.0), [("ex", k // 2)], [("tabE", k)])
-        else:
-            dve(512, lambda o_=o_, i_=i_: V.tensor_scalar(o_, i_, -2048.0, None, A.add), [("ex", k // 2)], [("tabE", k)])
+        pri[0] = AT["tab"] + AT["tabs"] * k
+        shift("tab%d" % k, 512, T.tab[:, EXO + 512 * k:EXO + 512 * k + 512], T.ex_s[:, 512 * k:512 * k + 512], -2048.0, [("ex", k // 2)], [("tabE", k)])
     tabk = ["tabI", "tabD"] + [("tabE", k) for k in range(4)]
     land = landing(T)
-    pri[0] = 0.6
-    for k in range(2):
-        send(rank - 3, land[k], T.inc_s[:, 1024 * k:1024 * k + 1024], 1 << 18, ["inc_s"], [("pfi", k)], True)
-    for k in range(4):
-        send(rank - 3, land[2 + k], T.tab[:, EXO + 512 * k:EXO + 512 * k + 512], 1 << 18, [("tabE", k)], [("pfe", k)], True)
-    pri[0] = NC
+
+    def piece(k):
+        what, j = PIECES[k]
+        pri[0] = AT["relay"] + 0.5 * k
+        if what == "e":
+            send(rank - 3, land[k], T.tab[:, EXO + 512 * j:EXO + 512 * j + 512], 1 << 18, [("tabE", j)], [("pfe", j)], True)
+        else:
+            send(rank - 3, land[k], T.inc_s[:, 1024 * j:1024 * j + 1024], 1 << 18, ["inc_s"], [("pfi", j)], True)
+
+    for k in range(len(PIECES)):
+        piece(k)
+
+    pri[0] = -0.3
     for h in range(16):
         add("q", 148, [lambda h=h: g.affine_select(T.wh[:, 128 * h:128 * h + 128], T.drop[:], [[-16, 8], [0, 16]], A.is_equal, 0.0, -h, 1)],
-            ["drop"], [("wh", h)])
+            ["drop"], [("wh", h)], after=["tabI"])
+    whk = [("wh", h) for h in range(16)]
 
-    def route(c, src, e, o, cyc, key, stop):
+    def route(c, src, wide, key, stop):
         n, px = NS[c], T["px%d" % c]
+        e, o, keys = (T.r32e, T.r32o, [("r32", 0), ("r32", 1)]) if wide else (T.r16e, T.r16o, ["r16e", "r16o"])
         E = [[e[:, 16:144], e[:, 0:128]], [o[:, 32:160], o[:, 16:144]]]
-        pe(4 * max(64, 8 * n) * cyc, [lambda x=x, y=y: P.matmul(px[:, x:n:2, :], E[x][y], src[:, y:n:2, :], False, stop and x == 1 and y == 1)
-                                      for x in range(2) for y in range(2)], key + [("px", c)], [("px", c)], ["px%d" % c])
+        pe(4 * max(64, 8 * n) * (4 if wide else 1),
+           [lambda x=x, y=y: P.matmul(px[:, x:n:2, :], E[x][y], src[:, y:n:2, :], False, stop and x == 1 and y == 1) for x in range(2) for y in range(2)],
+           keys + [key, ("px", c)], [("px", c)], ["px%d" % c])
 
     def kept(t, c, offsets):
         n, W, px = NS[c], 16 * NS[c], T["px%d" % c]
-        if t == 0:
-            fns, cyc, r = [lambda: P.matmul(px[:, 0:n, :], W2[13], T.ones[:, 0:W], True, False)], W, [("w2", 13), "ones"]
-        else:
-            fns = [lambda: P.matmul(px[:, 0:n, :], T.i32[:], T["sm%d_%d" % (t - 1, c)][:], True, False),
-                   lambda: P.matmul(px[:, 0:n, :], T["sT%d" % c][0:n, 128 * t - 128:128 * t], T.exb[0:n, 0:W], False, False)]
-            cyc, r = 5 * W, ["i32", ("sm", t - 1, c), ("sT", t - 1, c), "exb"]
         if offsets:
-            fns.append(lambda: P.matmul(px[:, 0:n, :], T.bo[:], T.rt[:, WM * t:WM * t + W], False, False))
-            cyc, r = cyc + W, r + ["bo", ("rt", t)]
+            fns, cyc, r = [lambda: P.matmul(px[:, 0:n, :], T.bo[:], T.rt[:, WM * t:WM * t + W], True, False)], W, ["bo", ("rt", t)]
+        else:
+            fns, cyc, r = [lambda: P.matmul(px[:, 0:n, :], W2[13], T.ones[:, 0:W], True, False)], W, [("w2", 13), "ones"]
+        if t == 1:
+            fns.append(lambda: P.matmul(px[:, 0:n, :], T.i16[:], T["sm0_%d" % c][:], False, False))
+            cyc, r = cyc + W, r + ["i16", ("sm", 0, c)]
+        if t == 2:
+            fns += [lambda: P.matmul(px[:, 0:n, :], T.i32[:], T["sm1_%d" % c][:], False, False),
+                    lambda: P.matmul(px[:, 0:n, :], T["sT%d" % c][0:n, 128:256], T.exb[0:n, 0:W], False, False)]
+            cyc, r = cyc + 5 * W, r + ["i32", ("sm", 1, c), ("sT", 1, c), "exb"]
         pe(cyc, fns, r, [("px", c)], ["px%d" % c])
 
     def sets(t, c):
@@ -249,26 +285,34 @@ def build(g, core, T, topo):
 
     def update(t, c):
         n, W, f0 = NS[c], 16 * NS[c], 16 * C0[c]
-        aT, px, li, x0, pk = T["aT%d" % c], T["px%d" % c], T["li%d" % c], T["x0%d" % c], "px%d" % c
+        aT, px, li, x0, pk = T["aT%d_%d" % (t, c)], T["px%d" % c], T["li%d" % c], T["x0%d" % c], "px%d" % c
         if t == 0:
-            dve(W, lambda: V.tensor_scalar(T.s16[:, f0:f0 + W], T.shp_s[:, f0:f0 + W], -2048.0, None, A.add), [("shp", c)], [("s16", c)])
+            shift("s%d" % c, W, T.s16[:, f0:f0 + W], T.shp_s[:, f0:f0 + W], -2048.0, [("shp", c)], [("s16", c)])
             src, key = T.s16[:, f0:f0 + W], ("s16", c)
         else:
             src, key = T.an_i[:, 768 * (t - 1) + f0:768 * (t - 1) + f0 + W], ("an_i", t - 1, c)
+        pri[0] -= AT["kept"]
         kept(t, c, True)
-        dve(W, lambda: V.transpose(aT[:], src), [key], [("aT", c)], k=0.5)
-        route(c, aT, T.r16e, T.r16o, 1, [("aT", c), "r16e", "r16o"], True)
+        pri[0] += AT["kept"]
+        if t == 0 or not OWNT:
+            dve(W, lambda: V.transpose(aT[:], src), [key], [("aT", t, c)], k=0.5)
+        route(c, aT, False, ("aT", t, c), True)
         if t == 0:
-            dve(W, lambda: V.tensor_scalar(x0[:], px[:, 0:n, :], 4096.0 - LIFT, None, A.add), [("px", c)], [("x0", c)], [pk])
+            shift("x%d" % c, W, x0[:], px[:, 0:n, :], 4096.0, [("px", c)], [("x0", c)], [pk])
             dve(W, lambda: V.tensor_scalar(x0[:], x0[:], 4095, None, A.bitwise_and), [("x0", c)], [("x0", c)])
+            p0 = pri[0]
+            pri[0] = -0.45 if c in CO[:EARLY] else AT["st"]
+            kept(t, c, False)
+            route(c, aT, False, ("aT", t, c), True)
+            shift("st%d" % c, W, T["st%d" % c][:], px[:, 0:n, :], -LIFT, [("px", c)], [("st", c)], [pk])
+            pri[0] = p0
         o = 0
         for j, (lo, hi, st) in enumerate(sets(t, c)):
             w = n * size((lo, hi, st))
             if t == 0:
-                dve(w, lambda o=o, w=w, lo=lo, hi=hi, st=st: V.tensor_copy(li[:, o:o + w], x0[:, :, lo:hi:st]), [("x0", c)], [("li", c, j)])
+                shift("lz%d" % c, w, li[:, o:o + w], x0[:, :, lo:hi:st], 0.0, [("x0", c)], [("li", c, j)])
             else:
-                dve(w, lambda o=o, w=w, lo=lo, hi=hi, st=st: V.tensor_scalar(li[:, o:o + w], px[:, 0:n, lo:hi:st], 4096.0 - LIFT + PAD, None, A.add),
-                    [("px", c)], [("li", c, j)], [pk])
+                shift("li%d%d" % (t, j), w, li[:, o:o + w], px[:, 0:n, lo:hi:st], 4096.0 - LIFT * (t - 1) + PAD, [("px", c)], [("li", c, j)], [pk])
             o += w
 
     def compute(t, c):
@@ -283,9 +327,17 @@ def build(g, core, T, topo):
         ck = lambda o, a, b: [("cc", c, o, x) for x in range(a, b, 2)]
         lst = lambda j, k, a, b: li[:, lo_[j] + a * k:lo_[j] + b * k]
         M = lambda s, a, b: mm[s][:, 16 * size(sr[s]) * a:16 * size(sr[s]) * b]
+        j0 = pri[0]
+        when, acc, tot = {}, 0.0, sum(size(x) for x in sr) * n
+        for a, s, b in sorted((a, s, b) for s, x in enumerate(sr) for a, b in pieces(n, size(x), PA)):
+            for x in range(a, b, 2):
+                when[s, x] = j0 + 0.95 * acc / tot
+            acc += size(sr[s]) * (b - a)
+        ready = lambda s, a, b: max(when[s, x] for x in range(a, b, 2))
         for s, x in enumerate(sr):
             k = size(x)
             for a, b in pieces(n, k, PA):
+                pri[0] = when[s, a]
                 act(16 * (b - a) * k, lambda s=s, a=a, b=b, k=k: S_.activation(M(s, a, b), win.indirect(lst(s, k, a, b)), F.Identity),
                     [("li", c, s)] + wk, mk(s, a, b), k="g")
         pv, pvk = T["pv%d" % cnt["pv"]], "pv%d" % cnt["pv"]
@@ -299,25 +351,30 @@ def build(g, core, T, topo):
             if signs:
                 fns.append(lambda: P.matmul(pv[:, o0:o1], W2[4], T.ones[:, 0:o1 - o0], False, True))
             vk.append((pvk, "v", len(vk)))
+            pri[0] += AT["vote"]
             pe(len(fns) * max(64, o1 - o0), fns, keys + ["ub", "uh", ("w2", 4), "ones"], vk[-1:], [pvk])
 
-        o = 0
+        o, o0, keys = 0, 0, []
         for x, side, s in vr:
             k, j = size(x), rs.index(x)
             for z, i in enumerate(range(*x)):
                 at[i if side == "L" else i - d] = (o + z, o + n * k, k)
             for a, b in pieces(n, k, PV):
+                pri[0] = ready(s, a, b) + AT["lag"] + 0.01 * o / n
                 dve(16 * (b - a) * k, lambda o=o, a=a, b=b, k=k, j=j, s=s, side=side: V.tensor_tensor(
                     cc[:, 16 * (o + a * k):16 * (o + b * k)], win.indirect(lst(j, k, a, b)), M(s, a, b), A.is_gt if side == "L" else A.is_lt),
                     [("li", c, j)] + wk + mk(s, a, b), ck(o // n, a, b), k="g")
-            votes(o, o + n * k, ck(o // n, 0, n), False)
+            keys += ck(o // n, 0, n)
             o += n * k
-        o0, keys = o, []
+            if o - o0 >= VMIN or (x, side, s) == vr[-1]:
+                votes(o0, o, keys, False)
+                o0, keys = o, []
         for s0, i0, s1, i1, k in dr:
             for z, i in enumerate(list(range(*sr[s0]))[i0:i0 + k]):
                 at[i] = (o + z, o + n * k, k)
             ks = size(sr[s0])
             for a, b in pieces(n, 2 if ks == 2 else 4, 512):
+                pri[0] = max(ready(s0, a, b), ready(s1, a, b)) + AT["sign"]
                 pd, pk = T["pd%d" % cnt["pd"]], "pd%d" % cnt["pd"]
                 cnt["pd"] = (cnt["pd"] + 1) % NPD
                 rows = (b - a) // 2 if ks == 2 else b - a
@@ -336,51 +393,56 @@ def build(g, core, T, topo):
             o += n * k
         if dr:
             votes(o0, o, keys, True)
-        q = 11 * n
+        q = o
+        pri[0] = j0 + AT["thr"]
         act(q, lambda: S_.activation(bb[:, 2 * q:3 * q], pv[:, 0:q], F.Abs, bias=-7.5), vk, [("bb", c, 2)], [pvk])
-        if CONFV[t]:
-            dve(q, lambda: V.tensor_scalar(bb[:, q:2 * q], bb[:, 2 * q:3 * q], 4.0, None, A.is_ge), [("bb", c, 2)], [("bb", c, 1)], k=0.5)
-        else:
-            act(q, lambda: S_.activation(bb[:, q:2 * q], bb[:, 2 * q:3 * q], F.Sign, bias=-4.0), [("bb", c, 2)], [("bb", c, 1)])
+        act(q, lambda: S_.activation(bb[:, q:2 * q], bb[:, 2 * q:3 * q], F.Sign, bias=-4.0), [("bb", c, 2)], [("bb", c, 1)])
         act(q, lambda: S_.activation(bb[:, 0:q], pv[:, 0:q], F.Sign, bias=-8.5), vk, [("bb", c, 0)], [pvk])
         B = lambda z, m: bb[:, z + at[m][0]:z + at[m][1]:at[m][2]]
         pe(11 * 64, [lambda m=m: P.matmul(pv[:, 256:256 + n], W2[1], B(q, m), m == 0, m == 10) for m in range(11)],
            [("bb", c, 1), ("w2", 1)], [(pvk, "c")], [pvk])
         pe(11 * 64, [lambda m=m: P.matmul(T.ps[:, 0:n], W2[m], B(0, m), m == 0, False) for m in range(11)],
            [("bb", c, 0)] + [("w2", m) for m in range(11)], ["ps"], ["ps"])
+        pri[0] = j0 + AT["su"]
         act(n, lambda: S_.activation(su[:], pv[:, 256:256 + n], F.Sign, bias=T.thc[:, t:t + 1]), [(pvk, "c"), "thc"], [("su", c)], [pvk])
-        pe(64, [lambda: P.matmul(T.ps[:, 0:n], W2[12], su[:], False, True)], [("su", c), ("w2", 12), "ps"], ["ps"], ["ps"])
+        pe(64, [lambda: P.matmul(T.ps[:, 0:n], T.exo[:], su[:], False, True)], [("su", c), "exo", "ps"], ["ps"], ["ps"])
         r0, c0, pk = 48 * t + C0[c], C0[c], "px%d" % c
-        dve(n, lambda: V.tensor_scalar(T.rq_o[:, r0:r0 + n], T.ps[:, 0:n], 1023.5 + EXO / 2, None, A.add), ["ps"], [("rq_o", t, c)], ["ps"])
+        pri[0] = j0 + AT["rq"]
+        shift("rq%d" % t, n, T.rq_o[:, r0:r0 + n], T.ps[:, 0:n], 1023.5 + EXO / 2, ["ps"], [("rq_o", t, c)], ["ps"])
         if t == 2:
             pe(16 * 64, [lambda h=h: P.matmul(px[:, 0:n, h], T.wh[:, 128 * h:128 * h + 128], su[:], False, h == 15) for h in range(16)],
-               [("su", c), ("px", c)] + [("wh", h) for h in range(16)], [("px", c)], [pk])
+               [("su", c), ("px", c)] + whk, [("px", c)], [pk])
             return
         send(rank + 1 + t, T.rq_i[:, r0:r0 + n], T.rq_o[:, r0:r0 + n], 256 * n, [("rq_o", t, c)], [("rq_i", t, c)])
-        if t == 1 and c == CO[0]:
+        if t == 1 and c == CO[1]:
             dma("q", T.pft[:, 0:2048], T.pfi[:], 1 << 20, [("pfi", 0), ("pfi", 1)], ["pfI"], [("rq_i", t, c)])
         a0 = 768 * t + 16 * c0
-        if ANSA:
-            act(W, lambda: S_.activation(T.an_o[:, a0:a0 + W], T.tab[:, 0:TABW].indirect(T.rq_i[:, r0:r0 + n]), F.Identity),
-                [("rq_i", t, c)] + tabk, [("an_o", t, c)], k="g")
+        pri[0] = j0 + AT["an"]
+        shift("an%d" % t, W, T.an_o[:, a0:a0 + W], T.tab[:, 0:TABW].indirect(T.rq_i[:, r0:r0 + n]), 0.0, [("rq_i", t, c)] + tabk, [("an_o", t, c)], k="g")
+        if OWNT:
+            oT = T["oT%d_%d" % (t, c)]
+            dve(W, lambda: V.transpose(oT[:], T.an_o[:, a0:a0 + W]), [("an_o", t, c)], [("oT", t, c)], k=0.5)
+            send(rank - 1 - t, T["aT%d_%d" % (t + 1, c)][:], oT[:], 256 * W, [("oT", t, c)], [("an_i", t, c), ("aT", t + 1, c)])
         else:
-            dve(W, lambda: V.tensor_copy(T.an_o[:, a0:a0 + W], T.tab[:, 0:TABW].indirect(T.rq_i[:, r0:r0 + n])),
-                [("rq_i", t, c)] + tabk, [("an_o", t, c)], k="g")
-        send(rank - 1 - t, T.an_i[:, a0:a0 + W], T.an_o[:, a0:a0 + W], 256 * W, [("an_o", t, c)], [("an_i", t, c)])
-        pri[0] += 1.5
-        pe(128, [lambda: P.matmul(pv[0:n, 384:512], su[:], W2[1], True, True)], [("su", c), ("w2", 1)], [(pvk, "t")], [pvk])
-        act(128, lambda: S_.activation(sT[0:n, 128 * t:128 * t + 128], pv[0:n, 384:512], F.Relu, scale=-1.0), [(pvk, "t")], [("sT", t, c)], [pvk])
+            send(rank - 1 - t, T.an_i[:, a0:a0 + W], T.an_o[:, a0:a0 + W], 256 * W, [("an_o", t, c)], [("an_i", t, c)])
+        pri[0] = j0 + AT["sT"]
+        pe(128, [lambda: P.matmul(pv[0:n, 384:512], su[:], T.i16[:], True, True)], [("su", c), "i16"], [(pvk, "t")], [pvk])
+        act(128, lambda: S_.activation(sT[0:n, 128 * t:128 * t + 128], pv[0:n, 384:512], F.Relu, scale=1.0 - 2 * t), [(pvk, "t")], [("sT", t, c)], [pvk])
+        if t == 0:
+            pe(W, [lambda: P.matmul(px[:, 0:n, :], sT[0:n, 0:128], T.exc[0:n, 0:W], True, True)], [("sT", t, c), "exc"], [("px", c)], [pk])
+            dve(W, lambda: V.tensor_tensor(T["sm0_%d" % c][:], T["st%d" % c][:], px[:, 0:n, :], A.mult), [("px", c), ("st", c)], [("sm", t, c)], [pk])
+            return
         kept(t, c, False)
-        route(c, T["aT%d" % c], T.r16e, T.r16o, 1, [("aT", c), "r16e", "r16o"], False)
-        pe(W, [lambda: P.matmul(px[:, 0:n, :], sT[0:n, 128 * t:128 * t + 128], T.exa[0:n, 0:W], False, True)],
-           [("sT", t, c), "exa", ("px", c)], [("px", c)], [pk])
-        act(W, lambda: S_.activation(T["sm%d_%d" % (t, c)][:], px[:, 0:n, :], F.Relu), [("px", c)], [("sm", t, c)], [pk])
+        route(c, T["aT%d_%d" % (t, c)], False, ("aT", t, c), False)
+        pe(W, [lambda: P.matmul(px[:, 0:n, :], sT[0:n, 128:256], T.exa[0:n, 0:W], False, True)], [("sT", t, c), "exa", ("px", c)], [("px", c)], [pk])
+        pri[0] = j0 + AT["sm"]
+        act(W, lambda: S_.activation(T["sm1_%d" % c][:], px[:, 0:n, :], F.Relu), [("px", c)], [("sm", t, c)], [pk])
 
     def back(c):
         n, W, px, tp, pk = NS[c], 16 * NS[c], T["px%d" % c], T["tp%d" % c], "px%d" % c
         dve(W, lambda: V.transpose(tp[:], px[:, 0:n, :]), [("px", c)], [("tp", c)], [pk])
         pe(W, [lambda: P.matmul(px[:, 0:n, :], W2[13], T.ones[:, 0:W], True, False)], [("w2", 13), "ones"], [("px", c)], [pk])
-        route(c, tp, T.r32e, T.r32o, 4, [("tp", c), ("r32", 0), ("r32", 1)], False)
+        route(c, tp, True, ("tp", c), False)
 
     def finish(c):
         n, W, f0, r0 = NS[c], 16 * NS[c], 16 * C0[c], 96 + C0[c]
@@ -388,62 +450,76 @@ def build(g, core, T, topo):
         dve(W, lambda: V.tensor_scalar(zz, px[:, 0:n, :], T.oc[:, 3:4], 2048.0, A.add, A.max), [("px", c), "oc3"], [("zz", c)], ["px%d" % c])
         dve(W, lambda: V.tensor_tensor(xi, T.pft[:, 0:TABW].indirect(T.rq_o[:, r0:r0 + n]), zz, A.add),
             [("rq_o", 2, c), ("zz", c), "pfI", "pfD"] + [("pfe", k) for k in range(4)], [("xi", c)], k="g")
+        pri[0] += AT["fin2"]
         dve(W, lambda: V.tensor_scalar(xi, xi, 4095, None, A.bitwise_and), [("xi", c)], [("xi", c)])
-        dve(W, lambda: V.tensor_copy(yo, xi), [("xi", c)], [("yo", c)])
+        shift("yo%d" % c, W, yo, xi, 0.0, [("xi", c)], [("yo", c)])
         dma("s", T.ys[:, f0:f0 + W], yo, 512 * W, [("yo", c)], [("ys", c)])
 
     def scatter(win, tl, l0, src, h0, r, w):
         for k in range(8):
+            pri[0] += AT["sc"]
             dve(16, lambda k=k: V.tensor_copy(win[:, 0:EXO].indirect(tl[:, l0 + 2 * k:l0 + 2 * k + 1]), src[:, h0 + 16 * k:h0 + 16 * k + 16]), r, w, k="s")
 
     def halve(t):
         rk = [("rq_i", t, k) for k in range(NC) if C0[k] < 8 * t + 8 and C0[k] + NS[k] > 8 * t]
-        r0, h0 = 56 * t, 144 * t
+        r0, h0, j0 = 56 * t, 144 * t, NC * t + max(CO.index(x[2]) for x in rk)
         hi, ht = T.hi[:, h0:h0 + 128], T.hi[:, h0 + 128:h0 + 136]
         if t == 2:
+            pri[0] = j0 + AT["rq"] + 0.01
             send(rank + 3, T.rq_i[:, r0:r0 + 8], T.rq_o[:, r0:r0 + 8], 2048, [("rq_o",) + x[1:] for x in rk], rk)
-        dve(1, lambda: V.tensor_scalar(T.hl[:], T.rq_i[:, r0:r0 + 8], float(EXO), None, A.min), rk, ["hl"])
-        dve(1, lambda: V.tensor_copy(T.hf[:], T.hl[:]), ["hl"], ["hf"])
-        act(128, lambda: S_.activation(T.rr[:], T.idn[:, 0:EXO + 16].indirect(T.hl[:, 0:8]), F.Identity), [("idn", 0), ("idn", 1), "hl"], ["rr"], k="g")
+        pri[0] = j0 + AT["dedup%d" % t]
+        dve(8, lambda: V.tensor_scalar(T.hf[:], T.rq_i[:, r0:r0 + 8], float(EXO), -EXO / 2, A.min, A.add), rk, ["hf"])
         if t < 2:
-            a0 = 896 * t
-            dve(128, lambda: V.tensor_scalar(hi, T.an_o[:, a0:a0 + 128], 0.5, -0.25, A.mult, A.add), [("an_o",) + x[1:] for x in rk], [("hi", t)])
+            shift("hi%d" % t, 128, hi, T.an_o[:, 896 * t:896 * t + 128], -0.25, [("an_o",) + x[1:] for x in rk], [("hi", t)], times=0.5)
         else:
-            dve(128, lambda: V.tensor_scalar(hi, T.tab[:, 0:EXO + 16].indirect(T.hl[:, 0:8]), 0.5, -0.25, A.mult, A.add), tabk + ["hl"], [("hi", t)], k="g")
-        dve(128, lambda: V.tensor_tensor(T.eq[:], T.hf[:, 0:8].indirect(T.kl[:, 0:8]), T.rr[:], A.is_equal), ["hf", "kl", "rr"], ["eq"], k="g")
+            shift("hi%d" % t, 128, hi, T.tab[:, 0:TABW].indirect(T.rq_i[:, r0:r0 + 8]), -0.25, tabk + rk, [("hi", t)], k="g", times=0.5)
+        pd, pk = T["pd%d" % cnt["pd"]], "pd%d" % cnt["pd"]
+        cnt["pd"] = (cnt["pd"] + 1) % NPD
+        pe(128 + 32 * 64, [lambda: P.matmul(pd[:, :, 0, :], W2[13], T.ones[:, 0:128], True, False)]
+           + [lambda h=h, z=z: P.matmul(pd[:, :, 0, h], T.wh[:, 128 * h:128 * h + 128] if z else T.nd[:], T.hf[:], False, h == 15 and z == 1)
+              for h in range(16) for z in range(2)], [("w2", 13), "ones", "nd", "hf"] + whk, [pk], [pk])
+        dve(128, lambda: V.tensor_scalar(T.eq[:], pd[:, :, 0, :], LIFT, None, A.is_equal), [pk], ["eq"], [pk])
         dve(128, lambda: V.tensor_tensor_scan(T.sc[:], T.eq[:], T.tri[:], 0.0, A.max, A.mult), ["eq", "tri"], ["sc"], k=0.5)
-        dve(1, lambda: V.tensor_tensor(T.hg[:], T.sc[:, 15:128:16], T.hf[:], A.max), ["sc", "hf"], ["hg"])
-        dve(1, lambda: V.tensor_scalar(T.tl[:, 0:16:2], T.hg[:], col[5], None, A.min), ["hg", "cl5"], ["tl"])
+        dve(8, lambda: V.tensor_tensor(T.hg[:], T.sc[:, 15:128:16], T.hf[:], A.add), ["sc", "hf"], ["hg"])
+        dve(8, lambda: V.tensor_scalar(T.tl[:, 0:16:2], T.hg[:], col[5], EXO / 2, A.min, A.add), ["hg", "cl5"], ["tl"])
+        p0 = pri[0]
+        if t < 2:
+            pri[0] = NC * t + NC + AT["scat%d" % t]
         scatter(T.tab, T.tl, 0, T.hi, h0, ["tl", ("hi", t)], ["tabI", "tabD"])
         if t == 2:
             dma("q", T.yi[:], T.tab[:, 0:2048], 1 << 19, ["tabI"], ["yi"])
             return
-        dve(1, lambda: V.tensor_scalar(ht, T.hg[:], col[5], None, A.min), ["hg", "cl5"], [("ht", t)])
+        pri[0] = p0
+        shift("ht", 8, ht, T.tl[:, 0:16:2], 0.0, ["tl"], [("ht", t)])
         send(rank - 3, T.hx[:, h0:h0 + 136], T.hi[:, h0:h0 + 136], 512 * 136, [("hi", t), ("ht", t)], [("hx", t)])
 
     def mirror(t):
         h0 = 144 * t
-        dve(1, lambda: V.tensor_copy(T.tx[:, 16 * t:16 * t + 16:2], T.hx[:, h0 + 128:h0 + 136]), [("hx", t)], [("tx", t)])
+        shift("tx", 8, T.tx[:, 16 * t:16 * t + 16:2], T.hx[:, h0 + 128:h0 + 136], 0.0, [("hx", t)], [("tx", t)])
         scatter(T.pft, T.tx, 16 * t, T.hx, h0, [("tx", t), ("hx", t)], ["pfI", "pfD"])
 
     for t in range(3):
         for k, c in enumerate(CO):
-            pri[0] = -0.5 + 0.01 * k if t == 0 else NC * t + k
+            pri[0] = -0.7 + 0.01 * k if t == 0 and k < EARLY else NC * t + k + AT["up"]
             update(t, c)
         if t == 2:
             for k, c in enumerate(CO):
-                pri[0] = NC * t + k + 0.7
+                pri[0] = NC * t + k + AT["back"]
                 back(c)
         for k, c in enumerate(CO):
             pri[0] = NC * t + k
             compute(t, c)
-        pri[0] = NC * t + NC - 0.5
-        halve(t)
+            if t == 2 and k == 1:
+                halve(t)
+        if t < 2:
+            halve(t)
         if t == 1:
+            pri[0] = NC + AT["mir0"]
             mirror(0)
+            pri[0] = 2 * NC - 1 + AT["mir1"]
             mirror(1)
     for k, c in enumerate(CO):
-        pri[0] = 2 * NC + k + 0.5
+        pri[0] = 2 * NC + k + AT["fin"]
         finish(c)
     return ops
 
@@ -451,26 +527,17 @@ def build(g, core, T, topo):
 def depend(ops):
     last_w, readers, bank = {}, {}, {}
     for k, o in enumerate(ops):
-        dep = set()
-        for x in o["r"]:
-            if x in last_w:
-                dep.add(last_w[x])
-        o["raw"] = set(dep)
+        dep = set(last_w[x] for x in o["r"] + o["w"] if x in last_w)
         for x in o["w"]:
-            if x in last_w:
-                dep.add(last_w[x])
             dep.update(readers.get(x, []))
         for b in o["banks"]:
             e, cur, prev = bank.get(b, (o["eng"], [], []))
             if e != o["eng"]:
                 cur, prev = [], cur
             dep.update(prev)
-            if o["eng"] == "p":
-                dep.update(cur[-1:])
             bank[b] = (o["eng"], cur + [k], prev)
-        dep.discard(k)
-        o["dep"] = sorted(dep)
         o["pre"] = sorted(dep | set(last_w[x] for x in o["after"]))
+        o["dep"] = sorted(j for j in dep if o["eng"] != "p" or ops[j]["eng"] != "p")
         for x in o["r"]:
             readers.setdefault(x, []).append(k)
         for x in o["w"]:
@@ -479,7 +546,7 @@ def depend(ops):
 
 
 def costs(ops, m):
-    cy, gam, sca, pcy, rfix, rbw, riss, dbw = m[:8]
+    cy, gam, sca, pcy, rfix, rbw, riss, dbw, hop = m[:9]
     out = []
     for o in ops:
         e, n, k = o["eng"], o["n"], o["k"]
@@ -487,6 +554,8 @@ def costs(ops, m):
             out.append((1000.0 if e == "q" else 100.0, 60 + n / dbw))
         elif o["kind"] == "r":
             out.append((riss, 150 + n / rbw))
+        elif e == "l":
+            out.append((0.0, riss - rfix - hop))
         elif e == "p":
             out.append((n * pcy, 60.0))
         elif e == "q":
@@ -496,145 +565,6 @@ def costs(ops, m):
         else:
             out.append((40 + max(64, n * k) * cy, 0.0))
     return out
-
-
-def step(o, e, kind, t, cost, m, wire):
-    occ, lat = cost
-    t += occ
-    if kind == "c":
-        return t, t + lat
-    if e == "q" and kind not in wire[3]:
-        wire[3] += kind
-        t += m[9]
-    if kind == "d":
-        wire[0], wire[1] = max(wire[0], t) + lat, max(wire[1], t) + lat
-        return t, max(wire[0], wire[1]) + 2000.0
-    if len(o["k"]) == 2:
-        wire[0] = max(wire[0], t) + lat
-        return t, wire[0] + m[4] - m[6]
-    wire[1] = max(wire[1], t) + 0.6 * lat
-    wire[2] = max(wire[2], wire[1] + m[4]) + lat
-    return t, wire[2] + m[4] - m[6]
-
-
-def replay(ops, order, cost, m, why=None, ends=None):
-    hop = m[8]
-    free = {"v": 0.0, "a": 0.0, "p": 0.0, "q": 0.0, "s": 0.0}
-    prev, wire = {}, [0.0, 0.0, 0.0, ""]
-    end = [0.0] * len(ops) if ends is None else ends
-    last, lastk = 0.0, 0
-    for k in order:
-        e, kind, dep = ops[k]["key"]
-        t, w = free[e], prev.get(e, -1)
-        for j in dep:
-            if end[j] > t:
-                t, w = end[j] + hop, -2 - j
-        if kind == "c":
-            t += cost[k][0]
-            free[e], t = t, t + cost[k][1]
-        else:
-            free[e], t = step(ops[k], e, kind, t, cost[k], m, wire)
-        prev[e], end[k] = k, t
-        if why is not None:
-            why[k] = w
-        if t > last:
-            last, lastk = t, k
-    return last, lastk
-
-
-def listed(ops, succ, cost, m, key):
-    n = len(ops)
-    left = [len(o["pre"]) for o in ops]
-    lim = [0.0] * n
-    free = {e: 0.0 for e in "vapqs"}
-    wire = [0.0, 0.0, 0.0, ""]
-    pool = [k for k in range(n) if left[k] == 0]
-    order = []
-    while pool:
-        j = min(pool, key=lambda x: max(lim[x], free[ops[x]["eng"]]) + cost[x][0])
-        e = ops[j]["eng"]
-        first = max(lim[j], free[e]) + cost[j][0]
-        k = min((x for x in pool if ops[x]["eng"] == e and (x == j or lim[x] < first)), key=key)
-        pool.remove(k)
-        order.append(k)
-        free[e], end = step(ops[k], e, ops[k]["kind"], max(lim[k], free[e]), cost[k], m, wire)
-        for x in succ[k]:
-            if k in ops[x]["key"][2]:
-                lim[x] = max(lim[x], end + m[8])
-            left[x] -= 1
-            if left[x] == 0:
-                pool.append(x)
-    return order
-
-
-def schedule(ops):
-    n = len(ops)
-    for o in ops:
-        o["key"] = (o["eng"], o["kind"], [j for j in o["dep"] if o["eng"] != "p" or ops[j]["eng"] != "p"])
-    cost = [costs(ops, m) for m in MODELS]
-    succ = [[] for _ in range(n)]
-    for k, o in enumerate(ops):
-        for j in o["pre"]:
-            succ[j].append(k)
-    tail = [0.0] * n
-    for k in range(n - 1, -1, -1):
-        tail[k] = sum(cost[0][k]) + (0.0 if ops[k]["kind"] == "c" else 2000.0) + max([0.0] + [tail[x] + MODELS[0][8] for x in succ[k]])
-    seed = [SEED]
-
-    def rnd():
-        seed[0] = (seed[0] * 1103515245 + 12345) % 2147483648
-        return seed[0] / 2147483648.0
-
-    base = [replay(ops, range(n), c, m)[0] for c, m in zip(cost, MODELS)]
-    score = lambda od: sum(replay(ops, od, c, m)[0] / b_ for c, m, b_ in zip(cost, MODELS, base))
-    starts = []
-    for it in range(STARTS):
-        w = 2000.0 * (it % 4)
-        urge = [w * ops[k]["pri"] - tail[k] * (1.0 + NOISE * rnd() * (it >= 4)) for k in range(n)]
-        order = listed(ops, succ, cost[0], MODELS[0], lambda x: urge[x])
-        starts.append((score(order), order))
-    cur, order = min(starts)
-    base = [b_ * cur / len(MODELS) for b_ in base]
-    cur = best = score(order)
-    best_order = order
-    why = [0] * n
-    for it in range(ITERS):
-        i = int(rnd() * len(MODELS))
-        k = replay(ops, order, cost[i], MODELS[i], why)[1]
-        pairs = []
-        while k != -1:
-            w = why[k]
-            if w >= 0 and w not in ops[k]["pre"]:
-                pairs.append((w, k))
-            k = w if w >= -1 else -2 - w
-        if not pairs:
-            continue
-        j, k = pairs[int(rnd() * len(pairs))]
-        seg = order[order.index(j):order.index(k) + 1]
-        if rnd() < 0.5:
-            take = {k}
-            for x in reversed(seg[:-1]):
-                if any(y in take for y in succ[x]):
-                    take.add(x)
-            if j in take:
-                continue
-            new = [x for x in seg if x in take] + [x for x in seg if x not in take]
-        else:
-            take = {j}
-            for x in seg[1:]:
-                if any(y in take for y in ops[x]["pre"]):
-                    take.add(x)
-            if k in take:
-                continue
-            new = [x for x in seg if x not in take] + [x for x in seg if x in take]
-        p0 = order.index(j)
-        cand = order[:p0] + new + order[p0 + len(seg):]
-        val = score(cand)
-        if val < cur + TEMP * (1.0 - it / ITERS) * rnd():
-            order, cur = cand, val
-            if val < best:
-                best, best_order = val, cand
-    return best_order
 
 
 def book(busy, t, lat):
@@ -648,148 +578,140 @@ def book(busy, t, lat):
     return t + lat
 
 
-def step(o, e, kind, t, cost, m, wire):
-    occ, lat = cost
+def move(o, t, occ, lat, m, wire):
     t += occ
-    if kind == "c":
-        return t, t + lat
-    if e == "q" and kind not in wire[3]:
-        wire[3] += kind
+    if o["eng"] == "q" and o["kind"] not in wire[3]:
+        wire[3] += o["kind"]
         t += m[9]
-    if kind == "d":
+    if o["kind"] == "d":
         return t, max(book(wire[0], t, lat), book(wire[1], t, lat)) + 2000.0
     if len(o["k"]) == 2:
         return t, book(wire[0], t, lat) + m[4] - m[6]
     return t, book(wire[2], book(wire[1], t, 0.6 * lat) + m[4], lat) + m[4] - m[6]
 
 
-def replay(ops, order, cost, m, why=None, ends=None):
-    hop = m[8]
-    free = {"v": 0.0, "a": 0.0, "p": 0.0, "q": 0.0, "s": 0.0}
-    prev, wire = {}, [[], [], [], ""]
-    end = [0.0] * len(ops) if ends is None else ends
-    for k in order:
-        e, kind, dep = ops[k]["key"]
-        t, w = free[e], prev.get(e, -1)
-        for j in dep:
-            if end[j] + hop > t:
-                t, w = end[j] + hop, -2 - j
-        if kind == "c":
-            t += cost[k][0]
-            free[e] = t
-            t += cost[k][1]
-        else:
-            free[e], t = step(ops[k], e, kind, t, cost[k], m, wire)
-        prev[e], end[k] = k, t
-        if why is not None:
-            why[k] = w
-    last = max(end)
-    return last, end.index(last), sum(end) / len(end)
+QUEUES = "vapqsl"
 
 
-def listed(ops, pre, succ, hard, cost, m, urge, back=False):
+def listed(ops, succ, cost, m):
     n = len(ops)
-    left = [len(x) for x in pre]
+    left = [len(o["pre"]) for o in ops]
     lim = [0.0] * n
-    free = {e: 0.0 for e in "vapqs"}
+    free = {e: 0.0 for e in QUEUES}
     wire = [[], [], [], ""]
     pool = [k for k in range(n) if left[k] == 0]
-    order, at = [], [0.0] * n
+    order = []
     while pool:
-        j = min(pool, key=lambda x: max(lim[x], free[ops[x]["eng"]]) + cost[x][0])
+        j = min(pool, key=lambda x: max(lim[x], free[ops[x]["eng"]]))
         e = ops[j]["eng"]
-        first = max(lim[j], free[e]) + cost[j][0]
-        k = min((x for x in pool if ops[x]["eng"] == e and (x == j or lim[x] < first)), key=lambda x: urge[x])
+        first = max(lim[j], free[e]) + min(LOOK, cost[j][0])
+        k = min((x for x in pool if ops[x]["eng"] == e and (x == j or lim[x] < first)), key=lambda x: (ops[x]["pri"], x))
         pool.remove(k)
         order.append(k)
-        if back:
-            free[e] = end = max(lim[k], free[e]) + cost[k][0]
+        t = max(lim[k], free[e])
+        if ops[k]["kind"] in "dr":
+            free[e], end = move(ops[k], t, cost[k][0], cost[k][1], m, wire)
         else:
-            free[e], end = step(ops[k], e, ops[k]["kind"], max(lim[k], free[e]), cost[k], m, wire)
-        at[k] = free[e]
+            free[e], end = t + cost[k][0], t + sum(cost[k])
         for x in succ[k]:
-            if (x, k) in hard:
-                lim[x] = max(lim[x], end + m[8] + (cost[x][1] if back else 0.0))
+            if k in ops[x]["dep"]:
+                lim[x] = max(lim[x], end + m[8])
             left[x] -= 1
             if left[x] == 0:
                 pool.append(x)
-    return order, at
+    return order
+
+
+def replay(ops, info, m, od, p, mark, end, keep=None, why=None):
+    free, wire, prev = mark[0][:], [mark[1][:], mark[2][:], mark[3][:], mark[4]], mark[5][:]
+    for q in range(p, len(od)):
+        k = od[q]
+        e, d, occ, lat, plain = info[k]
+        t = free[e]
+        if keep is None:
+            for j in d:
+                if end[j] > t:
+                    t = end[j]
+        else:
+            if q % GAP == 0:
+                keep[q // GAP] = (free[:], wire[0][:], wire[1][:], wire[2][:], wire[3], prev[:])
+            why[k] = prev[e]
+            prev[e] = k
+            for j in d:
+                if end[j] > t:
+                    t, why[k] = end[j], -2 - j
+        if plain:
+            t += occ
+            free[e] = t
+            end[k] = t + lat
+        else:
+            free[e], t = move(ops[k], t, occ, lat - m[8], m, wire)
+            end[k] = t + m[8]
+    return max(end) + SOFT * sum(end) / len(end) + HURRY * sum([end[k] for k in info[-1]])
+
+
+def tables(ops):
+    above, dep = [0] * len(ops), []
+    for k, o in enumerate(ops):
+        seen = 0
+        for j in o["dep"]:
+            seen |= above[j]
+        dep.append(tuple(j for j in o["dep"] if not seen >> j & 1))
+        if o["eng"] != "l":
+            above[k] = seen | sum(1 << j for j in o["dep"] if not seen >> j & 1)
+    sends = [k for k, o in enumerate(ops) if o["kind"] == "r" and len(o["k"]) == 2]
+    return [[(QUEUES.index(o["eng"]), d, c[0], c[1] + m[8], o["kind"] not in "dr") for o, d, c in zip(ops, dep, costs(ops, m))] + [sends] for m in MODELS]
+
+
+START = ([0.0] * 5 + [-1e9], [], [], [], "", [-1] * 6)
 
 
 def schedule(ops):
-    n = len(ops)
-    for o in ops:
-        o["key"] = (o["eng"], o["kind"], [j for j in o["dep"] if o["eng"] != "p" or ops[j]["eng"] != "p"])
-    cost = [costs(ops, m) for m in MODELS]
+    n, nm = len(ops), len(MODELS)
     pre = [o["pre"] for o in ops]
     succ = [[] for _ in range(n)]
-    for k, o in enumerate(ops):
-        for j in o["pre"]:
+    for k in range(n):
+        for j in pre[k]:
             succ[j].append(k)
-    hard = set((k, j) for k in range(n) for j in ops[k]["key"][2])
-    drah = set((j, k) for k, j in hard)
+    order = listed(ops, succ, costs(ops, MODELS[0]), MODELS[0])
+    info = tables(ops)
     seed = [SEED]
 
     def rnd():
         seed[0] = (seed[0] * 1103515245 + 12345) % 2147483648
         return seed[0] / 2147483648.0
 
-    base = [replay(ops, range(n), c, m)[0] for c, m in zip(cost, MODELS)]
-
-    def score(od):
-        s = 0.0
-        for c, m, b_ in zip(cost, MODELS, base):
-            r = replay(ops, od, c, m)
-            s += (r[0] + SOFT * r[2]) / b_
-        return s
-
-    m0, c0 = MODELS[0], cost[0]
-    starts = []
-    for it in range(STARTS):
-        tail = [0.0] * n
-        for k in range(n - 1, -1, -1):
-            tail[k] = sum(c0[k]) * (1 + NOISE * rnd()) + (0.0 if ops[k]["kind"] == "c" else 2000.0) + max([0.0] + [tail[x] + m0[8] for x in succ[k]])
-        urge = [-x for x in tail]
-        for r in range(ROUNDS):
-            order, at = listed(ops, pre, succ, hard, c0, m0, urge)
-            starts.append((score(order), order))
-            ends = [0.0] * n
-            replay(ops, order, c0, m0, None, ends)
-            cb = [(c0[k][0], ends[k] - at[k]) for k in range(n)]
-            urge = [-x for x in listed(ops, succ, pre, drah, cb, m0, [-x for x in at], True)[1]]
-    cur, order = min(starts)
-    base = [b_ * cur / len(MODELS) for b_ in base]
-    cur = best = score(order)
-    best_order, moved, pairs = order, True, []
-    why = [0] * n
+    keeps = [[None] * (n // GAP + 1) for _ in range(nm)]
+    ends = [[0.0] * n for _ in range(nm)]
+    whys = [[0] * n for _ in range(nm)]
+    base = [replay(ops, info[i], MODELS[i], order, 0, START, ends[i], keeps[i], whys[i]) for i in range(nm)]
+    cur = [1.0] * nm
+    best, best_order, pairs, fresh = float(nm), order, [], True
     for it in range(ITERS):
-        if it % 8 == 0 or moved:
-            i = int(rnd() * len(MODELS))
-            k = replay(ops, order, cost[i], MODELS[i], why)[1]
-            pairs = []
+        if fresh or it % 16 == 0:
+            i = int(rnd() * nm)
+            k, pairs, fresh = ends[i].index(max(ends[i])), [], False
             while k != -1:
-                w = why[k]
+                w = whys[i][k]
                 if w >= 0 and w not in pre[k]:
                     pairs.append((w, k))
                 k = w if w >= -1 else -2 - w
-        moved = False
-        if pairs and rnd() < 0.7:
+        if pairs and rnd() < CRIT:
             j, k = pairs[int(rnd() * len(pairs))]
             p0, p1 = order.index(j), order.index(k)
         else:
             p0 = int(rnd() * (n - 1))
             j = order[p0]
-            p1 = p0 + 1
-            while p1 < n and ops[order[p1]]["eng"] != ops[j]["eng"]:
-                p1 += 1
-            if p1 == n:
+            later = [q for q in range(p0 + 1, min(n, p0 + 60)) if ops[order[q]]["eng"] == ops[j]["eng"]][:1 + int(rnd() * 3)]
+            if not later:
                 continue
+            p1 = later[-1]
             k = order[p1]
         seg = order[p0:p1 + 1]
         if rnd() < 0.5:
             take = {k}
             for x in reversed(seg[:-1]):
-                if any(y in take for y in succ[x]):
+                if not take.isdisjoint(succ[x]):
                     take.add(x)
             if j in take:
                 continue
@@ -797,17 +719,22 @@ def schedule(ops):
         else:
             take = {j}
             for x in seg[1:]:
-                if any(y in take for y in pre[x]):
+                if not take.isdisjoint(pre[x]):
                     take.add(x)
             if k in take:
                 continue
             new = [x for x in seg if x not in take] + [x for x in seg if x in take]
         cand = order[:p0] + new + order[p1 + 1:]
-        val = score(cand)
-        if val < cur + TEMP * (1.0 - it / ITERS) * rnd():
-            order, cur, moved = cand, val, True
-            if val < best:
-                best, best_order = val, cand
+        room, b, up = TEMP * (1.0 - it / ITERS) * rnd(), p0 // GAP, 0.0
+        for i in range(nm):
+            up += replay(ops, info[i], MODELS[i], cand, b * GAP, keeps[i][b], ends[i][:]) / base[i] - cur[i]
+            if up > (room if i == nm - 1 else 0.7 * room + 0.001):
+                break
+        else:
+            order, fresh = cand, True
+            cur = [replay(ops, info[i], MODELS[i], order, b * GAP, keeps[i][b], ends[i], keeps[i], whys[i]) / base[i] for i in range(nm)]
+            if sum(cur) < best:
+                best, best_order = sum(cur), order
     return best_order
 
 
@@ -822,11 +749,10 @@ def hand_on(g, core, T, topo):
         if core not in hs:
             continue
         rid, pid, _ = topo.addr(dst)
-        came = len([e for e in topo.engines(owner, core) if e not in topo.engines(owner, dst)])
         sent = 0
         for k, piece in enumerate(landing(T)):
             if hs[k % len(hs)] == core:
-                g.wait_ge(T.sem["r%d" % k], came)
+                g.wait_ge(T.sem["r%d" % k], len(inward(owner, core, dst, k, topo)))
                 g.remote_dma(piece, piece, T.sem["r%d" % k], T.sem.loc, pid, rid, topo.mask(core, dst))
                 sent += len(topo.engines(core, dst))
         g.wait_ge(T.sem.loc, sent)
@@ -848,10 +774,12 @@ def rank_program(g, core, T, topo):
     for k in ORDER["order"]:
         o = ops[k]
         e = o["eng"]
+        if e == "l":
+            done[k] = o["sem"]
+            total[done[k][0]] = done[k][1]
+            continue
         need = {}
         for j in o["dep"]:
-            if e == "p" and ops[j]["eng"] == "p":
-                continue
             s, val = done[j]
             need[s] = max(need.get(s, 0), val)
         for s, val in need.items():

from concourse.mybir import AluOpType as A, ActivationFunctionType as F

NS = [16, 16, 16]
CO = [1, 0, 2]
PLANS = {
    "5a": ([(6, 10, 1), (0, 16, 5)], [((1, 5, 1), "L", 0), ((11, 15, 1), "R", 0)], [(1, 0, 1, 1, 3)]),
    "5b": ([(5, 10, 1), (10, 16, 5)], [((0, 5, 1), "L", 0), ((10, 15, 1), "R", 0)], [(1, 0, 1, 1, 1)]),
    "5c": ([(5, 10, 1), (15, 16, 1)], [((10, 11, 1), "L", 1), ((0, 5, 1), "L", 0), ((10, 15, 1), "R", 0)], []),
    "4a": ([(4, 8, 1), (7, 11, 1)], [((0, 4, 1), "L", 0), ((11, 15, 1), "R", 1)], [(0, 0, 1, 1, 3)]),
    "4b": ([(4, 8, 1), (12, 15, 1)], [((8, 11, 1), "L", 1), ((0, 4, 1), "L", 0), ((8, 12, 1), "R", 0)], []),
    "3a": ([(3, 7, 1), (7, 11, 1)], [((0, 4, 1), "L", 0), ((10, 14, 1), "R", 1)], [(0, 1, 1, 0, 3)]),
    "3d": ([(3, 6, 1), (9, 12, 1)], [((0, 3, 1), "L", 0), ((6, 9, 1), "R", 0), ((6, 9, 1), "L", 1), ((12, 15, 1), "R", 1)], []),
    "3b": ([(3, 7, 1), (7, 11, 1), (10, 14, 1)], [((0, 4, 1), "L", 0)], [(0, 1, 1, 0, 3), (1, 0, 2, 0, 4)]),
}
PLAN = [["5c", "5c", "5c"], ["4a", "4b", "4b"], ["3a", "3a", "3a"]]
ONA = {"an", "rq", "tab", "tx", "yo", "li", "hi", "ht", "s0", "st0", "st2"}
EARLY = 2
GATE = (0, [], [])
OWNT = False
PA = 900
PV = 900
VMIN = 64
LOOK = 51.0
AT = {'lag': -2.58, 'sign': -2.15, 'thr': 1.42, 'su': -4.52, 'rq': -2.34, 'sT': 31.17, 'sm': -1.2, 'an': 2.68, 'up': -3.25, 'back': 0.85, 'dedup0': 8.23, 'dedup1': 3.03, 'dedup2': -11.02, 'scat0': -0.33, 'scat1': -3.7, 'fin': 13.52, 'tab': -4.39, 'mir0': 2.79, 'mir1': -9.61, 'kept': 2.67, 'tabs': 10.88, 'relay': -2.43, 'sc': 2.34, 'vote': -4.62, 'fin2': -5.91, 'st': 13.7}
SEED = 212
ITERS = 165000
HURRY = 0.01
TEMP, SOFT, CRIT, GAP = 0.0035, 0.1, 0.7, 24
MODELS = [(0.95, 1.4, 3.2, 0.48, 2100, 85.0, 550, 370.0, 90, 1600), (0.85, 1.25, 2.5, 0.43, 2700, 55.0, 750, 330.0, 120, 2200),
          (1.15, 1.25, 4.0, 0.6, 1800, 100.0, 450, 400.0, 80, 1400), (1.1, 1.9, 5.0, 0.55, 2300, 70.0, 600, 300.0, 110, 1800)]
NC = len(NS)
C0 = [sum(NS[:c]) for c in range(NC)]
WM = 16 * max(NS)
SPARE, EXO, TABW, PAD = 2048, 2176, 4224, 512
LIFT, DROP = 3072.0, 8192.0
PIECES = [("e", 0), ("i", 0), ("i", 1), ("e", 1), ("e", 2), ("e", 3)]


def plan(t, c):
    return PLANS[PLAN[t][CO.index(c)]]


def size(x):
    return len(range(*x))


def _sb(n, dtype):
    return ("sbuf", [128, n], dtype)


SCRATCH = {
    "pic_s": _sb(9216, "bfloat16"), "shp_s": _sb(768, "int32"), "ex_s": _sb(2048, "int32"), "inc_s": _sb(2048, "bfloat16"),
    "tab": _sb(TABW, "float32"), "pft": _sb(TABW, "float32"), "pfi": _sb(2048, "bfloat16"),
    "ofs_s": _sb(4, "int32"), "thr_s": _sb(4, "int32"), "thf": _sb(4, "float32"), "thc": _sb(4, "float32"), "oc": _sb(4, "float32"),
    "ci": _sb(4, "int32"), "cl": _sb(8, "float32"), "cf": _sb(160, "bfloat16"), "iI": _sb(WM, "bfloat16"), "iG": _sb(128, "bfloat16"),
    "iC": _sb(WM, "bfloat16"), "wh": _sb(2048, "float16"), "drop": _sb(128, "float16"), "nd": _sb(128, "float16"),
    "r16e": _sb(160, "float16"), "r16o": _sb(160, "float16"), "r32e": _sb(160, "float32"), "r32o": _sb(160, "float32"),
    "bo": _sb(128, "float16"), "i32": _sb(128, "float32"), "i16": _sb(128, "float16"), "exo": _sb(128, "float16"), "rep": _sb(128, "float32"), "rt": _sb(3 * WM, "float16"),
    "ub": _sb(144, "bfloat16"), "uh": _sb(144, "bfloat16"), "w2": _sb(14 * 128, "bfloat16"),
    "exa": _sb(WM, "bfloat16"), "exb": _sb(WM, "bfloat16"), "exc": _sb(WM, "bfloat16"), "ones": _sb(WM, "bfloat16"),
    "tri": _sb(128, "bfloat16"), "s16": _sb(768, "float16"),
    "rq_o": _sb(144, "uint16"), "rq_i": _sb(144, "uint16"), "an_o": _sb(1536, "float16"), "an_i": _sb(1536, "float16"),
    "xi": _sb(768, "int32"), "zz": _sb(768, "float32"), "yo": _sb(768, "float32"),
    "hf": _sb(8, "float16"), "hg": _sb(8, "float32"), "tl": _sb(16, "uint16"), "tx": _sb(32, "uint16"),
    "eq": _sb(128, "bfloat16"), "sc": _sb(128, "bfloat16"), "hi": _sb(432, "int32"), "hx": _sb(288, "int32"),
}
for _k in ("ps", "pv0", "pv1", "pd0", "pd1")[:8 - NC]:
    SCRATCH[_k] = ("psum", [128, 8, 4, 16] if _k[1] == "d" else [128, 512], "float32")
NPD = 5 - NC
for _c in range(NC):
    _n = NS[_c]
    SCRATCH["px%d" % _c] = ("psum", [128, 32, 16], "float32")
    SCRATCH["x0%d" % _c] = ("sbuf", [128, _n, 16], "int32")
    SCRATCH["tp%d" % _c] = ("sbuf", [128, _n, 16], "float32")
    SCRATCH["li%d" % _c] = _sb(20 * _n, "uint16")
    SCRATCH["cc%d" % _c] = _sb(12 * 16 * _n, "bfloat16")
    SCRATCH["bb%d" % _c] = _sb(3 * 12 * _n, "bfloat16")
    SCRATCH["su%d" % _c] = _sb(_n, "float16")
    SCRATCH["sT%d" % _c] = _sb(256, "bfloat16")
    SCRATCH["st%d" % _c] = _sb(16 * _n, "float16")
    for _t in range(2):
        SCRATCH["sm%d_%d" % (_t, _c)] = _sb(16 * _n, ("float16", "float32")[_t])
        if OWNT:
            SCRATCH["oT%d_%d" % (_t, _c)] = ("sbuf", [128, _n, 16], "float16")
    for _t in range(3):
        SCRATCH["aT%d_%d" % (_t, _c)] = ("sbuf", [128, _n, 16], "float16")
        for _s, _r in enumerate(plan(_t, _c)[0]):
            SCRATCH["mm%d_%d_%d" % (_t, _c, _s)] = _sb(_n * 16 * size(_r), "bfloat16")
SEMAPHORES = ["v", "a", "p", "q", "loc"] + ["d%d" % k for k in range(24)] + ["r%d" % k for k in range(4 * NC + 9)]


def pieces(n, k, most):
    m = -(-(16 * n * k) // most)
    cut = [2 * ((n // 2) * j // m) for j in range(m + 1)]
    return [(a, b) for a, b in zip(cut, cut[1:]) if b > a]


def relays(core, T, topo):
    dst = T.cores[(T.rank_of(core) - 3) % len(T.cores)]
    return dst, [h for h in topo.cores_of(core) if T.rank_of(h) is None and topo.die(h) != topo.die(core) and topo.may_write(h, dst)]


def inward(core, h, dst, k, topo):
    return [e for e in topo.engines(core, h) if k == 0 or e not in topo.engines(core, dst)]


def landing(T):
    return [T.pfi[:, 1024 * j:1024 * j + 1024] if what == "i" else T.pft[:, EXO + 512 * j:EXO + 512 * j + 512] for what, j in PIECES]


def build(g, core, T, topo):
    rank = T.rank_of(core)
    N = len(T.cores)
    V, S_, P = g.vector, g.scalar, g.tensor
    ops = []
    cnt = {"pd": 0, "pv": 0, "h": 0, "r": len(PIECES), "wh": 0}
    pri = [-1.0]

    def add(eng, n, fns, r, w, banks=(), k=1.0, kind="c", sem=None, after=()):
        ops.append({"pri": pri[0], "eng": eng, "n": n, "k": k, "fns": fns, "r": list(r), "w": list(w), "banks": list(banks),
                    "kind": kind, "sem": sem, "after": list(after)})

    def dve(n, fn, r, w, banks=(), k=1.0):
        add("v", n, [fn], r, w, banks, k)

    def act(n, fn, r, w, banks=(), k=1.0):
        add("a", n, [fn], r, w, banks, k)

    def shift(tag, n, out, in_, c, r, w, banks=(), k=1.0, times=1.0):
        if tag in ONA or tag.rstrip("0123456789") in ONA:
            act(n, lambda: S_.activation(out, in_, F.Identity, bias=c, scale=times), r, w, banks, k)
        else:
            dve(n, lambda: V.tensor_scalar(out, in_, times, c, A.mult, A.add), r, w, banks, k)

    def pe(cyc, fns, r, w, banks):
        add("p", cyc, fns, r, w, banks)

    def dma(q, out, in_, nbytes, r, w, after=()):
        Q = {"s": g.sync, "a": S_, "q": g}[q]
        add(q, nbytes, [lambda: Q.dma_start(out, in_)], r, w, kind="d", after=after)

    def send(dst_rank, out, in_, nbytes, r, w, relay=False, left=None):
        dst = T.cores[dst_rank % N]
        k = cnt["h" if relay else "r"]
        cnt["h" if relay else "r"] += 1
        eng = topo.engines(core, dst)
        arrive = len(eng)
        if relay:
            hs = relays(core, T, topo)[1]
            h = hs[k % len(hs)]
            eng, arrive, dst = inward(core, h, dst, k, topo), len(topo.engines(h, dst)), h
        rid, pid, _ = topo.addr(dst)
        add("q", nbytes, [lambda: g.remote_dma(out, in_, T.sem["r%d" % k], T.sem[left or "loc"], pid, rid, sum(1 << e for e in eng))],
            r, w + [("h", k)], k=(2,) if relay else (0, 1), kind="r", sem=("r%d" % k, arrive, 0 if left else len(eng)),
            after=[("h", k - 1)] if relay and k else [])
        if left:
            add("l", 0, [], [("h", k)], [left], kind="l", sem=(left, len(eng)))

    def iota(out, pat, base, cm, n, key):
        add("q", n, [lambda: g.iota(out, pat, base, cm, allow_small_or_imprecise_dtypes=True)], [], [key])

    W2 = [T.w2[:, 128 * m:128 * (m + 1)] for m in range(14)]
    col = [T.cl[:, k:k + 1] for k in range(6)]
    main = T.pic_s[:, PAD:PAD + 4096]

    def marks(c, after):
        f0, W = 16 * C0[c], 16 * NS[c]
        dma("s", T.shp_s[:, f0:f0 + W], T.shp[:, f0:f0 + W], 512 * W, [], [("shp", c)], after)

    for k, c in enumerate(CO[:EARLY]):
        marks(c, [("shp", x) for x in CO[:k]])
    dma("a", T.ofs_s[:, 0:3], T.ofs[:], 1536, [], ["ofs"])
    dma("s", main, T.pic[:], 1 << 20, [], ["pic"], [("shp", x) for x in CO[:EARLY]])
    for k, c in enumerate(CO[EARLY:]):
        marks(c, ["pic"] + [("shp", x) for x in CO[:EARLY + k]])
    dma("a", T.thr_s[0:8, 0:3], T.thr[:], 96, [], ["thr"], ["ofs"])
    dma("s", T.ex_s[:, 0:1024], T.ex[:, 0:1024], 1 << 19, [], [("ex", 0)], ["pic", ("shp", CO[-1])])
    dma("s", T.ex_s[:, 1024:2048], T.ex[:, 1024:2048], 1 << 19, [], [("ex", 1)], [("ex", 0)])

    add("q", 4, [lambda: g.iota(T.ci[:], [[0, 4]], 0, 1)], [], ["ci"])
    iota(T.cf[:], [[1, 160]], -16, 0, 160, "cf")
    iota(T.iI[:], [[0, WM // 16], [1, 16]], 0, 0, WM, "iI")
    iota(T.iG[:], [[16, 8], [0, 16]], 0, 0, 128, "iG")
    iota(T.iC[:], [[1, WM // 16], [0, 16]], 0, 0, WM, "iC")
    dma("q", T.tab[:, 0:2048], T.inc[:], 1 << 20, [("shp", CO[EARLY - 1])], ["tabI"], ["ci", "cf", "iI", "iG", "iC"])
    dma("s", T.inc_s[:], T.inc[:], 1 << 19, [("ex", GATE[0])], ["inc_s"], [("ex", 1)])
    dma("s", T.pic_s[:, PAD + 4096:PAD + 6144], T.pic[:, 0:2048], 1 << 19, GATE[1], ["picx1"], ["inc_s"])
    dma("s", T.pic_s[:, PAD + 6144:PAD + 8192], T.pic[:, 2048:4096], 1 << 19, GATE[2], ["picx3"], ["picx1"])
    dma("s", T.pic_s[:, 0:PAD], T.pic[:, 4096 - PAD:4096], 1 << 17, [], ["picx0"], ["picx3"])
    dma("s", T.pic_s[:, PAD + 8192:9216], T.pic[:, 0:PAD], 1 << 17, [], ["picx2"], ["picx0"])
    dve(1, lambda: V.tensor_scalar(T.ci[:, 1:2], T.ci[:, 0:1], 15, None, A.bitwise_and), ["ci"], ["ci1"])
    dve(1, lambda: V.tensor_scalar(T.ci[:, 2:3], T.ci[:, 0:1], 112, None, A.bitwise_and), ["ci"], ["ci2"])
    dve(1, lambda: V.tensor_scalar(T.ci[:, 3:4], T.ci[:, 0:1], 4, 1, A.arith_shift_right, A.bitwise_and), ["ci"], ["ci3"])
    dve(1, lambda: V.tensor_copy(T.cl[:, 0:4], T.ci[:]), ["ci", "ci1", "ci2", "ci3"], ["cl"])
    act(1, lambda: S_.activation(col[4], col[3], F.Identity, bias=1.0, scale=-1.0), ["cl"], ["cl4"])
    act(1, lambda: S_.activation(col[5], col[1], F.Identity, bias=SPARE - EXO / 2), ["cl"], ["cl5"])
    for buf, cc_, key in ((T.r16e, 4, "r16e"), (T.r16o, 3, "r16o")):
        dve(160, lambda buf=buf, cc_=cc_: V.tensor_scalar(buf[:], T.cf[:], col[0], col[cc_], A.is_equal, A.mult), ["cf", "cl", "cl4"], [key], k=0.5)
    dve(128, lambda: V.tensor_scalar(T.bo[:], T.iG[:], col[2], None, A.is_equal), ["iG", "cl"], ["bo"], k=0.5)
    dve(1, lambda: V.tensor_scalar(T.oc[:, 0:3], T.ofs_s[:, 0:3], -2048.0, None, A.add), ["ofs"], ["oc"])
    dve(WM, lambda: V.tensor_scalar(T.rt[:, 0:WM], T.iI[:], col[1], T.oc[:, 0:1], A.is_equal, A.mult), ["iI", "cl", "oc"], [("rt", 0)], k=0.5)
    dve(128, lambda: V.tensor_scalar(W2[1], T.cf[:, 16:144], col[0], None, A.is_equal), ["cf", "cl"], [("w2", 1)], k=0.5)
    act(WM, lambda: S_.activation(T.ones[:], T.iI[:], F.Identity, bias=1.0, scale=0.0), ["iI"], ["ones"])
    pri[0] = -0.5
    for m in (13, 11, 4, 0, 2, 3, 5, 6, 7, 8, 9, 10):
        sc = -1.0 if m == 11 else LIFT if m == 13 else 2.0 ** (m - 1)
        act(128, lambda m=m, sc=sc: S_.activation(W2[m], W2[1], F.Identity, scale=sc), [("w2", 1)], [("w2", m)])
    pri[0] = -0.4
    dve(143, lambda: V.tensor_scalar(T.ub[:, 0:143], T.cf[:, 1:144], col[2], None, A.is_equal), ["cf", "cl"], ["ub"], k=0.5)
    act(143, lambda: S_.activation(T.uh[:, 0:143], T.ub[:, 0:143], F.Identity, scale=0.5), ["ub"], ["uh"])
    act(128, lambda: S_.activation(T.i32[:], W2[1], F.Identity), [("w2", 1)], ["i32"])
    for t in (1, 2):
        dve(WM, lambda t=t: V.tensor_scalar(T.rt[:, WM * t:WM * t + WM], T.iI[:], col[1], T.oc[:, t:t + 1], A.is_equal, A.mult),
            ["iI", "cl", "oc"], [("rt", t)], k=0.5)
    dve(WM, lambda: V.tensor_scalar(T.exa[:], T.iC[:], col[0], -DROP, A.is_equal, A.mult), ["iC", "cl"], ["exa"], k=0.5)
    act(WM, lambda: S_.activation(T.exb[:], T.exa[:], F.Identity, scale=-LIFT / DROP), ["exa"], ["exb"])
    act(WM, lambda: S_.activation(T.exc[:], T.exa[:], F.Identity, scale=-1.0 / DROP), ["exa"], ["exc"])
    act(128, lambda: S_.activation(T.exo[:], W2[1], F.Identity, scale=-EXO / 2.0), [("w2", 1)], ["exo"])
    act(128, lambda: S_.activation(T.i16[:], W2[1], F.Identity), [("w2", 1)], ["i16"])
    act(128, lambda: S_.activation(T.tab[:, SPARE:EXO], T.iG[:], F.Identity, scale=0.0), ["iG"], ["tabD"])
    act(128, lambda: S_.activation(T.pft[:, SPARE:EXO], T.iG[:], F.Identity, scale=0.0), ["iG"], ["pfD"])
    act(128, lambda: S_.activation(T.drop[:], T.iG[:], F.Identity, bias=DROP, scale=0.0), ["iG"], ["drop"])
    for k, (e16, e32) in enumerate(((T.r16e, T.r32e), (T.r16o, T.r32o))):
        act(160, lambda e16=e16, e32=e32: S_.activation(e32[:], e16[:], F.Identity), ["r16e", "r16o"], [("r32", k)])
    dve(128, lambda: V.tensor_scalar(T.tri[:], T.iI[:, 0:128], col[1], None, A.is_gt), ["iI", "cl"], ["tri"], k=0.5)
    act(8, lambda: S_.activation(T.tri[:, 15:128:16], T.tri[:, 15:128:16], F.Identity, scale=4096.0), ["tri"], ["tri"])
    act(128, lambda: S_.activation(T.nd[:], W2[1], F.Identity, scale=-DROP), [("w2", 1)], ["nd"])
    act(1, lambda: S_.activation(T.oc[:, 3:4], T.oc[:, 2:3], F.Identity, bias=6144.0 - 2 * LIFT - DROP, scale=-1.0), ["oc"], ["oc3"])
    dve(128, lambda: V.tensor_scalar(T.rep[0:8, :], T.iG[0:8, :], 0.0625, T.cl[0:8, 0:1], A.mult, A.is_equal), ["iG", "cl"], ["rep"])
    dve(1, lambda: V.tensor_scalar(T.thf[0:8, 0:3], T.thr_s[0:8, 0:3], -2.0, 11.5, A.mult, A.add), ["thr"], ["thf"])
    pe(256, [lambda: P.matmul(T.ps[:, 0:3], T.rep[0:8, :], T.thf[0:8, 0:3], True, True)], ["rep", "thf"], ["ps"], ["ps"])
    act(1, lambda: S_.activation(T.thc[:, 0:3], T.ps[:, 0:3], F.Identity), ["ps"], ["thc"], ["ps"])
    for k in range(4):
        pri[0] = AT["tab"] + AT["tabs"] * k
        shift("tab%d" % k, 512, T.tab[:, EXO + 512 * k:EXO + 512 * k + 512], T.ex_s[:, 512 * k:512 * k + 512], -2048.0, [("ex", k // 2)], [("tabE", k)])
    tabk = ["tabI", "tabD"] + [("tabE", k) for k in range(4)]
    land = landing(T)

    def piece(k):
        what, j = PIECES[k]
        pri[0] = AT["relay"] + 0.5 * k
        if what == "e":
            send(rank - 3, land[k], T.tab[:, EXO + 512 * j:EXO + 512 * j + 512], 1 << 18, [("tabE", j)], [("pfe", j)], True)
        else:
            send(rank - 3, land[k], T.inc_s[:, 1024 * j:1024 * j + 1024], 1 << 18, ["inc_s"], [("pfi", j)], True)

    for k in range(len(PIECES)):
        piece(k)

    pri[0] = -0.3
    for h in range(16):
        add("q", 148, [lambda h=h: g.affine_select(T.wh[:, 128 * h:128 * h + 128], T.drop[:], [[-16, 8], [0, 16]], A.is_equal, 0.0, -h, 1)],
            ["drop"], [("wh", h)], after=["tabI"])
    whk = [("wh", h) for h in range(16)]

    def route(c, src, wide, key, stop):
        n, px = NS[c], T["px%d" % c]
        e, o, keys = (T.r32e, T.r32o, [("r32", 0), ("r32", 1)]) if wide else (T.r16e, T.r16o, ["r16e", "r16o"])
        E = [[e[:, 16:144], e[:, 0:128]], [o[:, 32:160], o[:, 16:144]]]
        pe(4 * max(64, 8 * n) * (4 if wide else 1),
           [lambda x=x, y=y: P.matmul(px[:, x:n:2, :], E[x][y], src[:, y:n:2, :], False, stop and x == 1 and y == 1) for x in range(2) for y in range(2)],
           keys + [key, ("px", c)], [("px", c)], ["px%d" % c])

    def kept(t, c, offsets):
        n, W, px = NS[c], 16 * NS[c], T["px%d" % c]
        if offsets:
            fns, cyc, r = [lambda: P.matmul(px[:, 0:n, :], T.bo[:], T.rt[:, WM * t:WM * t + W], True, False)], W, ["bo", ("rt", t)]
        else:
            fns, cyc, r = [lambda: P.matmul(px[:, 0:n, :], W2[13], T.ones[:, 0:W], True, False)], W, [("w2", 13), "ones"]
        if t == 1:
            fns.append(lambda: P.matmul(px[:, 0:n, :], T.i16[:], T["sm0_%d" % c][:], False, False))
            cyc, r = cyc + W, r + ["i16", ("sm", 0, c)]
        if t == 2:
            fns += [lambda: P.matmul(px[:, 0:n, :], T.i32[:], T["sm1_%d" % c][:], False, False),
                    lambda: P.matmul(px[:, 0:n, :], T["sT%d" % c][0:n, 128:256], T.exb[0:n, 0:W], False, False)]
            cyc, r = cyc + 5 * W, r + ["i32", ("sm", 1, c), ("sT", 1, c), "exb"]
        pe(cyc, fns, r, [("px", c)], ["px%d" % c])

    def sets(t, c):
        out = []
        for x in plan(t, c)[0] + [y[0] for y in plan(t, c)[1]]:
            if x not in out:
                out.append(x)
        return out

    def update(t, c):
        n, W, f0 = NS[c], 16 * NS[c], 16 * C0[c]
        aT, px, li, x0, pk = T["aT%d_%d" % (t, c)], T["px%d" % c], T["li%d" % c], T["x0%d" % c], "px%d" % c
        if t == 0:
            shift("s%d" % c, W, T.s16[:, f0:f0 + W], T.shp_s[:, f0:f0 + W], -2048.0, [("shp", c)], [("s16", c)])
            src, key = T.s16[:, f0:f0 + W], ("s16", c)
        else:
            src, key = T.an_i[:, 768 * (t - 1) + f0:768 * (t - 1) + f0 + W], ("an_i", t - 1, c)
        pri[0] -= AT["kept"]
        kept(t, c, True)
        pri[0] += AT["kept"]
        if t == 0 or not OWNT:
            dve(W, lambda: V.transpose(aT[:], src), [key], [("aT", t, c)], k=0.5)
        route(c, aT, False, ("aT", t, c), True)
        if t == 0:
            shift("x%d" % c, W, x0[:], px[:, 0:n, :], 4096.0, [("px", c)], [("x0", c)], [pk])
            dve(W, lambda: V.tensor_scalar(x0[:], x0[:], 4095, None, A.bitwise_and), [("x0", c)], [("x0", c)])
            p0 = pri[0]
            pri[0] = -0.45 if c in CO[:EARLY] else AT["st"]
            kept(t, c, False)
            route(c, aT, False, ("aT", t, c), True)
            shift("st%d" % c, W, T["st%d" % c][:], px[:, 0:n, :], -LIFT, [("px", c)], [("st", c)], [pk])
            pri[0] = p0
        o = 0
        for j, (lo, hi, st) in enumerate(sets(t, c)):
            w = n * size((lo, hi, st))
            if t == 0:
                shift("lz%d" % c, w, li[:, o:o + w], x0[:, :, lo:hi:st], 0.0, [("x0", c)], [("li", c, j)])
            else:
                shift("li%d%d" % (t, j), w, li[:, o:o + w], px[:, 0:n, lo:hi:st], 4096.0 - LIFT * (t - 1) + PAD, [("px", c)], [("li", c, j)], [pk])
            o += w

    def compute(t, c):
        n, W, d = NS[c], 16 * NS[c], 5 - t
        li, cc, bb, su, sT, px = [T["%s%d" % (s, c)] for s in ("li", "cc", "bb", "su", "sT", "px")]
        win, wk = (main, ["pic"]) if t == 0 else (T.pic_s[:, 0:9216], ["pic", "picx0", "picx1", "picx2", "picx3"])
        sr, vr, dr = plan(t, c)
        rs = sets(t, c)
        lo_ = [n * sum(size(x) for x in rs[:j]) for j in range(len(rs))]
        mm = [T["mm%d_%d_%d" % (t, c, s)] for s in range(len(sr))]
        mk = lambda s, a, b: [("mm", t, c, s, x) for x in range(a, b, 2)]
        ck = lambda o, a, b: [("cc", c, o, x) for x in range(a, b, 2)]
        lst = lambda j, k, a, b: li[:, lo_[j] + a * k:lo_[j] + b * k]
        M = lambda s, a, b: mm[s][:, 16 * size(sr[s]) * a:16 * size(sr[s]) * b]
        j0 = pri[0]
        when, acc, tot = {}, 0.0, sum(size(x) for x in sr) * n
        for a, s, b in sorted((a, s, b) for s, x in enumerate(sr) for a, b in pieces(n, size(x), PA)):
            for x in range(a, b, 2):
                when[s, x] = j0 + 0.95 * acc / tot
            acc += size(sr[s]) * (b - a)
        ready = lambda s, a, b: max(when[s, x] for x in range(a, b, 2))
        for s, x in enumerate(sr):
            k = size(x)
            for a, b in pieces(n, k, PA):
                pri[0] = when[s, a]
                act(16 * (b - a) * k, lambda s=s, a=a, b=b, k=k: S_.activation(M(s, a, b), win.indirect(lst(s, k, a, b)), F.Identity),
                    [("li", c, s)] + wk, mk(s, a, b), k="g")
        pv, pvk = T["pv%d" % cnt["pv"]], "pv%d" % cnt["pv"]
        cnt["pv"] ^= 1
        at, vk = {}, []

        def votes(o0, o1, keys, signs):
            u = T.uh if signs else T.ub
            fns = [lambda j=j: P.matmul(pv[:, o0:o1], u[:, 15 - j:143 - j], cc[:, 16 * o0 + j:16 * o1:16], j == 0, j == 15 and not signs)
                   for j in range(16)]
            if signs:
                fns.append(lambda: P.matmul(pv[:, o0:o1], W2[4], T.ones[:, 0:o1 - o0], False, True))
            vk.append((pvk, "v", len(vk)))
            pri[0] += AT["vote"]
            pe(len(fns) * max(64, o1 - o0), fns, keys + ["ub", "uh", ("w2", 4), "ones"], vk[-1:], [pvk])

        o, o0, keys = 0, 0, []
        for x, side, s in vr:
            k, j = size(x), rs.index(x)
            for z, i in enumerate(range(*x)):
                at[i if side == "L" else i - d] = (o + z, o + n * k, k)
            for a, b in pieces(n, k, PV):
                pri[0] = ready(s, a, b) + AT["lag"] + 0.01 * o / n
                dve(16 * (b - a) * k, lambda o=o, a=a, b=b, k=k, j=j, s=s, side=side: V.tensor_tensor(
                    cc[:, 16 * (o + a * k):16 * (o + b * k)], win.indirect(lst(j, k, a, b)), M(s, a, b), A.is_gt if side == "L" else A.is_lt),
                    [("li", c, j)] + wk + mk(s, a, b), ck(o // n, a, b), k="g")
            keys += ck(o // n, 0, n)
            o += n * k
            if o - o0 >= VMIN or (x, side, s) == vr[-1]:
                votes(o0, o, keys, False)
                o0, keys = o, []
        for s0, i0, s1, i1, k in dr:
            for z, i in enumerate(list(range(*sr[s0]))[i0:i0 + k]):
                at[i] = (o + z, o + n * k, k)
            ks = size(sr[s0])
            for a, b in pieces(n, 2 if ks == 2 else 4, 512):
                pri[0] = max(ready(s0, a, b), ready(s1, a, b)) + AT["sign"]
                pd, pk = T["pd%d" % cnt["pd"]], "pd%d" % cnt["pd"]
                cnt["pd"] = (cnt["pd"] + 1) % NPD
                rows = (b - a) // 2 if ks == 2 else b - a
                seen = pd[:, 0:rows, 0:4:2, :] if ks == 2 and k == 1 else pd[:, 0:rows, 0:(4 if ks == 2 else k), :]
                if k == ks:
                    parts = [(seen, M(s0, a, b), M(s1, a, b), 16 * k * (b - a))]
                else:
                    z0, z1, e, e1 = 16 * (ks * a + i0), 16 * (ks * a + i1), 64 * (rows - 1), 4 - ks + k
                    parts = [(pd[:, 0:rows - 1], mm[s0][:, z0:z0 + e], mm[s1][:, z1:z1 + e], e),
                             (pd[:, rows - 1, 0:e1, :], mm[s0][:, z0 + e:z0 + e + 16 * e1], mm[s1][:, z1 + e:z1 + e + 16 * e1], 64)]
                pe(2 * sum(x[3] for x in parts), [lambda x=x, z=z: P.matmul(x[0], W2[(1, 11)[z]], x[1 + z], z == 0, z == 1) for x in parts for z in range(2)],
                   mk(s0, a, b) + mk(s1, a, b) + [("w2", 1), ("w2", 11)], [pk], [pk])
                act(16 * k * (b - a), lambda seen=seen, o=o, a=a, b=b, k=k: S_.activation(cc[:, 16 * (o + a * k):16 * (o + b * k)], seen, F.Sign, bias=-2.0 ** -110),
                    [pk], ck(o // n, a, b), [pk])
            keys += ck(o // n, 0, n)
            o += n * k
        if dr:
            votes(o0, o, keys, True)
        q = o
        pri[0] = j0 + AT["thr"]
        act(q, lambda: S_.activation(bb[:, 2 * q:3 * q], pv[:, 0:q], F.Abs, bias=-7.5), vk, [("bb", c, 2)], [pvk])
        act(q, lambda: S_.activation(bb[:, q:2 * q], bb[:, 2 * q:3 * q], F.Sign, bias=-4.0), [("bb", c, 2)], [("bb", c, 1)])
        act(q, lambda: S_.activation(bb[:, 0:q], pv[:, 0:q], F.Sign, bias=-8.5), vk, [("bb", c, 0)], [pvk])
        B = lambda z, m: bb[:, z + at[m][0]:z + at[m][1]:at[m][2]]
        pe(11 * 64, [lambda m=m: P.matmul(pv[:, 256:256 + n], W2[1], B(q, m), m == 0, m == 10) for m in range(11)],
           [("bb", c, 1), ("w2", 1)], [(pvk, "c")], [pvk])
        pe(11 * 64, [lambda m=m: P.matmul(T.ps[:, 0:n], W2[m], B(0, m), m == 0, False) for m in range(11)],
           [("bb", c, 0)] + [("w2", m) for m in range(11)], ["ps"], ["ps"])
        pri[0] = j0 + AT["su"]
        act(n, lambda: S_.activation(su[:], pv[:, 256:256 + n], F.Sign, bias=T.thc[:, t:t + 1]), [(pvk, "c"), "thc"], [("su", c)], [pvk])
        pe(64, [lambda: P.matmul(T.ps[:, 0:n], T.exo[:], su[:], False, True)], [("su", c), "exo", "ps"], ["ps"], ["ps"])
        r0, c0, pk = 48 * t + C0[c], C0[c], "px%d" % c
        pri[0] = j0 + AT["rq"]
        shift("rq%d" % t, n, T.rq_o[:, r0:r0 + n], T.ps[:, 0:n], 1023.5 + EXO / 2, ["ps"], [("rq_o", t, c)], ["ps"])
        if t == 2:
            pe(16 * 64, [lambda h=h: P.matmul(px[:, 0:n, h], T.wh[:, 128 * h:128 * h + 128], su[:], False, h == 15) for h in range(16)],
               [("su", c), ("px", c)] + whk, [("px", c)], [pk])
            return
        send(rank + 1 + t, T.rq_i[:, r0:r0 + n], T.rq_o[:, r0:r0 + n], 256 * n, [("rq_o", t, c)], [("rq_i", t, c)])
        if t == 1 and c == CO[1]:
            dma("q", T.pft[:, 0:2048], T.pfi[:], 1 << 20, [("pfi", 0), ("pfi", 1)], ["pfI"], [("rq_i", t, c)])
        a0 = 768 * t + 16 * c0
        pri[0] = j0 + AT["an"]
        shift("an%d" % t, W, T.an_o[:, a0:a0 + W], T.tab[:, 0:TABW].indirect(T.rq_i[:, r0:r0 + n]), 0.0, [("rq_i", t, c)] + tabk, [("an_o", t, c)], k="g")
        if OWNT:
            oT = T["oT%d_%d" % (t, c)]
            dve(W, lambda: V.transpose(oT[:], T.an_o[:, a0:a0 + W]), [("an_o", t, c)], [("oT", t, c)], k=0.5)
            send(rank - 1 - t, T["aT%d_%d" % (t + 1, c)][:], oT[:], 256 * W, [("oT", t, c)], [("an_i", t, c), ("aT", t + 1, c)])
        else:
            send(rank - 1 - t, T.an_i[:, a0:a0 + W], T.an_o[:, a0:a0 + W], 256 * W, [("an_o", t, c)], [("an_i", t, c)])
        pri[0] = j0 + AT["sT"]
        pe(128, [lambda: P.matmul(pv[0:n, 384:512], su[:], T.i16[:], True, True)], [("su", c), "i16"], [(pvk, "t")], [pvk])
        act(128, lambda: S_.activation(sT[0:n, 128 * t:128 * t + 128], pv[0:n, 384:512], F.Relu, scale=1.0 - 2 * t), [(pvk, "t")], [("sT", t, c)], [pvk])
        if t == 0:
            pe(W, [lambda: P.matmul(px[:, 0:n, :], sT[0:n, 0:128], T.exc[0:n, 0:W], True, True)], [("sT", t, c), "exc"], [("px", c)], [pk])
            dve(W, lambda: V.tensor_tensor(T["sm0_%d" % c][:], T["st%d" % c][:], px[:, 0:n, :], A.mult), [("px", c), ("st", c)], [("sm", t, c)], [pk])
            return
        kept(t, c, False)
        route(c, T["aT%d_%d" % (t, c)], False, ("aT", t, c), False)
        pe(W, [lambda: P.matmul(px[:, 0:n, :], sT[0:n, 128:256], T.exa[0:n, 0:W], False, True)], [("sT", t, c), "exa", ("px", c)], [("px", c)], [pk])
        pri[0] = j0 + AT["sm"]
        act(W, lambda: S_.activation(T["sm1_%d" % c][:], px[:, 0:n, :], F.Relu), [("px", c)], [("sm", t, c)], [pk])

    def back(c):
        n, W, px, tp, pk = NS[c], 16 * NS[c], T["px%d" % c], T["tp%d" % c], "px%d" % c
        dve(W, lambda: V.transpose(tp[:], px[:, 0:n, :]), [("px", c)], [("tp", c)], [pk])
        pe(W, [lambda: P.matmul(px[:, 0:n, :], W2[13], T.ones[:, 0:W], True, False)], [("w2", 13), "ones"], [("px", c)], [pk])
        route(c, tp, True, ("tp", c), False)

    def finish(c):
        n, W, f0, r0 = NS[c], 16 * NS[c], 16 * C0[c], 96 + C0[c]
        xi, zz, yo, px = T.xi[:, f0:f0 + W], T.zz[:, f0:f0 + W], T.yo[:, f0:f0 + W], T["px%d" % c]
        dve(W, lambda: V.tensor_scalar(zz, px[:, 0:n, :], T.oc[:, 3:4], 2048.0, A.add, A.max), [("px", c), "oc3"], [("zz", c)], ["px%d" % c])
        dve(W, lambda: V.tensor_tensor(xi, T.pft[:, 0:TABW].indirect(T.rq_o[:, r0:r0 + n]), zz, A.add),
            [("rq_o", 2, c), ("zz", c), "pfI", "pfD"] + [("pfe", k) for k in range(4)], [("xi", c)], k="g")
        pri[0] += AT["fin2"]
        dve(W, lambda: V.tensor_scalar(xi, xi, 4095, None, A.bitwise_and), [("xi", c)], [("xi", c)])
        shift("yo%d" % c, W, yo, xi, 0.0, [("xi", c)], [("yo", c)])
        dma("s", T.ys[:, f0:f0 + W], yo, 512 * W, [("yo", c)], [("ys", c)])

    def scatter(win, tl, l0, src, h0, r, w):
        for k in range(8):
            pri[0] += AT["sc"]
            dve(16, lambda k=k: V.tensor_copy(win[:, 0:EXO].indirect(tl[:, l0 + 2 * k:l0 + 2 * k + 1]), src[:, h0 + 16 * k:h0 + 16 * k + 16]), r, w, k="s")

    def halve(t):
        rk = [("rq_i", t, k) for k in range(NC) if C0[k] < 8 * t + 8 and C0[k] + NS[k] > 8 * t]
        r0, h0, j0 = 56 * t, 144 * t, NC * t + max(CO.index(x[2]) for x in rk)
        hi, ht = T.hi[:, h0:h0 + 128], T.hi[:, h0 + 128:h0 + 136]
        if t == 2:
            pri[0] = j0 + AT["rq"] + 0.01
            send(rank + 3, T.rq_i[:, r0:r0 + 8], T.rq_o[:, r0:r0 + 8], 2048, [("rq_o",) + x[1:] for x in rk], rk)
        pri[0] = j0 + AT["dedup%d" % t]
        dve(8, lambda: V.tensor_scalar(T.hf[:], T.rq_i[:, r0:r0 + 8], float(EXO), -EXO / 2, A.min, A.add), rk, ["hf"])
        if t < 2:
            shift("hi%d" % t, 128, hi, T.an_o[:, 896 * t:896 * t + 128], -0.25, [("an_o",) + x[1:] for x in rk], [("hi", t)], times=0.5)
        else:
            shift("hi%d" % t, 128, hi, T.tab[:, 0:TABW].indirect(T.rq_i[:, r0:r0 + 8]), -0.25, tabk + rk, [("hi", t)], k="g", times=0.5)
        pd, pk = T["pd%d" % cnt["pd"]], "pd%d" % cnt["pd"]
        cnt["pd"] = (cnt["pd"] + 1) % NPD
        pe(128 + 32 * 64, [lambda: P.matmul(pd[:, :, 0, :], W2[13], T.ones[:, 0:128], True, False)]
           + [lambda h=h, z=z: P.matmul(pd[:, :, 0, h], T.wh[:, 128 * h:128 * h + 128] if z else T.nd[:], T.hf[:], False, h == 15 and z == 1)
              for h in range(16) for z in range(2)], [("w2", 13), "ones", "nd", "hf"] + whk, [pk], [pk])
        dve(128, lambda: V.tensor_scalar(T.eq[:], pd[:, :, 0, :], LIFT, None, A.is_equal), [pk], ["eq"], [pk])
        dve(128, lambda: V.tensor_tensor_scan(T.sc[:], T.eq[:], T.tri[:], 0.0, A.max, A.mult), ["eq", "tri"], ["sc"], k=0.5)
        dve(8, lambda: V.tensor_tensor(T.hg[:], T.sc[:, 15:128:16], T.hf[:], A.add), ["sc", "hf"], ["hg"])
        dve(8, lambda: V.tensor_scalar(T.tl[:, 0:16:2], T.hg[:], col[5], EXO / 2, A.min, A.add), ["hg", "cl5"], ["tl"])
        p0 = pri[0]
        if t < 2:
            pri[0] = NC * t + NC + AT["scat%d" % t]
        scatter(T.tab, T.tl, 0, T.hi, h0, ["tl", ("hi", t)], ["tabI", "tabD"])
        if t == 2:
            dma("q", T.yi[:], T.tab[:, 0:2048], 1 << 19, ["tabI"], ["yi"])
            return
        pri[0] = p0
        shift("ht", 8, ht, T.tl[:, 0:16:2], 0.0, ["tl"], [("ht", t)])
        send(rank - 3, T.hx[:, h0:h0 + 136], T.hi[:, h0:h0 + 136], 512 * 136, [("hi", t), ("ht", t)], [("hx", t)])

    def mirror(t):
        h0 = 144 * t
        shift("tx", 8, T.tx[:, 16 * t:16 * t + 16:2], T.hx[:, h0 + 128:h0 + 136], 0.0, [("hx", t)], [("tx", t)])
        scatter(T.pft, T.tx, 16 * t, T.hx, h0, [("tx", t), ("hx", t)], ["pfI", "pfD"])

    for t in range(3):
        for k, c in enumerate(CO):
            pri[0] = -0.7 + 0.01 * k if t == 0 and k < EARLY else NC * t + k + AT["up"]
            update(t, c)
        if t == 2:
            for k, c in enumerate(CO):
                pri[0] = NC * t + k + AT["back"]
                back(c)
        for k, c in enumerate(CO):
            pri[0] = NC * t + k
            compute(t, c)
            if t == 2 and k == 1:
                halve(t)
        if t < 2:
            halve(t)
        if t == 1:
            pri[0] = NC + AT["mir0"]
            mirror(0)
            pri[0] = 2 * NC - 1 + AT["mir1"]
            mirror(1)
    for k, c in enumerate(CO):
        pri[0] = 2 * NC + k + AT["fin"]
        finish(c)
    return ops


def depend(ops):
    last_w, readers, bank = {}, {}, {}
    for k, o in enumerate(ops):
        dep = set(last_w[x] for x in o["r"] + o["w"] if x in last_w)
        for x in o["w"]:
            dep.update(readers.get(x, []))
        for b in o["banks"]:
            e, cur, prev = bank.get(b, (o["eng"], [], []))
            if e != o["eng"]:
                cur, prev = [], cur
            dep.update(prev)
            bank[b] = (o["eng"], cur + [k], prev)
        o["pre"] = sorted(dep | set(last_w[x] for x in o["after"]))
        o["dep"] = sorted(j for j in dep if o["eng"] != "p" or ops[j]["eng"] != "p")
        for x in o["r"]:
            readers.setdefault(x, []).append(k)
        for x in o["w"]:
            last_w[x] = k
            readers[x] = []


def costs(ops, m):
    cy, gam, sca, pcy, rfix, rbw, riss, dbw, hop = m[:9]
    out = []
    for o in ops:
        e, n, k = o["eng"], o["n"], o["k"]
        if o["kind"] == "d":
            out.append((1000.0 if e == "q" else 100.0, 60 + n / dbw))
        elif o["kind"] == "r":
            out.append((riss, 150 + n / rbw))
        elif e == "l":
            out.append((0.0, riss - rfix - hop))
        elif e == "p":
            out.append((n * pcy, 60.0))
        elif e == "q":
            out.append((130 + 2 * n * cy, 0.0))
        elif k in ("g", "s"):
            out.append((55 + n * cy * (gam if k == "g" else sca), 0.0))
        else:
            out.append((40 + max(64, n * k) * cy, 0.0))
    return out


def book(busy, t, lat):
    for i, (lo, hi) in enumerate(busy):
        if t + lat <= lo:
            busy.insert(i, (t, t + lat))
            return t + lat
        if hi > t:
            t = hi
    busy.append((t, t + lat))
    return t + lat


def move(o, t, occ, lat, m, wire):
    t += occ
    if o["eng"] == "q" and o["kind"] not in wire[3]:
        wire[3] += o["kind"]
        t += m[9]
    if o["kind"] == "d":
        return t, max(book(wire[0], t, lat), book(wire[1], t, lat)) + 2000.0
    if len(o["k"]) == 2:
        return t, book(wire[0], t, lat) + m[4] - m[6]
    return t, book(wire[2], book(wire[1], t, 0.6 * lat) + m[4], lat) + m[4] - m[6]


QUEUES = "vapqsl"


def listed(ops, succ, cost, m):
    n = len(ops)
    left = [len(o["pre"]) for o in ops]
    lim = [0.0] * n
    free = {e: 0.0 for e in QUEUES}
    wire = [[], [], [], ""]
    pool = [k for k in range(n) if left[k] == 0]
    order = []
    while pool:
        j = min(pool, key=lambda x: max(lim[x], free[ops[x]["eng"]]))
        e = ops[j]["eng"]
        first = max(lim[j], free[e]) + min(LOOK, cost[j][0])
        k = min((x for x in pool if ops[x]["eng"] == e and (x == j or lim[x] < first)), key=lambda x: (ops[x]["pri"], x))
        pool.remove(k)
        order.append(k)
        t = max(lim[k], free[e])
        if ops[k]["kind"] in "dr":
            free[e], end = move(ops[k], t, cost[k][0], cost[k][1], m, wire)
        else:
            free[e], end = t + cost[k][0], t + sum(cost[k])
        for x in succ[k]:
            if k in ops[x]["dep"]:
                lim[x] = max(lim[x], end + m[8])
            left[x] -= 1
            if left[x] == 0:
                pool.append(x)
    return order


def replay(ops, info, m, od, p, mark, end, keep=None, why=None):
    free, wire, prev = mark[0][:], [mark[1][:], mark[2][:], mark[3][:], mark[4]], mark[5][:]
    for q in range(p, len(od)):
        k = od[q]
        e, d, occ, lat, plain = info[k]
        t = free[e]
        if keep is None:
            for j in d:
                if end[j] > t:
                    t = end[j]
        else:
            if q % GAP == 0:
                keep[q // GAP] = (free[:], wire[0][:], wire[1][:], wire[2][:], wire[3], prev[:])
            why[k] = prev[e]
            prev[e] = k
            for j in d:
                if end[j] > t:
                    t, why[k] = end[j], -2 - j
        if plain:
            t += occ
            free[e] = t
            end[k] = t + lat
        else:
            free[e], t = move(ops[k], t, occ, lat - m[8], m, wire)
            end[k] = t + m[8]
    return max(end) + SOFT * sum(end) / len(end) + HURRY * sum([end[k] for k in info[-1]])


def tables(ops):
    above, dep = [0] * len(ops), []
    for k, o in enumerate(ops):
        seen = 0
        for j in o["dep"]:
            seen |= above[j]
        dep.append(tuple(j for j in o["dep"] if not seen >> j & 1))
        if o["eng"] != "l":
            above[k] = seen | sum(1 << j for j in o["dep"] if not seen >> j & 1)
    sends = [k for k, o in enumerate(ops) if o["kind"] == "r" and len(o["k"]) == 2]
    return [[(QUEUES.index(o["eng"]), d, c[0], c[1] + m[8], o["kind"] not in "dr") for o, d, c in zip(ops, dep, costs(ops, m))] + [sends] for m in MODELS]


START = ([0.0] * 5 + [-1e9], [], [], [], "", [-1] * 6)


def schedule(ops):
    n, nm = len(ops), len(MODELS)
    pre = [o["pre"] for o in ops]
    succ = [[] for _ in range(n)]
    for k in range(n):
        for j in pre[k]:
            succ[j].append(k)
    order = listed(ops, succ, costs(ops, MODELS[0]), MODELS[0])
    info = tables(ops)
    seed = [SEED]

    def rnd():
        seed[0] = (seed[0] * 1103515245 + 12345) % 2147483648
        return seed[0] / 2147483648.0

    keeps = [[None] * (n // GAP + 1) for _ in range(nm)]
    ends = [[0.0] * n for _ in range(nm)]
    whys = [[0] * n for _ in range(nm)]
    base = [replay(ops, info[i], MODELS[i], order, 0, START, ends[i], keeps[i], whys[i]) for i in range(nm)]
    cur = [1.0] * nm
    best, best_order, pairs, fresh = float(nm), order, [], True
    for it in range(ITERS):
        if fresh or it % 16 == 0:
            i = int(rnd() * nm)
            k, pairs, fresh = ends[i].index(max(ends[i])), [], False
            while k != -1:
                w = whys[i][k]
                if w >= 0 and w not in pre[k]:
                    pairs.append((w, k))
                k = w if w >= -1 else -2 - w
        if pairs and rnd() < CRIT:
            j, k = pairs[int(rnd() * len(pairs))]
            p0, p1 = order.index(j), order.index(k)
        else:
            p0 = int(rnd() * (n - 1))
            j = order[p0]
            later = [q for q in range(p0 + 1, min(n, p0 + 60)) if ops[order[q]]["eng"] == ops[j]["eng"]][:1 + int(rnd() * 3)]
            if not later:
                continue
            p1 = later[-1]
            k = order[p1]
        seg = order[p0:p1 + 1]
        if rnd() < 0.5:
            take = {k}
            for x in reversed(seg[:-1]):
                if not take.isdisjoint(succ[x]):
                    take.add(x)
            if j in take:
                continue
            new = [x for x in seg if x in take] + [x for x in seg if x not in take]
        else:
            take = {j}
            for x in seg[1:]:
                if not take.isdisjoint(pre[x]):
                    take.add(x)
            if k in take:
                continue
            new = [x for x in seg if x not in take] + [x for x in seg if x in take]
        cand = order[:p0] + new + order[p1 + 1:]
        room, b, up = TEMP * (1.0 - it / ITERS) * rnd(), p0 // GAP, 0.0
        for i in range(nm):
            up += replay(ops, info[i], MODELS[i], cand, b * GAP, keeps[i][b], ends[i][:]) / base[i] - cur[i]
            if up > (room if i == nm - 1 else 0.7 * room + 0.001):
                break
        else:
            order, fresh = cand, True
            cur = [replay(ops, info[i], MODELS[i], order, b * GAP, keeps[i][b], ends[i], keeps[i], whys[i]) / base[i] for i in range(nm)]
            if sum(cur) < best:
                best, best_order = sum(cur), order
    return best_order


ORDER = {}


def hand_on(g, core, T, topo):
    for owner in topo.cores_of(core):
        if T.rank_of(owner) is None:
            continue
        dst, hs = relays(owner, T, topo)
        if core not in hs:
            continue
        rid, pid, _ = topo.addr(dst)
        sent = 0
        for k, piece in enumerate(landing(T)):
            if hs[k % len(hs)] == core:
                g.wait_ge(T.sem["r%d" % k], len(inward(owner, core, dst, k, topo)))
                g.remote_dma(piece, piece, T.sem["r%d" % k], T.sem.loc, pid, rid, topo.mask(core, dst))
                sent += len(topo.engines(core, dst))
        g.wait_ge(T.sem.loc, sent)


def rank_program(g, core, T, topo):
    if T.rank_of(core) is None:
        hand_on(g, core, T, topo)
        return
    ops = build(g, core, T, topo)
    depend(ops)
    if "order" not in ORDER:
        ORDER["order"] = schedule(ops)
    Q = {"v": g.vector, "a": g.scalar, "p": g.tensor, "q": g, "s": g.sync}
    count = {"v": 0, "a": 0, "p": 0, "q": 0}
    known = {e: {} for e in Q}
    done, total = {}, {}
    nd, loc = 0, 0
    for k in ORDER["order"]:
        o = ops[k]
        e = o["eng"]
        if e == "l":
            done[k] = o["sem"]
            total[done[k][0]] = done[k][1]
            continue
        need = {}
        for j in o["dep"]:
            s, val = done[j]
            need[s] = max(need.get(s, 0), val)
        for s, val in need.items():
            if known[e].get(s, 0) < val:
                Q[e].wait_ge(T.sem[s], val)
                known[e][s] = val
        ins = [fn() for fn in o["fns"]][-1]
        if o["kind"] == "c":
            count[e] += 1
            ins.then_inc(T.sem[e], 1)
            done[k] = (e, count[e])
        elif o["kind"] == "d":
            done[k] = ("d%d" % nd, 16)
            ins.then_inc(T.sem["d%d" % nd], 16)
            nd += 1
        else:
            done[k] = o["sem"][:2]
            loc += o["sem"][2]
        total[done[k][0]] = done[k][1]
    total["loc"] = loc
    for s, val in total.items():
        if all(known[e].get(s, 0) < val for e in Q):
            g.sync.wait_ge(T.sem[s], val)
